import numpy as np
import ml_dtypes


def mxq(x, axis, fmt="e4m3"):
    dtype, down = {"e4m3": (ml_dtypes.float8_e4m3fn, 7), "e5m2": (ml_dtypes.float8_e5m2, 14)}[fmt]
    v = np.moveaxis(np.asarray(x, np.float32).astype(ml_dtypes.bfloat16).astype(np.float64), axis, -1)
    blocks = v.reshape(v.shape[:-1] + (-1, 32))
    amax = np.abs(blocks).max(-1, keepdims=True)
    byte = np.maximum(np.where(amax > 0, np.frexp(amax)[1] - 1 + 127, 0) - down, 1)
    scale = np.exp2(byte - 127.0)
    codes = (blocks / scale).astype(np.float32).astype(dtype).astype(np.float64)
    return np.moveaxis((codes * scale).reshape(v.shape), -1, axis)


WIDE = False


def mx_kscale(k):
    if not WIDE:
        return np.ones(k)
    levels = np.array([10, -10, 5, -5, 0])
    if k % 512:
        return np.exp2(np.random.permutation(np.resize(levels, k // 32))).repeat(32)
    a = np.empty((k // 512, 16))
    for p in range(k // 512):
        a[p, :8] = np.random.permutation(np.resize(levels, 8))
        for g in range(8):
            far = levels[np.abs(levels - a[p, g]) >= 10]
            a[p, g + 8] = far[np.random.randint(len(far))]
    return np.exp2(a.ravel()).repeat(32)


def f64(x):
    return np.asarray(x).astype(np.float64)


def striped(idx):
    return np.tile(idx.reshape(-1, 16).T, (8, 1)).astype(np.uint16)


def unstriped(offs):
    return offs[:16].T.reshape(-1).astype(np.int64)


E2M1 = np.array([0.0, 0.5, 1.0, 1.5, 2.0, 3.0, 4.0, 6.0, -0.0, -0.5, -1.0, -1.5, -2.0, -3.0, -4.0, -6.0])


def pack_weight(w, fmt):
    k, n = w.shape
    w = f64(np.asarray(w, np.float32).astype(ml_dtypes.bfloat16)).reshape(k // 32, 32, n)
    amax = np.abs(w).max(1)
    if fmt == "e4m3":
        byte = np.frexp(amax)[1] - 1 + 127 - 7
    else:
        mant, ex = np.frexp(amax / 6.0)
        byte = np.where(mant > 0.5, ex, ex - 1) + 127
    byte = np.clip(np.where(amax > 0, byte, 1), 1, 254)
    scaled = (w * np.exp2(127.0 - byte)[:, None, :]).reshape(k, n).astype(np.float32)
    by_word = np.ascontiguousarray(scaled.reshape(k // 512, 128, 4, n).transpose(0, 1, 3, 2))
    if fmt == "e4m3":
        words = by_word.astype(ml_dtypes.float8_e4m3fn).view(np.uint8)
    else:
        c = by_word.astype(ml_dtypes.float4_e2m1fn).view(np.uint8) & 0xF
        words = (c[..., 0::2] | (c[..., 1::2] << 4)).reshape(k // 512, 128, 2 * n)
    return np.ascontiguousarray(words), np.ascontiguousarray(byte.astype(np.uint8).reshape(k // 512, 16, n))


def unpack_weight(words, scales, fmt):
    g, _, n = scales.shape
    words = np.ascontiguousarray(words).reshape(g, 128, n, -1)
    if fmt == "e4m3":
        vals = words.view(ml_dtypes.float8_e4m3fn).astype(np.float64)
    else:
        nib = np.empty((g, 128, n, 4), np.uint8)
        nib[..., 0::2] = words & 0xF
        nib[..., 1::2] = words >> 4
        vals = E2M1[nib]
    vals = vals * np.repeat(np.exp2(scales.astype(np.float64) - 127.0), 8, axis=1)[..., None]
    return vals.transpose(0, 1, 3, 2).reshape(g * 512, n)


def silu(v):
    return v / (1.0 + np.exp(-np.maximum(v, -700.0)))


K, T, E, C, H, N = 512, 640, 4, 128, 1024, 256
R = 4


def by_expert(wq, xq):
    return np.concatenate([wq[e].T @ xq[:, e * C:(e + 1) * C] for e in range(E)], axis=1)


def setup_inputs():
    n = np.random.standard_normal
    s = mx_kscale(K)[:, None]
    u = mx_kscale(H)
    slot_token = np.concatenate([r * (T // R) + np.random.permutation(T // R)[:C // R] for e in range(E) for r in range(R)])
    w1 = [pack_weight(m, "e2m1") for m in n((E, K, H)) / np.sqrt(K) / s[None] * u[None, None, :]]
    w2 = [pack_weight(m, "e2m1") for m in n((E, H, N)) / np.sqrt(H) / u[None, :, None]]
    return {
        "xT": (n((K, T)) * s).astype(np.float32),
        "w1_words": np.stack([m[0] for m in w1]),
        "w1_scales": np.stack([m[1] for m in w1]),
        "w2_words": np.stack([m[0] for m in w2]),
        "w2_scales": np.stack([m[1] for m in w2]),
        "offs": striped(slot_token),
    }


def reference(xT, w1_words, w1_scales, w2_words, w2_scales, offs):
    idx = unstriped(offs)
    w1 = np.stack([unpack_weight(w1_words[e], w1_scales[e], "e2m1") for e in range(E)])
    w2 = np.stack([unpack_weight(w2_words[e], w2_scales[e], "e2m1") for e in range(E)])
    xq = mxq(f64(xT)[:, idx], 0, "e4m3")
    h = silu(by_expert(w1, xq))
    y = by_expert(w2, mxq(h, 0, "e4m3"))
    return y.reshape(N, E, R, C // R).transpose(0, 2, 1, 3).reshape(N, E * C)

@@ -1,0 +1,173 @@
+from contextlib import ExitStack
+
+import concourse.mybir as mybir
+
+FLOPS = 805306368
+
+K, T, E, C, H, N = 512, 640, 4, 128, 1024, 256
+R = 4
+P = 128
+G = H // 512
+
+F32 = mybir.dt.float32
+BF16 = mybir.dt.bfloat16
+I32 = mybir.dt.int32
+U32 = mybir.dt.uint32
+U16 = mybir.dt.uint16
+U8 = mybir.dt.uint8
+FP8X4 = mybir.dt.float8_e4m3fn_x4
+FP4X4 = mybir.dt.float4_e2m1fn_x4
+ACT = mybir.ActivationFunctionType
+
+CHUNKS = [(0, 256), (256, 256), (512, 128)]
+CAST_ON_SCALAR = {0, 2, 3}
+
+
+def tile_moe_eps_mlp_silu_kernel(tc, xT, w1_words, w1_scales, w2_words, w2_scales, offs, out):
+    nc = tc.nc
+    with ExitStack() as ctx:
+        keep = ctx.enter_context(tc.tile_pool(name="keep", bufs=1))
+        work = ctx.enter_context(tc.tile_pool(name="work", bufs=4))
+        hp = ctx.enter_context(tc.psum_pool(name="hp", bufs=4))
+        yp = ctx.enter_context(tc.psum_pool(name="yp", bufs=2))
+
+        offsets = keep.tile([P, E * C // 16], U16, name="offsets")
+        raw_scales = keep.tile([P, H], U8, name="raw_scales", align_bytes=64)
+        perm_scales = keep.tile([P, H], U8, name="perm_scales", align_bytes=64)
+        x_codes = keep.tile([P, T], U32, name="x_codes", align_bytes=64)
+        x_bytes = keep.tile([P, T], U8, name="x_bytes", align_bytes=64)
+        w2_plane = keep.tile([P, E * G, N], U8, name="w2_plane", align_bytes=64)
+        w1_raw = [keep.tile([P, 2 * H], U8, name=f"w1_raw{e}", tag=f"w1_raw{e}", align_bytes=64) for e in range(E - 1)]
+        w1 = [keep.tile([P, 2 * H], U8, name=f"w1_{e}", align_bytes=64) for e in range(E)]
+        w1_plane = [perm_scales] + [keep.tile([P, H], U8, name=f"w1_plane{e}", align_bytes=64) for e in range(1, E)]
+        x_raw = [keep.tile([P, 4, w], F32, name=f"x_raw{i}", tag=f"x_raw{i}", align_bytes=64) for i, (c0, w) in enumerate(CHUNKS)]
+        results = [keep.tile([P, E * C], F32, name=f"results{i}") for i in range(2)]
+        warm = keep.tile([P, 1], F32, name="warm")
+        warm_out = keep.tile([P, 1], F32, name="warm_out")
+
+        nc.vector.memset(raw_scales[:].bitcast(I32), 0)
+        nc.vector.memset(warm[:], 0.0)
+        nc.scalar.activation(warm_out[:], warm[:], ACT.Silu)
+        nc.vector.memset(w2_plane[:].rearrange("p a n -> p (a n)").bitcast(I32), 0)
+        for e in range(1, E):
+            nc.vector.memset(w1_plane[e][:].bitcast(I32), 0)
+        nc.gpsimd.memset(x_bytes[:], 0)
+
+        for q in range(4):
+            nc.scalar.dma_start(raw_scales[32 * q : 32 * q + 16, :].bitcast(I32), w1_scales[:, 0, 4 * q : 4 * q + 4, :].bitcast(I32))
+        for i, (c0, w) in enumerate(CHUNKS):
+            nc.sync.dma_start(x_raw[i][:], xT[:, c0 : c0 + w].rearrange("(p j) w -> p j w", j=4))
+            if i == 0:
+                nc.sync.dma_start(w1_raw[0][:].bitcast(I32), w1_words[0, 0].bitcast(I32))
+        nc.sync.dma_start(offsets[:], offs)
+        for e in range(1, E - 1):
+            nc.sync.dma_start(w1_raw[e][:].bitcast(I32), w1_words[e, 0].bitcast(I32))
+
+        def permute_words(e):
+            nc.vector.tensor_copy(
+                w1[e][:].bitcast(U16).rearrange("p (g t m) -> p g t m", g=G, t=4),
+                w1_raw[e][:].bitcast(U16).rearrange("p (g m t) -> p g t m", g=G, t=4),
+            )
+
+        nc.vector.tensor_copy(
+            perm_scales[:].rearrange("p (g t m) -> p g t m", g=G, t=4),
+            raw_scales[:].rearrange("p (g m t) -> p g t m", g=G, t=4),
+        )
+        def move_scales(e):
+            nc.sync.dma_start(w1_plane[e][0:112, :].bitcast(I32), perm_scales[4 * e : 4 * e + 112, :].bitcast(I32))
+
+        move_scales(1)
+        permute_words(0)
+
+        grouped = {}
+
+        def cast(u):
+            i = 0 if u < 2 else 1 if u < 4 else 2
+            c = u * P - CHUNKS[i][0]
+            grouped[u] = work.tile([P, P, 4], BF16, name=f"grouped{u}", align_bytes=64, bufs=1)
+            src = x_raw[i][:, :, c : c + P].rearrange("p j w -> p w j")
+            if u in CAST_ON_SCALAR:
+                nc.scalar.activation(grouped[u][:], src, ACT.Copy)
+            else:
+                nc.vector.tensor_copy(grouped[u][:], src)
+
+        def quantise(u):
+            cols = slice(u * P, (u + 1) * P)
+            nc.vector.quantize_mx(x_codes[:, cols].bitcast(FP8X4), x_bytes[:, cols], grouped[u][:].rearrange("p w j -> p (w j)"))
+
+        cast(0)
+        cast(1)
+        w2 = keep.tile([P, E * G, 2 * N], U8, name="w2", tag="x_raw0", align_bytes=64)
+        nc.sync.dma_start(w2[:].bitcast(I32), w2_words.rearrange("e s p b -> p (e s) b").bitcast(I32))
+        w1_raw.append(keep.tile([P, 2 * H], U8, name="w1_raw3", tag="w1_raw0", align_bytes=64))
+        nc.sync.dma_start(w1_raw[3][:].bitcast(I32), w1_words[3, 0].bitcast(I32))
+        for q in range(4):
+            nc.sync.dma_start(
+                w2_plane[32 * q : 32 * q + 4].bitcast(I32),
+                w2_scales[:, :, 4 * q : 4 * q + 4, :].rearrange("e s q n -> q (e s) n").bitcast(I32),
+            )
+        move_scales(2)
+        move_scales(3)
+        quantise(0)
+        quantise(1)
+        for u in range(2, 5):
+            cast(u)
+        for u in range(2, 5):
+            quantise(u)
+
+        hq = {}
+
+        def stage_a(e):
+            if e > 0:
+                permute_words(e)
+            lst = offsets[:, 8 * e : 8 * e + 8]
+            s_codes = work.tile([P, C], U32, name="s_codes", align_bytes=64)
+            s_bytes = work.tile([P, C], U8, name="s_bytes", align_bytes=64)
+            nc.vector.tensor_copy(s_codes[:], x_codes[:].indirect(lst))
+            nc.vector.tensor_copy(s_bytes[:], x_bytes[:].indirect(lst))
+            for g in range(G):
+                a = hp.tile([P, 4, C], F32, name="a")
+                for t in range(4):
+                    c = g * 512 + t * P
+                    nc.tensor.matmul_mx(
+                        out=a[:, t, :],
+                        lhsT=w1[e][:, 2 * c : 2 * c + 2 * P].bitcast(FP4X4),
+                        lhsT_scale=w1_plane[e][:, c : c + P],
+                        rhs=s_codes[:].bitcast(FP8X4),
+                        rhs_scale=s_bytes[:],
+                        start=True,
+                        stop=True,
+                    )
+                h = work.tile([P, C, 4], BF16, name="h", align_bytes=64)
+                nc.scalar.activation(h[:], a[:].rearrange("p t n -> p n t"), ACT.Silu)
+                hq[e, g] = h
+
+        def stage_b(e):
+            y = [yp.tile([P, C], F32, name=f"y{i}") for i in range(2)]
+            for g in range(G):
+                h_codes = work.tile([P, C], U32, name="h_codes", align_bytes=64)
+                h_bytes = work.tile([P, C], U8, name="h_bytes", align_bytes=64)
+                nc.vector.quantize_mx(h_codes[:].bitcast(FP8X4), h_bytes[:], hq[e, g][:].rearrange("p n t -> p (n t)"))
+                for i in range(2):
+                    nc.tensor.matmul_mx(
+                        out=y[i][:],
+                        lhsT=w2[:, e * G + g, 2 * P * i : 2 * P * i + 2 * P].bitcast(FP4X4),
+                        lhsT_scale=w2_plane[:, e * G + g, P * i : P * i + P],
+                        rhs=h_codes[:].bitcast(FP8X4),
+                        rhs_scale=h_bytes[:],
+                        start=(g == 0),
+                        stop=(g == G - 1),
+                    )
+            for i in range(2):
+                nc.vector.tensor_copy(
+                    results[i][:].rearrange("p (m e u) -> p m e u", m=R, e=E)[:, :, e, :],
+                    y[i][:].rearrange("p (m u) -> p m u", m=R),
+                )
+
+        stage_a(0)
+        for e in range(1, E):
+            stage_a(e)
+            stage_b(e - 1)
+        stage_b(E - 1)
+        for i in range(2):
+            nc.sync.dma_start(out[i * P : (i + 1) * P, :], results[i][:])

@@ -20,111 +20,113 @@ FP4X4 = mybir.dt.float4_e2m1fn_x4
 ACT = mybir.ActivationFunctionType
 
 CHUNKS = [(0, 256), (256, 256), (512, 128)]
-CAST_ON_SCALAR = {0, 2, 3}
 
 
 def tile_moe_eps_mlp_silu_kernel(tc, xT, w1_words, w1_scales, w2_words, w2_scales, offs, out):
     nc = tc.nc
     with ExitStack() as ctx:
         keep = ctx.enter_context(tc.tile_pool(name="keep", bufs=1))
-        work = ctx.enter_context(tc.tile_pool(name="work", bufs=4))
+        slots = ctx.enter_context(tc.tile_pool(name="slots", bufs=2))
         hp = ctx.enter_context(tc.psum_pool(name="hp", bufs=4))
-        yp = ctx.enter_context(tc.psum_pool(name="yp", bufs=2))
+        yp = ctx.enter_context(tc.psum_pool(name="yp", bufs=1))
 
         offsets = keep.tile([P, E * C // 16], U16, name="offsets")
         raw_scales = keep.tile([P, H], U8, name="raw_scales", align_bytes=64)
         perm_scales = keep.tile([P, H], U8, name="perm_scales", align_bytes=64)
         x_codes = keep.tile([P, T], U32, name="x_codes", align_bytes=64)
-        x_bytes = keep.tile([P, T], U8, name="x_bytes", align_bytes=64)
-        w2_plane = keep.tile([P, E * G, N], U8, name="w2_plane", align_bytes=64)
-        w1_raw = [keep.tile([P, 2 * H], U8, name=f"w1_raw{e}", tag=f"w1_raw{e}", align_bytes=64) for e in range(E - 1)]
+        raw0 = keep.tile([P, 2 * H], U8, name="raw0", tag="raw0", align_bytes=64)
+        raw12 = keep.tile([P, 2 * 2 * H], U8, name="raw12", align_bytes=64)
+        raw3 = keep.tile([P, 2 * H], U8, name="raw3", align_bytes=64)
+        w1_raw = [raw0[:], raw12[:, 0 : 2 * H], raw12[:, 2 * H : 4 * H], raw3[:]]
         w1 = [keep.tile([P, 2 * H], U8, name=f"w1_{e}", align_bytes=64) for e in range(E)]
         w1_plane = [perm_scales] + [keep.tile([P, H], U8, name=f"w1_plane{e}", align_bytes=64) for e in range(1, E)]
-        x_raw = [keep.tile([P, 4, w], F32, name=f"x_raw{i}", tag=f"x_raw{i}", align_bytes=64) for i, (c0, w) in enumerate(CHUNKS)]
-        results = [keep.tile([P, E * C], F32, name=f"results{i}") for i in range(2)]
+        w2_plane = keep.tile([P, E * G * N], U8, name="w2_plane", align_bytes=64)
+        w2 = keep.tile([P, E * G, 2 * N], U8, name="w2", align_bytes=64)
+        x_raw = [keep.tile([P, 4, w], F32, name=f"x_raw{i}", align_bytes=64) for i, (c0, w) in enumerate(CHUNKS)]
+        results = keep.tile([P, 2, E * C], F32, name="results")
         warm = keep.tile([P, 1], F32, name="warm")
         warm_out = keep.tile([P, 1], F32, name="warm_out")
 
         nc.vector.memset(raw_scales[:].bitcast(I32), 0)
         nc.vector.memset(warm[:], 0.0)
         nc.scalar.activation(warm_out[:], warm[:], ACT.Silu)
-        nc.vector.memset(w2_plane[:].rearrange("p a n -> p (a n)").bitcast(I32), 0)
         for e in range(1, E):
             nc.vector.memset(w1_plane[e][:].bitcast(I32), 0)
-        nc.gpsimd.memset(x_bytes[:], 0)
+        nc.vector.memset(w2_plane[:].bitcast(I32), 0)
 
-        for q in range(4):
-            nc.scalar.dma_start(raw_scales[32 * q : 32 * q + 16, :].bitcast(I32), w1_scales[:, 0, 4 * q : 4 * q + 4, :].bitcast(I32))
-        for i, (c0, w) in enumerate(CHUNKS):
+        def load_x(i):
+            c0, w = CHUNKS[i]
             nc.sync.dma_start(x_raw[i][:], xT[:, c0 : c0 + w].rearrange("(p j) w -> p j w", j=4))
-            if i == 0:
-                nc.sync.dma_start(w1_raw[0][:].bitcast(I32), w1_words[0, 0].bitcast(I32))
+
+        load_x(0)
+        for q in range(4):
+            nc.sync.dma_start(raw_scales[32 * q : 32 * q + 16, :].bitcast(I32), w1_scales[:, 0, 4 * q : 4 * q + 4, :].bitcast(I32))
+        nc.sync.dma_start(raw0[:].bitcast(I32), w1_words[0, 0].bitcast(I32))
+        load_x(1)
+        load_x(2)
         nc.sync.dma_start(offsets[:], offs)
-        for e in range(1, E - 1):
-            nc.sync.dma_start(w1_raw[e][:].bitcast(I32), w1_words[e, 0].bitcast(I32))
+        nc.sync.dma_start(raw12[:].rearrange("p (e b) -> p e b", e=2).bitcast(I32), w1_words[1:3, 0].rearrange("e p b -> p e b").bitcast(I32))
 
         def permute_words(e):
             nc.vector.tensor_copy(
                 w1[e][:].bitcast(U16).rearrange("p (g t m) -> p g t m", g=G, t=4),
-                w1_raw[e][:].bitcast(U16).rearrange("p (g m t) -> p g t m", g=G, t=4),
+                w1_raw[e].bitcast(U16).rearrange("p (g m t) -> p g t m", g=G, t=4),
             )
+
+        def move_scales(e):
+            nc.sync.dma_start(w1_plane[e][0:112, :].bitcast(I32), perm_scales[4 * e : 4 * e + 112, :].bitcast(I32))
 
         nc.vector.tensor_copy(
             perm_scales[:].rearrange("p (g t m) -> p g t m", g=G, t=4),
             raw_scales[:].rearrange("p (g m t) -> p g t m", g=G, t=4),
         )
-        def move_scales(e):
-            nc.sync.dma_start(w1_plane[e][0:112, :].bitcast(I32), perm_scales[4 * e : 4 * e + 112, :].bitcast(I32))
-
         move_scales(1)
-        permute_words(0)
-
-        grouped = {}
-
-        def cast(u):
-            i = 0 if u < 2 else 1 if u < 4 else 2
-            c = u * P - CHUNKS[i][0]
-            grouped[u] = work.tile([P, P, 4], BF16, name=f"grouped{u}", align_bytes=64, bufs=1)
-            src = x_raw[i][:, :, c : c + P].rearrange("p j w -> p w j")
-            if u in CAST_ON_SCALAR:
-                nc.scalar.activation(grouped[u][:], src, ACT.Copy)
-            else:
-                nc.vector.tensor_copy(grouped[u][:], src)
-
-        def quantise(u):
-            cols = slice(u * P, (u + 1) * P)
-            nc.vector.quantize_mx(x_codes[:, cols].bitcast(FP8X4), x_bytes[:, cols], grouped[u][:].rearrange("p w j -> p (w j)"))
-
-        cast(0)
-        cast(1)
-        w2 = keep.tile([P, E * G, 2 * N], U8, name="w2", tag="x_raw0", align_bytes=64)
-        nc.sync.dma_start(w2[:].bitcast(I32), w2_words.rearrange("e s p b -> p (e s) b").bitcast(I32))
-        w1_raw.append(keep.tile([P, 2 * H], U8, name="w1_raw3", tag="w1_raw0", align_bytes=64))
-        nc.sync.dma_start(w1_raw[3][:].bitcast(I32), w1_words[3, 0].bitcast(I32))
-        for q in range(4):
-            nc.sync.dma_start(
-                w2_plane[32 * q : 32 * q + 4].bitcast(I32),
-                w2_scales[:, :, 4 * q : 4 * q + 4, :].rearrange("e s q n -> q (e s) n").bitcast(I32),
-            )
+        nc.sync.dma_start(raw3[:].bitcast(I32), w1_words[3, 0].bitcast(I32))
         move_scales(2)
         move_scales(3)
-        quantise(0)
-        quantise(1)
-        for u in range(2, 5):
-            cast(u)
-        for u in range(2, 5):
-            quantise(u)
+        for q in range(4):
+            nc.sync.dma_start(
+                w2_plane[32 * q : 32 * q + 4].rearrange("p (a n) -> p a n", n=N).bitcast(I32),
+                w2_scales[:, :, 4 * q : 4 * q + 4, :].rearrange("e s q n -> q (e s) n").bitcast(I32),
+            )
+        nc.sync.dma_start(w2[:].bitcast(I32), w2_words.rearrange("e s p b -> p (e s) b").bitcast(I32))
+        permute_words(0)
+        x_bytes = keep.tile([P, T], U8, name="x_bytes", tag="raw0", align_bytes=64)
+        nc.vector.memset(x_bytes[:].bitcast(I32), 0)
 
-        hq = {}
+        def cast(chunk, c, w, on_scalar):
+            grouped = keep.tile([P, 4 * w], BF16, name=f"grouped{chunk}_{c}", align_bytes=64)
+            dst = grouped[:].rearrange("p (c i j) -> p c j i", i=4, j=4)
+            src = x_raw[chunk][:, :, c : c + w].rearrange("p j (c i) -> p c j i", i=4)
+            if on_scalar:
+                nc.scalar.activation(dst, src, ACT.Copy)
+            else:
+                nc.vector.tensor_copy(dst, src)
+            return grouped
 
-        def stage_a(e):
+        def quantise(grouped, c0, w):
+            nc.vector.quantize_mx(x_codes[:, c0 : c0 + w].bitcast(FP8X4), x_bytes[:, c0 : c0 + w], grouped[:])
+
+        quantise(cast(0, 0, 256, True), 0, 256)
+        first = cast(1, 0, P, False)
+        second = cast(1, P, P, True)
+        quantise(first, 256, P)
+        third = cast(2, 0, P, False)
+        quantise(second, 384, P)
+        quantise(third, 512, P)
+
+        hidden = []
+        for e in range(E):
             if e > 0:
                 permute_words(e)
             lst = offsets[:, 8 * e : 8 * e + 8]
-            s_codes = work.tile([P, C], U32, name="s_codes", align_bytes=64)
-            s_bytes = work.tile([P, C], U8, name="s_bytes", align_bytes=64)
+            s_codes = slots.tile([P, C], U32, name="s_codes", align_bytes=64)
+            s_bytes = slots.tile([P, C], U8, name="s_bytes", align_bytes=64)
             nc.vector.tensor_copy(s_codes[:], x_codes[:].indirect(lst))
             nc.vector.tensor_copy(s_bytes[:], x_bytes[:].indirect(lst))
+            h = [keep.tile([P, G * C * 4], BF16, name=f"h{e}", align_bytes=64)]
+            if e == E - 1:
+                h = [keep.tile([P, C * 4], BF16, name=f"h{e}_{g}", align_bytes=64) for g in range(G)]
             for g in range(G):
                 a = hp.tile([P, 4, C], F32, name="a")
                 for t in range(4):
@@ -138,36 +140,45 @@ def tile_moe_eps_mlp_silu_kernel(tc, xT, w1_words, w1_scales, w2_words, w2_scale
                         start=True,
                         stop=True,
                     )
-                h = work.tile([P, C, 4], BF16, name="h", align_bytes=64)
-                nc.scalar.activation(h[:], a[:].rearrange("p t n -> p n t"), ACT.Silu)
-                hq[e, g] = h
+                dst = h[g][:] if e == E - 1 else h[0][:, g * 4 * C : (g + 1) * 4 * C]
+                nc.scalar.activation(dst.rearrange("p (n t) -> p n t", t=4), a[:].rearrange("p t n -> p n t"), ACT.Silu)
+            hidden.append(h)
 
-        def stage_b(e):
-            y = [yp.tile([P, C], F32, name=f"y{i}") for i in range(2)]
-            for g in range(G):
-                h_codes = work.tile([P, C], U32, name="h_codes", align_bytes=64)
-                h_bytes = work.tile([P, C], U8, name="h_bytes", align_bytes=64)
-                nc.vector.quantize_mx(h_codes[:].bitcast(FP8X4), h_bytes[:], hq[e, g][:].rearrange("p n t -> p (n t)"))
-                for i in range(2):
-                    nc.tensor.matmul_mx(
-                        out=y[i][:],
-                        lhsT=w2[:, e * G + g, 2 * P * i : 2 * P * i + 2 * P].bitcast(FP4X4),
-                        lhsT_scale=w2_plane[:, e * G + g, P * i : P * i + P],
-                        rhs=h_codes[:].bitcast(FP8X4),
-                        rhs_scale=h_bytes[:],
-                        start=(g == 0),
-                        stop=(g == G - 1),
-                    )
+        ranked = results[:].rearrange("p i (m e u) -> p e i m u", m=R, e=E)
+
+        def second_pass(y, e, g, i, codes, scales):
+            a = e * G + g
+            nc.tensor.matmul_mx(
+                out=y,
+                lhsT=w2[:, a, 2 * P * i : 2 * P * i + 2 * P].bitcast(FP4X4),
+                lhsT_scale=w2_plane[:, a * N + P * i : a * N + P * i + P],
+                rhs=codes.bitcast(FP8X4),
+                rhs_scale=scales,
+                start=(g == 0),
+                stop=(g == G - 1),
+            )
+
+        y0 = yp.tile([P, 2, C], F32, name="y0")
+        y12 = yp.tile([P, 2, 2, C], F32, name="y12")
+        ys = [y0[:], y12[:, 0], y12[:, 1]]
+        for e in range(E - 1):
+            h_codes = keep.tile([P, G * C], U32, name=f"h_codes{e}", align_bytes=64)
+            h_bytes = keep.tile([P, G * C], U8, name=f"h_bytes{e}", align_bytes=64)
+            nc.vector.quantize_mx(h_codes[:].bitcast(FP8X4), h_bytes[:], hidden[e][0][:])
             for i in range(2):
-                nc.vector.tensor_copy(
-                    results[i][:].rearrange("p (m e u) -> p m e u", m=R, e=E)[:, :, e, :],
-                    y[i][:].rearrange("p (m u) -> p m u", m=R),
-                )
-
-        stage_a(0)
-        for e in range(1, E):
-            stage_a(e)
-            stage_b(e - 1)
-        stage_b(E - 1)
-        for i in range(2):
-            nc.sync.dma_start(out[i * P : (i + 1) * P, :], results[i][:])
+                for g in range(G):
+                    second_pass(ys[e][:, i, :], e, g, i, h_codes[:, g * C : (g + 1) * C], h_bytes[:, g * C : (g + 1) * C])
+        e = E - 1
+        last = [yp.tile([P, C], F32, name=f"last{i}") for i in range(2)]
+        for g in range(G):
+            h_codes = keep.tile([P, C], U32, name=f"h_codes{e}_{g}", align_bytes=64)
+            h_bytes = keep.tile([P, C], U8, name=f"h_bytes{e}_{g}", align_bytes=64)
+            nc.vector.quantize_mx(h_codes[:].bitcast(FP8X4), h_bytes[:], hidden[e][g][:])
+            for i in range(2):
+                second_pass(last[i][:], e, g, i, h_codes[:], h_bytes[:])
+        nc.vector.tensor_copy(ranked[:, 0], y0[:].rearrange("p i (m u) -> p i m u", m=R))
+        nc.scalar.copy(ranked[:, 1:3], y12[:].rearrange("p e i (m u) -> p e i m u", m=R))
+        nc.vector.tensor_copy(ranked[:, e, 0], last[0][:].rearrange("p (m u) -> p m u", m=R))
+        nc.scalar.copy(ranked[:, e, 1], last[1][:].rearrange("p (m u) -> p m u", m=R))
+        nc.sync.dma_start(out[0:P, :], results[:, 0, :])
+        nc.scalar.dma_start(out[P : 2 * P, :], results[:, 1, :])

@@ -19,26 +19,28 @@ FP8X4 = mybir.dt.float8_e4m3fn_x4
 FP4X4 = mybir.dt.float4_e2m1fn_x4
 ACT = mybir.ActivationFunctionType
 
-CHUNKS = [(0, 256), (256, 256), (512, 128)]
+CHUNKS = [(0, 256), (256, 128), (384, 128), (512, 128)]
 
 
 def tile_moe_eps_mlp_silu_kernel(tc, xT, w1_words, w1_scales, w2_words, w2_scales, offs, out):
     nc = tc.nc
     with ExitStack() as ctx:
         keep = ctx.enter_context(tc.tile_pool(name="keep", bufs=1))
-        slots = ctx.enter_context(tc.tile_pool(name="slots", bufs=2))
+        shared = [ctx.enter_context(tc.tile_pool(name=f"shared{e}", bufs=1)) for e in range(E - 1)]
         hp = ctx.enter_context(tc.psum_pool(name="hp", bufs=4))
         yp = ctx.enter_context(tc.psum_pool(name="yp", bufs=1))
 
         offsets = keep.tile([P, E * C // 16], U16, name="offsets")
-        raw_scales = keep.tile([P, H], U8, name="raw_scales", align_bytes=64)
+        raw_scales = keep.tile([P, H], U8, name="raw_scales", tag="raw_scales", align_bytes=64)
         perm_scales = keep.tile([P, H], U8, name="perm_scales", align_bytes=64)
-        x_codes = keep.tile([P, T], U32, name="x_codes", align_bytes=64)
-        raw0 = keep.tile([P, 2 * H], U8, name="raw0", tag="raw0", align_bytes=64)
-        raw12 = keep.tile([P, 2 * 2 * H], U8, name="raw12", align_bytes=64)
-        raw3 = keep.tile([P, 2 * H], U8, name="raw3", align_bytes=64)
-        w1_raw = [raw0[:], raw12[:, 0 : 2 * H], raw12[:, 2 * H : 4 * H], raw3[:]]
-        w1 = [keep.tile([P, 2 * H], U8, name=f"w1_{e}", align_bytes=64) for e in range(E)]
+        x_bytes = keep.tile([P, T], U8, name="x_bytes", align_bytes=64)
+        grouped = keep.tile([P, 4 * T], BF16, name="grouped", tag="grouped", align_bytes=64)
+        first_raw = [keep.tile([P, H], U8, name="raw0_0", align_bytes=64), shared[0].tile([P, H], U8, name="raw0_1", align_bytes=64, offset=0)]
+        later_raw = [shared[e].tile([P, 2 * H], U8, name=f"raw{e}", align_bytes=64, offset=0) for e in range(1, E - 1)]
+        later_raw.append(keep.tile([P, 2 * H], U8, name=f"raw{E - 1}", align_bytes=64))
+        w1_raw = [[t[:] for t in first_raw]] + [[t[:, 0:H], t[:, H : 2 * H]] for t in later_raw]
+        w1_first = keep.tile([P, 2 * H], U8, name="w1_first", align_bytes=64)
+        w1 = [w1_first[:]]
         w1_plane = [perm_scales] + [keep.tile([P, H], U8, name=f"w1_plane{e}", align_bytes=64) for e in range(1, E)]
         w2_plane = keep.tile([P, E * G * N], U8, name="w2_plane", align_bytes=64)
         w2 = keep.tile([P, E * G, 2 * N], U8, name="w2", align_bytes=64)
@@ -50,6 +52,7 @@ def tile_moe_eps_mlp_silu_kernel(tc, xT, w1_words, w1_scales, w2_words, w2_scale
         nc.vector.memset(raw_scales[:].bitcast(I32), 0)
         nc.vector.memset(warm[:], 0.0)
         nc.scalar.activation(warm_out[:], warm[:], ACT.Silu)
+        nc.vector.memset(x_bytes[:].bitcast(I32), 0)
         for e in range(1, E):
             nc.vector.memset(w1_plane[e][:].bitcast(I32), 0)
         nc.vector.memset(w2_plane[:].bitcast(I32), 0)
@@ -58,19 +61,26 @@ def tile_moe_eps_mlp_silu_kernel(tc, xT, w1_words, w1_scales, w2_words, w2_scale
             c0, w = CHUNKS[i]
             nc.sync.dma_start(x_raw[i][:], xT[:, c0 : c0 + w].rearrange("(p j) w -> p j w", j=4))
 
+        def load_words(e):
+            nc.sync.dma_start(later_raw[e - 1][:].bitcast(I32), w1_words[e, 0].bitcast(I32))
+
         load_x(0)
         for q in range(4):
             nc.sync.dma_start(raw_scales[32 * q : 32 * q + 16, :].bitcast(I32), w1_scales[:, 0, 4 * q : 4 * q + 4, :].bitcast(I32))
-        nc.sync.dma_start(raw0[:].bitcast(I32), w1_words[0, 0].bitcast(I32))
         load_x(1)
         load_x(2)
+        load_x(3)
+        nc.sync.dma_start(first_raw[0][:].bitcast(I32), w1_words[0, 0, :, 0:H].bitcast(I32))
         nc.sync.dma_start(offsets[:], offs)
-        nc.sync.dma_start(raw12[:].rearrange("p (e b) -> p e b", e=2).bitcast(I32), w1_words[1:3, 0].rearrange("e p b -> p e b").bitcast(I32))
+        nc.sync.dma_start(first_raw[1][:].bitcast(I32), w1_words[0, 0, :, H : 2 * H].bitcast(I32))
+        load_words(1)
+        load_words(2)
 
-        def permute_words(e):
+        def permute_words(e, g):
+            half = slice(g * H, (g + 1) * H)
             nc.vector.tensor_copy(
-                w1[e][:].bitcast(U16).rearrange("p (g t m) -> p g t m", g=G, t=4),
-                w1_raw[e].bitcast(U16).rearrange("p (g m t) -> p g t m", g=G, t=4),
+                w1[e][:, half].bitcast(U16).rearrange("p (t m) -> p t m", t=4),
+                w1_raw[e][g].bitcast(U16).rearrange("p (m t) -> p t m", t=4),
             )
 
         def move_scales(e):
@@ -81,7 +91,7 @@ def tile_moe_eps_mlp_silu_kernel(tc, xT, w1_words, w1_scales, w2_words, w2_scale
             raw_scales[:].rearrange("p (g m t) -> p g t m", g=G, t=4),
         )
         move_scales(1)
-        nc.sync.dma_start(raw3[:].bitcast(I32), w1_words[3, 0].bitcast(I32))
+        load_words(3)
         move_scales(2)
         move_scales(3)
         for q in range(4):
@@ -90,40 +100,47 @@ def tile_moe_eps_mlp_silu_kernel(tc, xT, w1_words, w1_scales, w2_words, w2_scale
                 w2_scales[:, :, 4 * q : 4 * q + 4, :].rearrange("e s q n -> q (e s) n").bitcast(I32),
             )
         nc.sync.dma_start(w2[:].bitcast(I32), w2_words.rearrange("e s p b -> p (e s) b").bitcast(I32))
-        permute_words(0)
-        x_bytes = keep.tile([P, T], U8, name="x_bytes", tag="raw0", align_bytes=64)
-        nc.vector.memset(x_bytes[:].bitcast(I32), 0)
+        x_codes = keep.tile([P, T], U32, name="x_codes", tag="raw_scales", align_bytes=64)
 
         def cast(chunk, c, w, on_scalar):
-            grouped = keep.tile([P, 4 * w], BF16, name=f"grouped{chunk}_{c}", align_bytes=64)
-            dst = grouped[:].rearrange("p (c i j) -> p c j i", i=4, j=4)
+            t0 = CHUNKS[chunk][0] + c
+            dst = grouped[:, 4 * t0 : 4 * (t0 + w)].rearrange("p (c i j) -> p c j i", i=4, j=4)
             src = x_raw[chunk][:, :, c : c + w].rearrange("p j (c i) -> p c j i", i=4)
             if on_scalar:
                 nc.scalar.activation(dst, src, ACT.Copy)
             else:
                 nc.vector.tensor_copy(dst, src)
-            return grouped
 
-        def quantise(grouped, c0, w):
-            nc.vector.quantize_mx(x_codes[:, c0 : c0 + w].bitcast(FP8X4), x_bytes[:, c0 : c0 + w], grouped[:])
+        def quantise(c0, w):
+            nc.vector.quantize_mx(x_codes[:, c0 : c0 + w].bitcast(FP8X4), x_bytes[:, c0 : c0 + w], grouped[:, 4 * c0 : 4 * (c0 + w)])
 
-        quantise(cast(0, 0, 256, True), 0, 256)
-        first = cast(1, 0, P, False)
-        second = cast(1, P, P, True)
-        quantise(first, 256, P)
-        third = cast(2, 0, P, False)
-        quantise(second, 384, P)
-        quantise(third, 512, P)
+        cast(0, 0, 128, False)
+        cast(0, 128, 128, True)
+        quantise(0, 256)
+        cast(1, 0, 128, True)
+        cast(2, 0, 64, False)
+        cast(2, 64, 64, True)
+        quantise(256, 128)
+        cast(3, 0, 80, False)
+        cast(3, 80, 48, True)
+        quantise(384, 128)
+        quantise(512, 128)
 
+        w1_rest = keep.tile([P, (E - 1) * 2 * H], U8, name="w1_rest", tag="grouped", align_bytes=64)
+        w1.extend(w1_rest[:, e * 2 * H : (e + 1) * 2 * H] for e in range(E - 1))
         hidden = []
         for e in range(E):
-            if e > 0:
-                permute_words(e)
+            permute_words(e, 0)
             lst = offsets[:, 8 * e : 8 * e + 8]
-            s_codes = slots.tile([P, C], U32, name="s_codes", align_bytes=64)
-            s_bytes = slots.tile([P, C], U8, name="s_bytes", align_bytes=64)
+            if e == 0:
+                s_codes = keep.tile([P, C], U32, name="s_codes0", align_bytes=64)
+                s_bytes = keep.tile([P, C], U8, name="s_bytes0", align_bytes=64)
+            else:
+                s_codes = shared[e - 1].tile([P, C], U32, name=f"s_codes{e}", align_bytes=64, offset=0)
+                s_bytes = shared[e - 1].tile([P, C], U8, name=f"s_bytes{e}", align_bytes=64, offset=4 * C)
             nc.vector.tensor_copy(s_codes[:], x_codes[:].indirect(lst))
             nc.vector.tensor_copy(s_bytes[:], x_bytes[:].indirect(lst))
+            permute_words(e, 1)
             h = [keep.tile([P, G * C * 4], BF16, name=f"h{e}", align_bytes=64)]
             if e == E - 1:
                 h = [keep.tile([P, C * 4], BF16, name=f"h{e}_{g}", align_bytes=64) for g in range(G)]

@@ -1,6 +1,7 @@
 from contextlib import ExitStack
 
 import concourse.mybir as mybir
+from concourse.masks import make_identity
 
 FLOPS = 805306368
 
@@ -19,29 +20,32 @@ FP8X4 = mybir.dt.float8_e4m3fn_x4
 FP4X4 = mybir.dt.float4_e2m1fn_x4
 ACT = mybir.ActivationFunctionType
 
-CHUNKS = [(0, 256), (256, 128), (384, 128), (512, 128)]
+CHUNKS = [(0, 240), (240, 144), (384, 128), (512, 128)]
 
 
 def tile_moe_eps_mlp_silu_kernel(tc, xT, w1_words, w1_scales, w2_words, w2_scales, offs, out):
     nc = tc.nc
     with ExitStack() as ctx:
         keep = ctx.enter_context(tc.tile_pool(name="keep", bufs=1))
-        shared = [ctx.enter_context(tc.tile_pool(name=f"shared{e}", bufs=1)) for e in range(E - 1)]
-        hp = ctx.enter_context(tc.psum_pool(name="hp", bufs=4))
+        shared = [ctx.enter_context(tc.tile_pool(name=f"shared{e}", bufs=1)) for e in range(E - 2)]
+        hp = ctx.enter_context(tc.psum_pool(name="hp", bufs=1))
         yp = ctx.enter_context(tc.psum_pool(name="yp", bufs=1))
 
         offsets = keep.tile([P, E * C // 16], U16, name="offsets")
-        raw_scales = keep.tile([P, H], U8, name="raw_scales", tag="raw_scales", align_bytes=64)
+        raw_scales = keep.tile([P, H], U8, name="raw_scales", align_bytes=64)
         perm_scales = keep.tile([P, H], U8, name="perm_scales", align_bytes=64)
         x_bytes = keep.tile([P, T], U8, name="x_bytes", align_bytes=64)
         grouped = keep.tile([P, 4 * T], BF16, name="grouped", tag="grouped", align_bytes=64)
-        first_raw = [keep.tile([P, H], U8, name="raw0_0", align_bytes=64), shared[0].tile([P, H], U8, name="raw0_1", align_bytes=64, offset=0)]
-        later_raw = [shared[e].tile([P, 2 * H], U8, name=f"raw{e}", align_bytes=64, offset=0) for e in range(1, E - 1)]
-        later_raw.append(keep.tile([P, 2 * H], U8, name=f"raw{E - 1}", align_bytes=64))
-        w1_raw = [[t[:] for t in first_raw]] + [[t[:, 0:H], t[:, H : 2 * H]] for t in later_raw]
-        w1_first = keep.tile([P, 2 * H], U8, name="w1_first", align_bytes=64)
-        w1 = [w1_first[:]]
-        w1_plane = [perm_scales] + [keep.tile([P, H], U8, name=f"w1_plane{e}", align_bytes=64) for e in range(1, E)]
+        raw0 = keep.tile([P, 2 * H], U8, name="raw0", align_bytes=64)
+        raw1 = [keep.tile([P, H], U8, name="raw1_0", align_bytes=64), shared[0].tile([P, H], U8, name="raw1_1", align_bytes=64, offset=0)]
+        raw2 = shared[1].tile([P, 2 * H], U8, name="raw2", align_bytes=64, offset=0)
+        raw3 = keep.tile([P, 2 * H], U8, name="raw3", align_bytes=64)
+        w1_raw = [None, [t[:] for t in raw1]] + [[t[:, 0:H], t[:, H : 2 * H]] for t in (raw2, raw3)]
+        w1_second = keep.tile([P, 2 * H], U8, name="w1_second", align_bytes=64)
+        w1 = [None, w1_second[:]]
+        identity = keep.tile([P, P], F32, name="identity")
+        make_identity(nc, identity[:])
+        w1_plane = [raw_scales] + [keep.tile([P, H], U8, name=f"w1_plane{e}", align_bytes=64) for e in range(1, E)]
         w2_plane = keep.tile([P, E * G * N], U8, name="w2_plane", align_bytes=64)
         w2 = keep.tile([P, E * G, 2 * N], U8, name="w2", align_bytes=64)
         x_raw = [keep.tile([P, 4, w], F32, name=f"x_raw{i}", align_bytes=64) for i, (c0, w) in enumerate(CHUNKS)]
@@ -61,8 +65,8 @@ def tile_moe_eps_mlp_silu_kernel(tc, xT, w1_words, w1_scales, w2_words, w2_scale
             c0, w = CHUNKS[i]
             nc.sync.dma_start(x_raw[i][:], xT[:, c0 : c0 + w].rearrange("(p j) w -> p j w", j=4))
 
-        def load_words(e):
-            nc.sync.dma_start(later_raw[e - 1][:].bitcast(I32), w1_words[e, 0].bitcast(I32))
+        def load_words(tile, words):
+            nc.sync.dma_start(tile[:].bitcast(I32), words.bitcast(I32))
 
         load_x(0)
         for q in range(4):
@@ -70,11 +74,11 @@ def tile_moe_eps_mlp_silu_kernel(tc, xT, w1_words, w1_scales, w2_words, w2_scale
         load_x(1)
         load_x(2)
         load_x(3)
-        nc.sync.dma_start(first_raw[0][:].bitcast(I32), w1_words[0, 0, :, 0:H].bitcast(I32))
+        load_words(raw1[0], w1_words[1, 0, :, 0:H])
         nc.sync.dma_start(offsets[:], offs)
-        nc.sync.dma_start(first_raw[1][:].bitcast(I32), w1_words[0, 0, :, H : 2 * H].bitcast(I32))
-        load_words(1)
-        load_words(2)
+        load_words(raw0, w1_words[0, 0])
+        load_words(raw1[1], w1_words[1, 0, :, H : 2 * H])
+        load_words(raw2, w1_words[2, 0])
 
         def permute_words(e, g):
             half = slice(g * H, (g + 1) * H)
@@ -91,8 +95,8 @@ def tile_moe_eps_mlp_silu_kernel(tc, xT, w1_words, w1_scales, w2_words, w2_scale
             raw_scales[:].rearrange("p (g m t) -> p g t m", g=G, t=4),
         )
         move_scales(1)
-        load_words(3)
         move_scales(2)
+        load_words(raw3, w1_words[3, 0])
         move_scales(3)
         for q in range(4):
             nc.sync.dma_start(
@@ -100,7 +104,7 @@ def tile_moe_eps_mlp_silu_kernel(tc, xT, w1_words, w1_scales, w2_words, w2_scale
                 w2_scales[:, :, 4 * q : 4 * q + 4, :].rearrange("e s q n -> q (e s) n").bitcast(I32),
             )
         nc.sync.dma_start(w2[:].bitcast(I32), w2_words.rearrange("e s p b -> p (e s) b").bitcast(I32))
-        x_codes = keep.tile([P, T], U32, name="x_codes", tag="raw_scales", align_bytes=64)
+        x_codes = keep.tile([P, T], U32, name="x_codes", align_bytes=64)
 
         def cast(chunk, c, w, on_scalar):
             t0 = CHUNKS[chunk][0] + c
@@ -114,10 +118,11 @@ def tile_moe_eps_mlp_silu_kernel(tc, xT, w1_words, w1_scales, w2_words, w2_scale
         def quantise(c0, w):
             nc.vector.quantize_mx(x_codes[:, c0 : c0 + w].bitcast(FP8X4), x_bytes[:, c0 : c0 + w], grouped[:, 4 * c0 : 4 * (c0 + w)])
 
-        cast(0, 0, 128, False)
-        cast(0, 128, 128, True)
+        cast(0, 0, 112, False)
+        cast(0, 112, 128, True)
+        cast(1, 0, 80, False)
+        cast(1, 80, 64, True)
         quantise(0, 256)
-        cast(1, 0, 128, True)
         cast(2, 0, 64, False)
         cast(2, 64, 64, True)
         quantise(256, 128)
@@ -126,26 +131,70 @@ def tile_moe_eps_mlp_silu_kernel(tc, xT, w1_words, w1_scales, w2_words, w2_scale
         quantise(384, 128)
         quantise(512, 128)
 
-        w1_rest = keep.tile([P, (E - 1) * 2 * H], U8, name="w1_rest", tag="grouped", align_bytes=64)
-        w1.extend(w1_rest[:, e * 2 * H : (e + 1) * 2 * H] for e in range(E - 1))
+        w1_rest = keep.tile([P, (E - 2) * 2 * H], U8, name="w1_rest", tag="grouped", align_bytes=64)
+        w1.extend(w1_rest[:, e * 2 * H : (e + 1) * 2 * H] for e in range(E - 2))
+        zeros = keep.tile([P, 4 * P], BF16, name="zeros", align_bytes=64)
+        zero_codes = keep.tile([P, P], U32, name="zero_codes", align_bytes=64)
+        zero_bytes = keep.tile([P, P], U8, name="zero_bytes", align_bytes=64)
+        nc.vector.memset(zeros[:], 0.0)
+        nc.vector.quantize_mx(zero_codes[:].bitcast(FP8X4), zero_bytes[:], zeros[:])
+        unused = yp.tile([P, 512], F32, name="unused", tag="last0")
+        for width in (512, 512, 256):
+            nc.tensor.matmul_mx(
+                out=unused[:, 0:width],
+                lhsT=zero_codes[:].bitcast(FP8X4),
+                lhsT_scale=zero_bytes[:],
+                rhs=raw1[0][:, 0 : 2 * width].bitcast(FP4X4),
+                rhs_scale=raw_scales[:, 0:width],
+                start=True,
+                stop=True,
+            )
         hidden = []
+        bank_of = {(0, 0): 0, (0, 1): 1, (1, 0): 2, (1, 1): 3, (2, 0): 0, (2, 1): 1, (3, 0): 3, (3, 1): 0}
+        by_slot = keep.tile([P, H], BF16, name="by_slot", align_bytes=64)
+        permute_words(1, 0)
         for e in range(E):
-            permute_words(e, 0)
+            if e > 1:
+                permute_words(e, 0)
+            if e == E - 1:
+                turned = hp.tile([P, 2 * G, C], F32, name="turned", tag="bank2")
+                for q in range(2 * G):
+                    nc.tensor.transpose(turned[:, q, :], by_slot[:].bitcast(F32)[:, q * P : (q + 1) * P], identity[:])
             lst = offsets[:, 8 * e : 8 * e + 8]
-            if e == 0:
-                s_codes = keep.tile([P, C], U32, name="s_codes0", align_bytes=64)
-                s_bytes = keep.tile([P, C], U8, name="s_bytes0", align_bytes=64)
+            if e < 2:
+                s_codes = keep.tile([P, C], U32, name=f"s_codes{e}", align_bytes=64)
+                s_bytes = keep.tile([P, C], U8, name=f"s_bytes{e}", align_bytes=64)
             else:
-                s_codes = shared[e - 1].tile([P, C], U32, name=f"s_codes{e}", align_bytes=64, offset=0)
-                s_bytes = shared[e - 1].tile([P, C], U8, name=f"s_bytes{e}", align_bytes=64, offset=4 * C)
+                s_codes = shared[e - 2].tile([P, C], U32, name=f"s_codes{e}", align_bytes=64, offset=0)
+                s_bytes = shared[e - 2].tile([P, C], U8, name=f"s_bytes{e}", align_bytes=64, offset=4 * C)
             nc.vector.tensor_copy(s_codes[:], x_codes[:].indirect(lst))
             nc.vector.tensor_copy(s_bytes[:], x_bytes[:].indirect(lst))
-            permute_words(e, 1)
+            if e > 0:
+                permute_words(e, 1)
             h = [keep.tile([P, G * C * 4], BF16, name=f"h{e}", align_bytes=64)]
             if e == E - 1:
                 h = [keep.tile([P, C * 4], BF16, name=f"h{e}_{g}", align_bytes=64) for g in range(G)]
             for g in range(G):
-                a = hp.tile([P, 4, C], F32, name="a")
+                a = hp.tile([P, 4, C], F32, name=f"a{e}_{g}", tag=f"bank{bank_of[e, g]}")
+                if e == 0:
+                    first = yp.tile([P, 256], F32, name=f"first{g}", tag=("y0", "y12")[g])
+                    for half, sums in enumerate((first[:], a[:].rearrange("p t n -> p (t n)")[:, 0:256])):
+                        c = g * 512 + half * 256
+                        nc.tensor.matmul_mx(
+                            out=sums,
+                            lhsT=s_codes[:].bitcast(FP8X4),
+                            lhsT_scale=s_bytes[:],
+                            rhs=raw0[:, 2 * c : 2 * c + 512].bitcast(FP4X4),
+                            rhs_scale=raw_scales[:, c : c + 256],
+                            start=True,
+                            stop=True,
+                        )
+                        nc.scalar.activation(
+                            by_slot[:, g * 512 : (g + 1) * 512].rearrange("s (u p d) -> s u p d", u=2, d=2)[:, :, half * 64 : (half + 1) * 64, :],
+                            sums.rearrange("s (p u d) -> s u p d", u=2, d=2),
+                            ACT.Silu,
+                        )
+                    continue
                 for t in range(4):
                     c = g * 512 + t * P
                     nc.tensor.matmul_mx(
@@ -161,6 +210,10 @@ def tile_moe_eps_mlp_silu_kernel(tc, xT, w1_words, w1_scales, w2_words, w2_scale
                 nc.scalar.activation(dst.rearrange("p (n t) -> p n t", t=4), a[:].rearrange("p t n -> p n t"), ACT.Silu)
             hidden.append(h)
 
+        nc.vector.tensor_copy(
+            hidden[0][0][:].bitcast(F32).rearrange("p (g s u) -> p g s u", g=G, u=2),
+            turned[:].rearrange("p (g u) s -> p g s u", u=2),
+        )
         ranked = results[:].rearrange("p i (m e u) -> p e i m u", m=R, e=E)
 
         def second_pass(y, e, g, i, codes, scales):
@@ -175,8 +228,8 @@ def tile_moe_eps_mlp_silu_kernel(tc, xT, w1_words, w1_scales, w2_words, w2_scale
                 stop=(g == G - 1),
             )
 
-        y0 = yp.tile([P, 2, C], F32, name="y0")
-        y12 = yp.tile([P, 2, 2, C], F32, name="y12")
+        y0 = yp.tile([P, 2, C], F32, name="y0", tag="y0")
+        y12 = yp.tile([P, 2, 2, C], F32, name="y12", tag="y12")
         ys = [y0[:], y12[:, 0], y12[:, 1]]
         for e in range(E - 1):
             h_codes = keep.tile([P, G * C], U32, name=f"h_codes{e}", align_bytes=64)
@@ -186,7 +239,7 @@ def tile_moe_eps_mlp_silu_kernel(tc, xT, w1_words, w1_scales, w2_words, w2_scale
                 for g in range(G):
                     second_pass(ys[e][:, i, :], e, g, i, h_codes[:, g * C : (g + 1) * C], h_bytes[:, g * C : (g + 1) * C])
         e = E - 1
-        last = [yp.tile([P, C], F32, name=f"last{i}") for i in range(2)]
+        last = [yp.tile([P, C], F32, name=f"last{i}", tag=f"last{i}") for i in range(2)]
         for g in range(G):
             h_codes = keep.tile([P, C], U32, name=f"h_codes{e}_{g}", align_bytes=64)
             h_bytes = keep.tile([P, C], U8, name=f"h_bytes{e}_{g}", align_bytes=64)

@@ -20,91 +20,83 @@ FP8X4 = mybir.dt.float8_e4m3fn_x4
 FP4X4 = mybir.dt.float4_e2m1fn_x4
 ACT = mybir.ActivationFunctionType
 
-CHUNKS = [(0, 240), (240, 144), (384, 128), (512, 128)]
+CHUNKS = [(0, 128), (128, 128), (256, 128), (384, 128), (512, 128)]
 
 
 def tile_moe_eps_mlp_silu_kernel(tc, xT, w1_words, w1_scales, w2_words, w2_scales, offs, out):
     nc = tc.nc
     with ExitStack() as ctx:
         keep = ctx.enter_context(tc.tile_pool(name="keep", bufs=1))
-        shared = [ctx.enter_context(tc.tile_pool(name=f"shared{e}", bufs=1)) for e in range(E - 2)]
-        hp = ctx.enter_context(tc.psum_pool(name="hp", bufs=1))
-        yp = ctx.enter_context(tc.psum_pool(name="yp", bufs=1))
+        banks = ctx.enter_context(tc.psum_pool(name="banks", bufs=1))
 
         offsets = keep.tile([P, E * C // 16], U16, name="offsets")
-        raw_scales = keep.tile([P, H], U8, name="raw_scales", align_bytes=64)
-        perm_scales = keep.tile([P, H], U8, name="perm_scales", align_bytes=64)
+        packed = keep.tile([P, H], U8, name="packed", align_bytes=64)
+        permuted = keep.tile([P, H], U8, name="permuted", align_bytes=64)
+        moved = keep.tile([P, H], U8, name="moved", align_bytes=64)
+        plain = keep.tile([P, 2 * H], U8, name="plain", align_bytes=64)
         x_bytes = keep.tile([P, T], U8, name="x_bytes", align_bytes=64)
-        grouped = keep.tile([P, 4 * T], BF16, name="grouped", tag="grouped", align_bytes=64)
-        raw0 = keep.tile([P, 2 * H], U8, name="raw0", align_bytes=64)
-        raw1 = [keep.tile([P, H], U8, name="raw1_0", align_bytes=64), shared[0].tile([P, H], U8, name="raw1_1", align_bytes=64, offset=0)]
-        raw2 = shared[1].tile([P, 2 * H], U8, name="raw2", align_bytes=64, offset=0)
-        raw3 = keep.tile([P, 2 * H], U8, name="raw3", align_bytes=64)
-        w1_raw = [None, [t[:] for t in raw1]] + [[t[:, 0:H], t[:, H : 2 * H]] for t in (raw2, raw3)]
-        w1_second = keep.tile([P, 2 * H], U8, name="w1_second", align_bytes=64)
-        w1 = [None, w1_second[:]]
+        x_codes = keep.tile([P, T], U32, name="x_codes", align_bytes=64)
+        grouped = keep.tile([P, 4 * T], BF16, name="grouped", align_bytes=64)
+        raw = [keep.tile([P, 2 * H], U8, name=f"raw{e}", align_bytes=64) for e in range(E)]
+        w1 = {e: keep.tile([P, 2 * H], U8, name=f"w1_{e}", align_bytes=64) for e in (2, 3)}
+        w1_plane = {2: permuted, 3: moved}
         identity = keep.tile([P, P], F32, name="identity")
         make_identity(nc, identity[:])
-        w1_plane = [raw_scales] + [keep.tile([P, H], U8, name=f"w1_plane{e}", align_bytes=64) for e in range(1, E)]
         w2_plane = keep.tile([P, E * G * N], U8, name="w2_plane", align_bytes=64)
         w2 = keep.tile([P, E * G, 2 * N], U8, name="w2", align_bytes=64)
         x_raw = [keep.tile([P, 4, w], F32, name=f"x_raw{i}", align_bytes=64) for i, (c0, w) in enumerate(CHUNKS)]
         results = keep.tile([P, 2, E * C], F32, name="results")
         warm = keep.tile([P, 1], F32, name="warm")
         warm_out = keep.tile([P, 1], F32, name="warm_out")
+        zeros = keep.tile([P, 4 * P], BF16, name="zeros", align_bytes=64)
+        zero_codes = keep.tile([P, P], U32, name="zero_codes", align_bytes=64)
+        zero_bytes = keep.tile([P, P], U8, name="zero_bytes", align_bytes=64)
 
-        nc.vector.memset(raw_scales[:].bitcast(I32), 0)
+        nc.vector.memset(packed[:].bitcast(I32), 0)
         nc.vector.memset(warm[:], 0.0)
         nc.scalar.activation(warm_out[:], warm[:], ACT.Silu)
         nc.vector.memset(x_bytes[:].bitcast(I32), 0)
-        for e in range(1, E):
-            nc.vector.memset(w1_plane[e][:].bitcast(I32), 0)
+        nc.vector.memset(plain[:].bitcast(I32), 0)
+        nc.vector.memset(moved[:].bitcast(I32), 0)
         nc.vector.memset(w2_plane[:].bitcast(I32), 0)
+        nc.vector.memset(zeros[:], 0.0)
+        nc.vector.quantize_mx(zero_codes[:].bitcast(FP8X4), zero_bytes[:], zeros[:])
 
         def load_x(i):
             c0, w = CHUNKS[i]
             nc.sync.dma_start(x_raw[i][:], xT[:, c0 : c0 + w].rearrange("(p j) w -> p j w", j=4))
 
-        def load_words(tile, words):
-            nc.sync.dma_start(tile[:].bitcast(I32), words.bitcast(I32))
+        def load_words(e):
+            nc.sync.dma_start(raw[e][:].bitcast(I32), w1_words[e, 0].bitcast(I32))
 
         load_x(0)
-        for q in range(4):
-            nc.sync.dma_start(raw_scales[32 * q : 32 * q + 16, :].bitcast(I32), w1_scales[:, 0, 4 * q : 4 * q + 4, :].bitcast(I32))
         load_x(1)
+        for r in range(4):
+            nc.sync.dma_start(packed[r:P:16, :].bitcast(I32), w1_scales[2:4, 0, r:16:4, :].rearrange("e q n -> q e n").bitcast(I32))
         load_x(2)
         load_x(3)
-        load_words(raw1[0], w1_words[1, 0, :, 0:H])
+        load_x(4)
+        load_words(0)
         nc.sync.dma_start(offsets[:], offs)
-        load_words(raw0, w1_words[0, 0])
-        load_words(raw1[1], w1_words[1, 0, :, H : 2 * H])
-        load_words(raw2, w1_words[2, 0])
-
-        def permute_words(e, g):
-            half = slice(g * H, (g + 1) * H)
-            nc.vector.tensor_copy(
-                w1[e][:, half].bitcast(U16).rearrange("p (t m) -> p t m", t=4),
-                w1_raw[e][g].bitcast(U16).rearrange("p (m t) -> p t m", t=4),
+        for q in range(4):
+            nc.sync.dma_start(
+                plain[32 * q : 32 * q + 4].rearrange("p (e n) -> p e n", e=2).bitcast(I32),
+                w1_scales[0:2, 0, 4 * q : 4 * q + 4, :].rearrange("e r n -> r e n").bitcast(I32),
             )
-
-        def move_scales(e):
-            nc.sync.dma_start(w1_plane[e][0:112, :].bitcast(I32), perm_scales[4 * e : 4 * e + 112, :].bitcast(I32))
-
+        load_words(1)
+        load_words(2)
+        load_words(3)
         nc.vector.tensor_copy(
-            perm_scales[:].rearrange("p (g t m) -> p g t m", g=G, t=4),
-            raw_scales[:].rearrange("p (g m t) -> p g t m", g=G, t=4),
+            permuted[:].rearrange("p (g t m) -> p g t m", g=G, t=4),
+            packed[:].rearrange("p (g m t) -> p g t m", g=G, t=4),
         )
-        move_scales(1)
-        move_scales(2)
-        load_words(raw3, w1_words[3, 0])
-        move_scales(3)
+        nc.sync.dma_start(moved[0:112, :].bitcast(I32), permuted[16:P, :].bitcast(I32))
         for q in range(4):
             nc.sync.dma_start(
                 w2_plane[32 * q : 32 * q + 4].rearrange("p (a n) -> p a n", n=N).bitcast(I32),
                 w2_scales[:, :, 4 * q : 4 * q + 4, :].rearrange("e s q n -> q (e s) n").bitcast(I32),
             )
         nc.sync.dma_start(w2[:].bitcast(I32), w2_words.rearrange("e s p b -> p (e s) b").bitcast(I32))
-        x_codes = keep.tile([P, T], U32, name="x_codes", align_bytes=64)
 
         def cast(chunk, c, w, on_scalar):
             t0 = CHUNKS[chunk][0] + c
@@ -118,103 +110,104 @@ def tile_moe_eps_mlp_silu_kernel(tc, xT, w1_words, w1_scales, w2_words, w2_scale
         def quantise(c0, w):
             nc.vector.quantize_mx(x_codes[:, c0 : c0 + w].bitcast(FP8X4), x_bytes[:, c0 : c0 + w], grouped[:, 4 * c0 : 4 * (c0 + w)])
 
-        cast(0, 0, 112, False)
-        cast(0, 112, 128, True)
-        cast(1, 0, 80, False)
-        cast(1, 80, 64, True)
-        quantise(0, 256)
-        cast(2, 0, 64, False)
-        cast(2, 64, 64, True)
+        cast(0, 0, 128, True)
+        quantise(0, 128)
+        cast(1, 0, 32, False)
+        cast(1, 32, 96, True)
+        quantise(128, 128)
+        cast(2, 0, 128, True)
+        cast(3, 0, 32, False)
+        cast(3, 32, 96, True)
         quantise(256, 128)
-        cast(3, 0, 80, False)
-        cast(3, 80, 48, True)
+        cast(4, 0, 80, False)
+        cast(4, 80, 48, True)
         quantise(384, 128)
         quantise(512, 128)
 
-        w1_rest = keep.tile([P, (E - 2) * 2 * H], U8, name="w1_rest", tag="grouped", align_bytes=64)
-        w1.extend(w1_rest[:, e * 2 * H : (e + 1) * 2 * H] for e in range(E - 2))
-        zeros = keep.tile([P, 4 * P], BF16, name="zeros", align_bytes=64)
-        zero_codes = keep.tile([P, P], U32, name="zero_codes", align_bytes=64)
-        zero_bytes = keep.tile([P, P], U8, name="zero_bytes", align_bytes=64)
-        nc.vector.memset(zeros[:], 0.0)
-        nc.vector.quantize_mx(zero_codes[:].bitcast(FP8X4), zero_bytes[:], zeros[:])
-        unused = yp.tile([P, 512], F32, name="unused", tag="last0")
-        for width in (512, 512, 256):
+        unused = banks.tile([P, 512], F32, name="unused", tag="bank7")
+        for width in (512, 512):
             nc.tensor.matmul_mx(
                 out=unused[:, 0:width],
                 lhsT=zero_codes[:].bitcast(FP8X4),
                 lhsT_scale=zero_bytes[:],
-                rhs=raw1[0][:, 0 : 2 * width].bitcast(FP4X4),
-                rhs_scale=raw_scales[:, 0:width],
+                rhs=raw[0][:, 0 : 2 * width].bitcast(FP4X4),
+                rhs_scale=packed[:, 0:width],
                 start=True,
                 stop=True,
             )
-        hidden = []
-        bank_of = {(0, 0): 0, (0, 1): 1, (1, 0): 2, (1, 1): 3, (2, 0): 0, (2, 1): 1, (3, 0): 3, (3, 1): 0}
-        by_slot = keep.tile([P, H], BF16, name="by_slot", align_bytes=64)
-        permute_words(1, 0)
-        for e in range(E):
-            if e > 1:
-                permute_words(e, 0)
-            if e == E - 1:
-                turned = hp.tile([P, 2 * G, C], F32, name="turned", tag="bank2")
-                for q in range(2 * G):
-                    nc.tensor.transpose(turned[:, q, :], by_slot[:].bitcast(F32)[:, q * P : (q + 1) * P], identity[:])
-            lst = offsets[:, 8 * e : 8 * e + 8]
-            if e < 2:
-                s_codes = keep.tile([P, C], U32, name=f"s_codes{e}", align_bytes=64)
-                s_bytes = keep.tile([P, C], U8, name=f"s_bytes{e}", align_bytes=64)
-            else:
-                s_codes = shared[e - 2].tile([P, C], U32, name=f"s_codes{e}", align_bytes=64, offset=0)
-                s_bytes = shared[e - 2].tile([P, C], U8, name=f"s_bytes{e}", align_bytes=64, offset=4 * C)
-            nc.vector.tensor_copy(s_codes[:], x_codes[:].indirect(lst))
-            nc.vector.tensor_copy(s_bytes[:], x_bytes[:].indirect(lst))
-            if e > 0:
-                permute_words(e, 1)
-            h = [keep.tile([P, G * C * 4], BF16, name=f"h{e}", align_bytes=64)]
-            if e == E - 1:
-                h = [keep.tile([P, C * 4], BF16, name=f"h{e}_{g}", align_bytes=64) for g in range(G)]
-            for g in range(G):
-                a = hp.tile([P, 4, C], F32, name=f"a{e}_{g}", tag=f"bank{bank_of[e, g]}")
-                if e == 0:
-                    first = yp.tile([P, 256], F32, name=f"first{g}", tag=("y0", "y12")[g])
-                    for half, sums in enumerate((first[:], a[:].rearrange("p t n -> p (t n)")[:, 0:256])):
-                        c = g * 512 + half * 256
-                        nc.tensor.matmul_mx(
-                            out=sums,
-                            lhsT=s_codes[:].bitcast(FP8X4),
-                            lhsT_scale=s_bytes[:],
-                            rhs=raw0[:, 2 * c : 2 * c + 512].bitcast(FP4X4),
-                            rhs_scale=raw_scales[:, c : c + 256],
-                            start=True,
-                            stop=True,
-                        )
-                        nc.scalar.activation(
-                            by_slot[:, g * 512 : (g + 1) * 512].rearrange("s (u p d) -> s u p d", u=2, d=2)[:, :, half * 64 : (half + 1) * 64, :],
-                            sums.rearrange("s (p u d) -> s u p d", u=2, d=2),
-                            ACT.Silu,
-                        )
-                    continue
-                for t in range(4):
-                    c = g * 512 + t * P
-                    nc.tensor.matmul_mx(
-                        out=a[:, t, :],
-                        lhsT=w1[e][:, 2 * c : 2 * c + 2 * P].bitcast(FP4X4),
-                        lhsT_scale=w1_plane[e][:, c : c + P],
-                        rhs=s_codes[:].bitcast(FP8X4),
-                        rhs_scale=s_bytes[:],
-                        start=True,
-                        stop=True,
-                    )
-                dst = h[g][:] if e == E - 1 else h[0][:, g * 4 * C : (g + 1) * 4 * C]
-                nc.scalar.activation(dst.rearrange("p (n t) -> p n t", t=4), a[:].rearrange("p t n -> p n t"), ACT.Silu)
-            hidden.append(h)
 
-        nc.vector.tensor_copy(
-            hidden[0][0][:].bitcast(F32).rearrange("p (g s u) -> p g s u", g=G, u=2),
-            turned[:].rearrange("p (g u) s -> p g s u", u=2),
-        )
-        ranked = results[:].rearrange("p i (m e u) -> p e i m u", m=R, e=E)
+        def gather(name, e0, count):
+            lst = offsets[:, 8 * e0 : 8 * (e0 + count)]
+            codes = keep.tile([P, count * C], U32, name=f"{name}_codes", align_bytes=64)
+            scales = keep.tile([P, count * C], U8, name=f"{name}_bytes", align_bytes=64)
+            nc.vector.tensor_copy(codes[:], x_codes[:].indirect(lst))
+            nc.vector.tensor_copy(scales[:], x_bytes[:].indirect(lst))
+            return [(codes[:, i * C : (i + 1) * C], scales[:, i * C : (i + 1) * C]) for i in range(count)]
+
+        slots = gather("s0", 0, 1) + gather("s1", 1, 1) + gather("s23", 2, 2)
+        by_slot = [keep.tile([P, H], BF16, name=f"by_slot{e}", align_bytes=64) for e in range(2)]
+        hidden = [keep.tile([P, 4 * G * C], BF16, name=f"h{e}", align_bytes=64) for e in range(E - 1)]
+        last_hidden = [keep.tile([P, 4 * C], BF16, name=f"h3_{g}", align_bytes=64) for g in range(G)]
+
+        def first_by_slot(e, c, width, bank):
+            sums = banks.tile([P, width], F32, name=f"a{e}_{c}", tag=f"bank{bank}")
+            nc.tensor.matmul_mx(
+                out=sums[:],
+                lhsT=slots[e][0].bitcast(FP8X4),
+                lhsT_scale=slots[e][1],
+                rhs=raw[e][:, 2 * c : 2 * (c + width)].bitcast(FP4X4),
+                rhs_scale=plain[:, e * H + c : e * H + c + width],
+                start=True,
+                stop=True,
+            )
+            g, p0 = c // 512, c % 512 // 4
+            nc.scalar.activation(
+                by_slot[e][:, g * 512 : (g + 1) * 512].rearrange("s (u p d) -> s u p d", u=2, d=2)[:, :, p0 : p0 + width // 4, :],
+                sums[:].rearrange("s (p u d) -> s u p d", u=2, d=2),
+                ACT.Silu,
+            )
+
+        def turn(e, bank):
+            turned = banks.tile([P, 2 * G, C], F32, name=f"turned{e}", tag=f"bank{bank}")
+            for q in range(2 * G):
+                nc.tensor.transpose(turned[:, q, :], by_slot[e][:].bitcast(F32)[:, q * P : (q + 1) * P], identity[:])
+            return turned
+
+        def copy_turned(e, turned):
+            nc.vector.tensor_copy(
+                hidden[e][:].bitcast(F32).rearrange("p (g s u) -> p g s u", g=G, u=2),
+                turned[:].rearrange("p (g u) s -> p g s u", u=2),
+            )
+
+        def permute_words(e):
+            for g in range(G):
+                half = slice(g * H, (g + 1) * H)
+                nc.vector.tensor_copy(
+                    w1[e][:, half].bitcast(U16).rearrange("p (t m) -> p t m", t=4),
+                    raw[e][:, half].bitcast(U16).rearrange("p (m t) -> p t m", t=4),
+                )
+
+        def first_by_column(e, g, bank):
+            sums = banks.tile([P, 4, C], F32, name=f"a{e}_{g}", tag=f"bank{bank}")
+            for t in range(4):
+                c = g * 512 + t * P
+                nc.tensor.matmul_mx(
+                    out=sums[:, t, :],
+                    lhsT=w1[e][:, 2 * c : 2 * c + 2 * P].bitcast(FP4X4),
+                    lhsT_scale=w1_plane[e][:, c : c + P],
+                    rhs=slots[e][0].bitcast(FP8X4),
+                    rhs_scale=slots[e][1],
+                    start=True,
+                    stop=True,
+                )
+            dst = last_hidden[g][:] if e == E - 1 else hidden[e][:, g * 4 * C : (g + 1) * 4 * C]
+            nc.scalar.activation(dst.rearrange("p (n t) -> p n t", t=4), sums[:].rearrange("p t n -> p n t"), ACT.Silu)
+
+        def quantise_hidden(name, h, words):
+            codes = keep.tile([P, words], U32, name=f"{name}_codes", align_bytes=64)
+            scales = keep.tile([P, words], U8, name=f"{name}_bytes", align_bytes=64)
+            nc.vector.quantize_mx(codes[:].bitcast(FP8X4), scales[:], h[:])
+            return codes, scales
 
         def second_pass(y, e, g, i, codes, scales):
             a = e * G + g
@@ -228,26 +221,40 @@ def tile_moe_eps_mlp_silu_kernel(tc, xT, w1_words, w1_scales, w2_words, w2_scale
                 stop=(g == G - 1),
             )
 
-        y0 = yp.tile([P, 2, C], F32, name="y0", tag="y0")
-        y12 = yp.tile([P, 2, 2, C], F32, name="y12", tag="y12")
-        ys = [y0[:], y12[:, 0], y12[:, 1]]
-        for e in range(E - 1):
-            h_codes = keep.tile([P, G * C], U32, name=f"h_codes{e}", align_bytes=64)
-            h_bytes = keep.tile([P, G * C], U8, name=f"h_bytes{e}", align_bytes=64)
-            nc.vector.quantize_mx(h_codes[:].bitcast(FP8X4), h_bytes[:], hidden[e][0][:])
+        def second(e, y):
+            codes, scales = quantise_hidden(f"h{e}", hidden[e], G * C)
             for i in range(2):
                 for g in range(G):
-                    second_pass(ys[e][:, i, :], e, g, i, h_codes[:, g * C : (g + 1) * C], h_bytes[:, g * C : (g + 1) * C])
+                    second_pass(y[:, i, :], e, g, i, codes[:, g * C : (g + 1) * C], scales[:, g * C : (g + 1) * C])
+
+        first_by_slot(0, 0, 256, 6)
+        first_by_slot(0, 256, 256, 0)
+        first_by_slot(0, 512, 512, 1)
+        first_by_slot(1, 0, 512, 2)
+        first_by_slot(1, 512, 512, 3)
+        permute_words(2)
+        first_by_column(2, 0, 0)
+        first_by_column(2, 1, 1)
+        copy_turned(0, turn(0, 4))
+        turned = turn(1, 5)
+        permute_words(3)
+        first_by_column(3, 0, 2)
+        first_by_column(3, 1, 3)
+        y02 = banks.tile([P, 2, 2, C], F32, name="y02", tag="bank4")
+        second(0, y02[:, 0])
+        copy_turned(1, turned)
+        second(2, y02[:, 1])
+        y1 = banks.tile([P, 2, C], F32, name="y1", tag="bank5")
+        second(1, y1[:])
         e = E - 1
-        last = [yp.tile([P, C], F32, name=f"last{i}", tag=f"last{i}") for i in range(2)]
+        last = [banks.tile([P, C], F32, name=f"last{i}", tag=f"bank{6 + i}") for i in range(2)]
         for g in range(G):
-            h_codes = keep.tile([P, C], U32, name=f"h_codes{e}_{g}", align_bytes=64)
-            h_bytes = keep.tile([P, C], U8, name=f"h_bytes{e}_{g}", align_bytes=64)
-            nc.vector.quantize_mx(h_codes[:].bitcast(FP8X4), h_bytes[:], hidden[e][g][:])
+            codes, scales = quantise_hidden(f"h{e}_{g}", last_hidden[g], C)
             for i in range(2):
-                second_pass(last[i][:], e, g, i, h_codes[:], h_bytes[:])
-        nc.vector.tensor_copy(ranked[:, 0], y0[:].rearrange("p i (m u) -> p i m u", m=R))
-        nc.scalar.copy(ranked[:, 1:3], y12[:].rearrange("p e i (m u) -> p e i m u", m=R))
+                second_pass(last[i][:], e, g, i, codes[:], scales[:])
+        ranked = results[:].rearrange("p i (m e u) -> p e i m u", m=R, e=E)
+        nc.scalar.copy(ranked[:, 0:3:2], y02[:].rearrange("p e i (m u) -> p e i m u", m=R))
+        nc.vector.tensor_copy(ranked[:, 1], y1[:].rearrange("p i (m u) -> p i m u", m=R))
         nc.vector.tensor_copy(ranked[:, e, 0], last[0][:].rearrange("p (m u) -> p m u", m=R))
         nc.scalar.copy(ranked[:, e, 1], last[1][:].rearrange("p (m u) -> p m u", m=R))
         nc.sync.dma_start(out[0:P, :], results[:, 0, :])

@@ -20,7 +20,7 @@ FP8X4 = mybir.dt.float8_e4m3fn_x4
 FP4X4 = mybir.dt.float4_e2m1fn_x4
 ACT = mybir.ActivationFunctionType
 
-CHUNKS = [(0, 128), (128, 128), (256, 128), (384, 128), (512, 128)]
+CHUNKS = [(0, 256), (256, 256), (512, 128)]
 
 
 def tile_moe_eps_mlp_silu_kernel(tc, xT, w1_words, w1_scales, w2_words, w2_scales, offs, out):
@@ -70,12 +70,10 @@ def tile_moe_eps_mlp_silu_kernel(tc, xT, w1_words, w1_scales, w2_words, w2_scale
             nc.sync.dma_start(raw[e][:].bitcast(I32), w1_words[e, 0].bitcast(I32))
 
         load_x(0)
-        load_x(1)
         for r in range(4):
             nc.sync.dma_start(packed[r:P:16, :].bitcast(I32), w1_scales[2:4, 0, r:16:4, :].rearrange("e q n -> q e n").bitcast(I32))
+        load_x(1)
         load_x(2)
-        load_x(3)
-        load_x(4)
         load_words(0)
         nc.sync.dma_start(offsets[:], offs)
         for q in range(4):
@@ -110,22 +108,17 @@ def tile_moe_eps_mlp_silu_kernel(tc, xT, w1_words, w1_scales, w2_words, w2_scale
         def quantise(c0, w):
             nc.vector.quantize_mx(x_codes[:, c0 : c0 + w].bitcast(FP8X4), x_bytes[:, c0 : c0 + w], grouped[:, 4 * c0 : 4 * (c0 + w)])
 
-        cast(0, 0, 128, True)
-        quantise(0, 128)
-        cast(1, 0, 32, False)
-        cast(1, 32, 96, True)
-        quantise(128, 128)
-        cast(2, 0, 128, True)
-        cast(3, 0, 32, False)
-        cast(3, 32, 96, True)
-        quantise(256, 128)
-        cast(4, 0, 80, False)
-        cast(4, 80, 48, True)
-        quantise(384, 128)
+        cast(0, 0, 128, False)
+        cast(0, 128, 128, True)
+        quantise(0, 256)
+        cast(1, 0, 80, False)
+        cast(1, 80, 176, True)
+        cast(2, 0, 128, False)
+        quantise(256, 256)
         quantise(512, 128)
 
         unused = banks.tile([P, 512], F32, name="unused", tag="bank7")
-        for width in (512, 512):
+        for width in (512, 256, 128):
             nc.tensor.matmul_mx(
                 out=unused[:, 0:width],
                 lhsT=zero_codes[:].bitcast(FP8X4),
@@ -225,9 +218,10 @@ def tile_moe_eps_mlp_silu_kernel(tc, xT, w1_words, w1_scales, w2_words, w2_scale
             codes, scales = quantise_hidden(f"h{e}", hidden[e], G * C)
             for i in range(2):
                 for g in range(G):
-                    second_pass(y[:, i, :], e, g, i, codes[:, g * C : (g + 1) * C], scales[:, g * C : (g + 1) * C])
+                    second_pass(y[i], e, g, i, codes[:, g * C : (g + 1) * C], scales[:, g * C : (g + 1) * C])
 
-        first_by_slot(0, 0, 256, 6)
+        first_by_slot(0, 0, 128, 6)
+        first_by_slot(0, 128, 128, 5)
         first_by_slot(0, 256, 256, 0)
         first_by_slot(0, 512, 512, 1)
         first_by_slot(1, 0, 512, 2)
@@ -241,11 +235,11 @@ def tile_moe_eps_mlp_silu_kernel(tc, xT, w1_words, w1_scales, w2_words, w2_scale
         first_by_column(3, 0, 2)
         first_by_column(3, 1, 3)
         y02 = banks.tile([P, 2, 2, C], F32, name="y02", tag="bank4")
-        second(0, y02[:, 0])
+        second(0, [y02[:, 0, i, :] for i in range(2)])
         copy_turned(1, turned)
-        second(2, y02[:, 1])
-        y1 = banks.tile([P, 2, C], F32, name="y1", tag="bank5")
-        second(1, y1[:])
+        second(2, [y02[:, 1, i, :] for i in range(2)])
+        y1 = [banks.tile([P, C], F32, name=f"y1_{i}", tag=f"bank{(5, 0)[i]}") for i in range(2)]
+        second(1, [y[:] for y in y1])
         e = E - 1
         last = [banks.tile([P, C], F32, name=f"last{i}", tag=f"bank{6 + i}") for i in range(2)]
         for g in range(G):
@@ -254,7 +248,8 @@ def tile_moe_eps_mlp_silu_kernel(tc, xT, w1_words, w1_scales, w2_words, w2_scale
                 second_pass(last[i][:], e, g, i, codes[:], scales[:])
         ranked = results[:].rearrange("p i (m e u) -> p e i m u", m=R, e=E)
         nc.scalar.copy(ranked[:, 0:3:2], y02[:].rearrange("p e i (m u) -> p e i m u", m=R))
-        nc.vector.tensor_copy(ranked[:, 1], y1[:].rearrange("p i (m u) -> p i m u", m=R))
+        nc.vector.tensor_copy(ranked[:, 1, 0], y1[0][:].rearrange("p (m u) -> p m u", m=R))
+        nc.scalar.copy(ranked[:, 1, 1], y1[1][:].rearrange("p (m u) -> p m u", m=R))
         nc.vector.tensor_copy(ranked[:, e, 0], last[0][:].rearrange("p (m u) -> p m u", m=R))
         nc.scalar.copy(ranked[:, e, 1], last[1][:].rearrange("p (m u) -> p m u", m=R))
         nc.sync.dma_start(out[0:P, :], results[:, 0, :])

@@ -27,6 +27,7 @@ def tile_moe_eps_mlp_silu_kernel(tc, xT, w1_words, w1_scales, w2_words, w2_scale
     nc = tc.nc
     with ExitStack() as ctx:
         keep = ctx.enter_context(tc.tile_pool(name="keep", bufs=1))
+        shared = ctx.enter_context(tc.tile_pool(name="shared", bufs=1))
         banks = ctx.enter_context(tc.psum_pool(name="banks", bufs=1))
 
         offsets = keep.tile([P, E * C // 16], U16, name="offsets")
@@ -37,7 +38,8 @@ def tile_moe_eps_mlp_silu_kernel(tc, xT, w1_words, w1_scales, w2_words, w2_scale
         x_bytes = keep.tile([P, T], U8, name="x_bytes", align_bytes=64)
         x_codes = keep.tile([P, T], U32, name="x_codes", align_bytes=64)
         grouped = keep.tile([P, 4 * T], BF16, name="grouped", align_bytes=64)
-        raw = [keep.tile([P, 2 * H], U8, name=f"raw{e}", align_bytes=64) for e in range(E)]
+        raw = {e: keep.tile([P, 2 * H], U8, name=f"raw{e}", align_bytes=64) for e in (0, 1, 3)}
+        raw.setdefault(2, shared.tile([P, 2 * H], U8, name="raw2", align_bytes=64, offset=0))
         w1 = {e: keep.tile([P, 2 * H], U8, name=f"w1_{e}", align_bytes=64) for e in (2, 3)}
         w1_plane = {2: permuted, 3: moved}
         identity = keep.tile([P, P], F32, name="identity")
@@ -118,7 +120,7 @@ def tile_moe_eps_mlp_silu_kernel(tc, xT, w1_words, w1_scales, w2_words, w2_scale
         quantise(512, 128)
 
         unused = banks.tile([P, 512], F32, name="unused", tag="bank7")
-        for width in (512, 256, 128):
+        for width in (512, 512, 128):
             nc.tensor.matmul_mx(
                 out=unused[:, 0:width],
                 lhsT=zero_codes[:].bitcast(FP8X4),
@@ -129,15 +131,16 @@ def tile_moe_eps_mlp_silu_kernel(tc, xT, w1_words, w1_scales, w2_words, w2_scale
                 stop=True,
             )
 
-        def gather(name, e0, count):
-            lst = offsets[:, 8 * e0 : 8 * (e0 + count)]
-            codes = keep.tile([P, count * C], U32, name=f"{name}_codes", align_bytes=64)
-            scales = keep.tile([P, count * C], U8, name=f"{name}_bytes", align_bytes=64)
+        def gather(e, codes, scales):
+            lst = offsets[:, 8 * e : 8 * (e + 1)]
             nc.vector.tensor_copy(codes[:], x_codes[:].indirect(lst))
             nc.vector.tensor_copy(scales[:], x_bytes[:].indirect(lst))
-            return [(codes[:, i * C : (i + 1) * C], scales[:, i * C : (i + 1) * C]) for i in range(count)]
+            return codes[:], scales[:]
 
-        slots = gather("s0", 0, 1) + gather("s1", 1, 1) + gather("s23", 2, 2)
+        slots = [
+            gather(e, keep.tile([P, C], U32, name=f"s_codes{e}", align_bytes=64), keep.tile([P, C], U8, name=f"s_bytes{e}", align_bytes=64))
+            for e in range(E - 1)
+        ]
         by_slot = [keep.tile([P, H], BF16, name=f"by_slot{e}", align_bytes=64) for e in range(2)]
         hidden = [keep.tile([P, 4 * G * C], BF16, name=f"h{e}", align_bytes=64) for e in range(E - 1)]
         last_hidden = [keep.tile([P, 4 * C], BF16, name=f"h3_{g}", align_bytes=64) for g in range(G)]
@@ -172,13 +175,12 @@ def tile_moe_eps_mlp_silu_kernel(tc, xT, w1_words, w1_scales, w2_words, w2_scale
                 turned[:].rearrange("p (g u) s -> p g s u", u=2),
             )
 
-        def permute_words(e):
-            for g in range(G):
-                half = slice(g * H, (g + 1) * H)
-                nc.vector.tensor_copy(
-                    w1[e][:, half].bitcast(U16).rearrange("p (t m) -> p t m", t=4),
-                    raw[e][:, half].bitcast(U16).rearrange("p (m t) -> p t m", t=4),
-                )
+        def permute_words(e, g):
+            half = slice(g * H, (g + 1) * H)
+            nc.vector.tensor_copy(
+                w1[e][:, half].bitcast(U16).rearrange("p (t m) -> p t m", t=4),
+                raw[e][:, half].bitcast(U16).rearrange("p (m t) -> p t m", t=4),
+            )
 
         def first_by_column(e, g, bank):
             sums = banks.tile([P, 4, C], F32, name=f"a{e}_{g}", tag=f"bank{bank}")
@@ -226,12 +228,21 @@ def tile_moe_eps_mlp_silu_kernel(tc, xT, w1_words, w1_scales, w2_words, w2_scale
         first_by_slot(0, 512, 512, 1)
         first_by_slot(1, 0, 512, 2)
         first_by_slot(1, 512, 512, 3)
-        permute_words(2)
+        permute_words(2, 0)
+        permute_words(2, 1)
         first_by_column(2, 0, 0)
         first_by_column(2, 1, 1)
+        permute_words(3, 0)
+        slots.append(
+            gather(
+                3,
+                shared.tile([P, C], U32, name="s_codes3", align_bytes=64, offset=0),
+                shared.tile([P, C], U8, name="s_bytes3", align_bytes=64, offset=4 * C),
+            )
+        )
         copy_turned(0, turn(0, 4))
         turned = turn(1, 5)
-        permute_words(3)
+        permute_words(3, 1)
         first_by_column(3, 0, 2)
         first_by_column(3, 1, 3)
         y02 = banks.tile([P, 2, 2, C], F32, name="y02", tag="bank4")

@@ -9,6 +9,7 @@ K, T, E, C, H, N = 512, 640, 4, 128, 1024, 256
 R = 4
 P = 128
 G = H // 512
+HALF = C // 2
 
 F32 = mybir.dt.float32
 BF16 = mybir.dt.bfloat16
@@ -47,7 +48,9 @@ def tile_moe_eps_mlp_silu_kernel(tc, xT, w1_words, w1_scales, w2_words, w2_scale
         w2_plane = keep.tile([P, E * G * N], U8, name="w2_plane", align_bytes=64)
         w2 = keep.tile([P, E * G, 2 * N], U8, name="w2", align_bytes=64)
         x_raw = [keep.tile([P, 4, w], F32, name=f"x_raw{i}", align_bytes=64) for i, (c0, w) in enumerate(CHUNKS)]
-        results = keep.tile([P, 2, E * C], F32, name="results")
+        results = [keep.tile([P, 2, E * HALF], F32, name=f"results{h}") for h in range(2)]
+        last_codes = [keep.tile([P, (3 + h) * HALF], U32, name=f"last_codes{h}", align_bytes=64) for h in range(2)]
+        last_bytes = [keep.tile([P, (3 + h) * HALF], U8, name=f"last_bytes{h}", align_bytes=64) for h in range(2)]
         warm = keep.tile([P, 1], F32, name="warm")
         warm_out = keep.tile([P, 1], F32, name="warm_out")
         zeros = keep.tile([P, 4 * P], BF16, name="zeros", align_bytes=64)
@@ -61,6 +64,9 @@ def tile_moe_eps_mlp_silu_kernel(tc, xT, w1_words, w1_scales, w2_words, w2_scale
         nc.vector.memset(plain[:].bitcast(I32), 0)
         nc.vector.memset(moved[:].bitcast(I32), 0)
         nc.vector.memset(w2_plane[:].bitcast(I32), 0)
+        for h in range(2):
+            nc.vector.memset(last_codes[h][:, (2 - h) * HALF :].bitcast(I32), 0)
+            nc.vector.memset(last_bytes[h][:, (2 - h) * HALF :].bitcast(I32), 0)
         nc.vector.memset(zeros[:], 0.0)
         nc.vector.quantize_mx(zero_codes[:].bitcast(FP8X4), zero_bytes[:], zeros[:])
 
@@ -78,10 +84,10 @@ def tile_moe_eps_mlp_silu_kernel(tc, xT, w1_words, w1_scales, w2_words, w2_scale
         load_x(2)
         load_words(0)
         nc.sync.dma_start(offsets[:], offs)
-        for q in range(4):
+        for r in range(4):
             nc.sync.dma_start(
-                plain[32 * q : 32 * q + 4].rearrange("p (e n) -> p e n", e=2).bitcast(I32),
-                w1_scales[0:2, 0, 4 * q : 4 * q + 4, :].rearrange("e r n -> r e n").bitcast(I32),
+                plain[r:P:32].rearrange("p (e n) -> p e n", e=2).bitcast(I32),
+                w1_scales[0:2, 0, r:16:4, :].rearrange("e q n -> q e n").bitcast(I32),
             )
         load_words(1)
         load_words(2)
@@ -91,10 +97,10 @@ def tile_moe_eps_mlp_silu_kernel(tc, xT, w1_words, w1_scales, w2_words, w2_scale
             packed[:].rearrange("p (g m t) -> p g t m", g=G, t=4),
         )
         nc.sync.dma_start(moved[0:112, :].bitcast(I32), permuted[16:P, :].bitcast(I32))
-        for q in range(4):
+        for r in range(4):
             nc.sync.dma_start(
-                w2_plane[32 * q : 32 * q + 4].rearrange("p (a n) -> p a n", n=N).bitcast(I32),
-                w2_scales[:, :, 4 * q : 4 * q + 4, :].rearrange("e s q n -> q (e s) n").bitcast(I32),
+                w2_plane[r:P:32].rearrange("p (a n) -> p a n", n=N).bitcast(I32),
+                w2_scales[:, :, r:16:4, :].rearrange("e s q n -> q (e s) n").bitcast(I32),
             )
         nc.sync.dma_start(w2[:].bitcast(I32), w2_words.rearrange("e s p b -> p (e s) b").bitcast(I32))
 
@@ -120,7 +126,7 @@ def tile_moe_eps_mlp_silu_kernel(tc, xT, w1_words, w1_scales, w2_words, w2_scale
         quantise(512, 128)
 
         unused = banks.tile([P, 512], F32, name="unused", tag="bank7")
-        for width in (512, 512, 128):
+        for width in (512, 512):
             nc.tensor.matmul_mx(
                 out=unused[:, 0:width],
                 lhsT=zero_codes[:].bitcast(FP8X4),
@@ -143,7 +149,7 @@ def tile_moe_eps_mlp_silu_kernel(tc, xT, w1_words, w1_scales, w2_words, w2_scale
         ]
         by_slot = [keep.tile([P, H], BF16, name=f"by_slot{e}", align_bytes=64) for e in range(2)]
         hidden = [keep.tile([P, 4 * G * C], BF16, name=f"h{e}", align_bytes=64) for e in range(E - 1)]
-        last_hidden = [keep.tile([P, 4 * C], BF16, name=f"h3_{g}", align_bytes=64) for g in range(G)]
+        last_hidden = [keep.tile([P, G, 4 * HALF], BF16, name=f"h3_{h}", align_bytes=64) for h in range(2)]
 
         def first_by_slot(e, c, width, bank):
             sums = banks.tile([P, width], F32, name=f"a{e}_{c}", tag=f"bank{bank}")
@@ -195,8 +201,10 @@ def tile_moe_eps_mlp_silu_kernel(tc, xT, w1_words, w1_scales, w2_words, w2_scale
                     start=True,
                     stop=True,
                 )
-            dst = last_hidden[g][:] if e == E - 1 else hidden[e][:, g * 4 * C : (g + 1) * 4 * C]
-            nc.scalar.activation(dst.rearrange("p (n t) -> p n t", t=4), sums[:].rearrange("p t n -> p n t"), ACT.Silu)
+            return sums
+
+        def silu_by_column(dst, sums):
+            nc.scalar.activation(dst.rearrange("p (n t) -> p n t", t=4), sums.rearrange("p t n -> p n t"), ACT.Silu)
 
         def quantise_hidden(name, h, words):
             codes = keep.tile([P, words], U32, name=f"{name}_codes", align_bytes=64)
@@ -230,8 +238,8 @@ def tile_moe_eps_mlp_silu_kernel(tc, xT, w1_words, w1_scales, w2_words, w2_scale
         first_by_slot(1, 512, 512, 3)
         permute_words(2, 0)
         permute_words(2, 1)
-        first_by_column(2, 0, 0)
-        first_by_column(2, 1, 1)
+        for g in range(G):
+            silu_by_column(hidden[2][:, g * 4 * C : (g + 1) * 4 * C], first_by_column(2, g, g)[:])
         permute_words(3, 0)
         slots.append(
             gather(
@@ -243,25 +251,51 @@ def tile_moe_eps_mlp_silu_kernel(tc, xT, w1_words, w1_scales, w2_words, w2_scale
         copy_turned(0, turn(0, 4))
         turned = turn(1, 5)
         permute_words(3, 1)
-        first_by_column(3, 0, 2)
-        first_by_column(3, 1, 3)
+        last_sums = [first_by_column(3, g, 2 + g) for g in range(G)]
+        for h in range(2):
+            for g in range(G):
+                silu_by_column(last_hidden[h][:, g, :], last_sums[g][:, :, h * HALF : (h + 1) * HALF])
         y02 = banks.tile([P, 2, 2, C], F32, name="y02", tag="bank4")
         second(0, [y02[:, 0, i, :] for i in range(2)])
         copy_turned(1, turned)
         second(2, [y02[:, 1, i, :] for i in range(2)])
-        y1 = [banks.tile([P, C], F32, name=f"y1_{i}", tag=f"bank{(5, 0)[i]}") for i in range(2)]
-        second(1, [y[:] for y in y1])
+        y1 = banks.tile([P, 2, C], F32, name="y1", tag="bank5")
+        second(1, [y1[:, i, :] for i in range(2)])
         e = E - 1
+
+        def quantise_last(h, g0, passes):
+            cols = slice(g0 * C, g0 * C + passes * HALF)
+            nc.vector.quantize_mx(
+                last_codes[h][:, cols].bitcast(FP8X4),
+                last_bytes[h][:, cols],
+                last_hidden[h][:, g0 : g0 + passes, :].rearrange("p g w -> p (g w)"),
+            )
+
+        def last_pass(y, h, g, i):
+            c0 = g * HALF * (1 + h)
+            cols = slice(c0, c0 + C)
+            second_pass(y, e, g, i, last_codes[h][:, cols], last_bytes[h][:, cols])
+
+        ranked = [res[:].rearrange("p i (m e u) -> p e i m u", m=2, e=E) for res in results]
+        by_rank = out.rearrange("(i p) (h c) -> h p i c", i=2, h=2)
+
+        y3 = banks.tile([P, 2, C], F32, name="y3", tag="bank1")
+        quantise_last(0, 0, G)
+        for i in range(2):
+            for g in range(G):
+                last_pass(y3[:, i, :], 0, g, i)
         last = [banks.tile([P, C], F32, name=f"last{i}", tag=f"bank{6 + i}") for i in range(2)]
         for g in range(G):
-            codes, scales = quantise_hidden(f"h{e}_{g}", last_hidden[g], C)
+            quantise_last(1, g, 1)
             for i in range(2):
-                second_pass(last[i][:], e, g, i, codes[:], scales[:])
-        ranked = results[:].rearrange("p i (m e u) -> p e i m u", m=R, e=E)
-        nc.scalar.copy(ranked[:, 0:3:2], y02[:].rearrange("p e i (m u) -> p e i m u", m=R))
-        nc.vector.tensor_copy(ranked[:, 1, 0], y1[0][:].rearrange("p (m u) -> p m u", m=R))
-        nc.scalar.copy(ranked[:, 1, 1], y1[1][:].rearrange("p (m u) -> p m u", m=R))
-        nc.vector.tensor_copy(ranked[:, e, 0], last[0][:].rearrange("p (m u) -> p m u", m=R))
-        nc.scalar.copy(ranked[:, e, 1], last[1][:].rearrange("p (m u) -> p m u", m=R))
-        nc.sync.dma_start(out[0:P, :], results[:, 0, :])
-        nc.scalar.dma_start(out[P : 2 * P, :], results[:, 1, :])
+                last_pass(last[i][:], 1, g, i)
+        nc.scalar.copy(ranked[0][:, 0:3:2], y02[:, :, :, 0:HALF].rearrange("p e i (m u) -> p e i m u", m=2))
+        nc.scalar.copy(ranked[0][:, 1], y1[:, :, 0:HALF].rearrange("p i (m u) -> p i m u", m=2))
+        nc.scalar.copy(ranked[0][:, e], y3[:, :, 0:HALF].rearrange("p i (m u) -> p i m u", m=2))
+        nc.sync.dma_start(by_rank[0], results[0][:])
+        nc.vector.tensor_copy(ranked[1][:, 0:3:2], y02[:, :, :, HALF:C].rearrange("p e i (m u) -> p e i m u", m=2))
+        nc.vector.tensor_copy(ranked[1][:, 1], y1[:, :, HALF:C].rearrange("p i (m u) -> p i m u", m=2))
+        nc.vector.tensor_copy(ranked[1][:, e, 0], last[0][:, 0:HALF].rearrange("p (m u) -> p m u", m=2))
+        nc.scalar.copy(ranked[1][:, e, 1], last[1][:, 0:HALF].rearrange("p (m u) -> p m u", m=2))
+        nc.sync.dma_start(by_rank[1, :, 0], results[1][:, 0, :])
+        nc.scalar.dma_start(by_rank[1, :, 1], results[1][:, 1, :])

@@ -9,7 +9,6 @@ K, T, E, C, H, N = 512, 640, 4, 128, 1024, 256
 R = 4
 P = 128
 G = H // 512
-HALF = C // 2
 
 F32 = mybir.dt.float32
 BF16 = mybir.dt.bfloat16
@@ -39,8 +38,11 @@ def tile_moe_eps_mlp_silu_kernel(tc, xT, w1_words, w1_scales, w2_words, w2_scale
         x_bytes = keep.tile([P, T], U8, name="x_bytes", align_bytes=64)
         x_codes = keep.tile([P, T], U32, name="x_codes", align_bytes=64)
         grouped = keep.tile([P, 4 * T], BF16, name="grouped", align_bytes=64)
-        raw = {e: keep.tile([P, 2 * H], U8, name=f"raw{e}", align_bytes=64) for e in (0, 1, 3)}
-        raw.setdefault(2, shared.tile([P, 2 * H], U8, name="raw2", align_bytes=64, offset=0))
+        raw01 = keep.tile([P, 2, 2 * H], U8, name="raw01", align_bytes=64)
+        raw = {
+            2: shared.tile([P, 2 * H], U8, name="raw2", align_bytes=64, offset=0),
+            3: keep.tile([P, 2 * H], U8, name="raw3", align_bytes=64),
+        }
         w1 = {e: keep.tile([P, 2 * H], U8, name=f"w1_{e}", align_bytes=64) for e in (2, 3)}
         w1_plane = {2: permuted, 3: moved}
         identity = keep.tile([P, P], F32, name="identity")
@@ -48,9 +50,7 @@ def tile_moe_eps_mlp_silu_kernel(tc, xT, w1_words, w1_scales, w2_words, w2_scale
         w2_plane = keep.tile([P, E * G * N], U8, name="w2_plane", align_bytes=64)
         w2 = keep.tile([P, E * G, 2 * N], U8, name="w2", align_bytes=64)
         x_raw = [keep.tile([P, 4, w], F32, name=f"x_raw{i}", align_bytes=64) for i, (c0, w) in enumerate(CHUNKS)]
-        results = [keep.tile([P, 2, E * HALF], F32, name=f"results{h}") for h in range(2)]
-        last_codes = [keep.tile([P, (3 + h) * HALF], U32, name=f"last_codes{h}", align_bytes=64) for h in range(2)]
-        last_bytes = [keep.tile([P, (3 + h) * HALF], U8, name=f"last_bytes{h}", align_bytes=64) for h in range(2)]
+        results = keep.tile([P, 2, E * C], F32, name="results")
         warm = keep.tile([P, 1], F32, name="warm")
         warm_out = keep.tile([P, 1], F32, name="warm_out")
         zeros = keep.tile([P, 4 * P], BF16, name="zeros", align_bytes=64)
@@ -64,9 +64,6 @@ def tile_moe_eps_mlp_silu_kernel(tc, xT, w1_words, w1_scales, w2_words, w2_scale
         nc.vector.memset(plain[:].bitcast(I32), 0)
         nc.vector.memset(moved[:].bitcast(I32), 0)
         nc.vector.memset(w2_plane[:].bitcast(I32), 0)
-        for h in range(2):
-            nc.vector.memset(last_codes[h][:, (2 - h) * HALF :].bitcast(I32), 0)
-            nc.vector.memset(last_bytes[h][:, (2 - h) * HALF :].bitcast(I32), 0)
         nc.vector.memset(zeros[:], 0.0)
         nc.vector.quantize_mx(zero_codes[:].bitcast(FP8X4), zero_bytes[:], zeros[:])
 
@@ -82,14 +79,13 @@ def tile_moe_eps_mlp_silu_kernel(tc, xT, w1_words, w1_scales, w2_words, w2_scale
             nc.sync.dma_start(packed[r:P:16, :].bitcast(I32), w1_scales[2:4, 0, r:16:4, :].rearrange("e q n -> q e n").bitcast(I32))
         load_x(1)
         load_x(2)
-        load_words(0)
         nc.sync.dma_start(offsets[:], offs)
         for r in range(4):
             nc.sync.dma_start(
                 plain[r:P:32].rearrange("p (e n) -> p e n", e=2).bitcast(I32),
                 w1_scales[0:2, 0, r:16:4, :].rearrange("e q n -> q e n").bitcast(I32),
             )
-        load_words(1)
+        nc.sync.dma_start(raw01[:].bitcast(I32), w1_words[0:2, 0].rearrange("e p b -> p e b").bitcast(I32))
         load_words(2)
         load_words(3)
         nc.vector.tensor_copy(
@@ -126,30 +122,30 @@ def tile_moe_eps_mlp_silu_kernel(tc, xT, w1_words, w1_scales, w2_words, w2_scale
         quantise(512, 128)
 
         unused = banks.tile([P, 512], F32, name="unused", tag="bank7")
-        for width in (512, 512):
+        for plane in (permuted, plain, plain):
             nc.tensor.matmul_mx(
-                out=unused[:, 0:width],
+                out=unused[:],
                 lhsT=zero_codes[:].bitcast(FP8X4),
                 lhsT_scale=zero_bytes[:],
-                rhs=raw[0][:, 0 : 2 * width].bitcast(FP4X4),
-                rhs_scale=packed[:, 0:width],
+                rhs=packed[:].bitcast(FP4X4),
+                rhs_scale=plane[:, 0:512],
                 start=True,
                 stop=True,
             )
 
-        def gather(e, codes, scales):
-            lst = offsets[:, 8 * e : 8 * (e + 1)]
-            nc.vector.tensor_copy(codes[:], x_codes[:].indirect(lst))
-            nc.vector.tensor_copy(scales[:], x_bytes[:].indirect(lst))
-            return codes[:], scales[:]
+        def gather(j0, j1, tokens, codes, scales):
+            lst = offsets[:, j0 // 16 : j1 // 16]
+            nc.vector.tensor_copy(codes, x_codes[:, 0:tokens].indirect(lst))
+            nc.vector.tensor_copy(scales, x_bytes[:, 0:tokens].indirect(lst))
 
-        slots = [
-            gather(e, keep.tile([P, C], U32, name=f"s_codes{e}", align_bytes=64), keep.tile([P, C], U8, name=f"s_bytes{e}", align_bytes=64))
-            for e in range(E - 1)
-        ]
+        s_codes = keep.tile([P, 3 * C], U32, name="s_codes", align_bytes=64)
+        s_bytes = keep.tile([P, 3 * C], U8, name="s_bytes", align_bytes=64)
+        for j0, j1, tokens in ((0, C, T), (C, 3 * C, T)):
+            gather(j0, j1, tokens, s_codes[:, j0:j1], s_bytes[:, j0:j1])
+        slots = [(s_codes[:, e * C : (e + 1) * C], s_bytes[:, e * C : (e + 1) * C]) for e in range(E - 1)]
         by_slot = [keep.tile([P, H], BF16, name=f"by_slot{e}", align_bytes=64) for e in range(2)]
         hidden = [keep.tile([P, 4 * G * C], BF16, name=f"h{e}", align_bytes=64) for e in range(E - 1)]
-        last_hidden = [keep.tile([P, G, 4 * HALF], BF16, name=f"h3_{h}", align_bytes=64) for h in range(2)]
+        last_hidden = [keep.tile([P, 4 * C], BF16, name=f"h3_{g}", align_bytes=64) for g in range(G)]
 
         def first_by_slot(e, c, width, bank):
             sums = banks.tile([P, width], F32, name=f"a{e}_{c}", tag=f"bank{bank}")
@@ -157,7 +153,7 @@ def tile_moe_eps_mlp_silu_kernel(tc, xT, w1_words, w1_scales, w2_words, w2_scale
                 out=sums[:],
                 lhsT=slots[e][0].bitcast(FP8X4),
                 lhsT_scale=slots[e][1],
-                rhs=raw[e][:, 2 * c : 2 * (c + width)].bitcast(FP4X4),
+                rhs=raw01[:, e, 2 * c : 2 * (c + width)].bitcast(FP4X4),
                 rhs_scale=plain[:, e * H + c : e * H + c + width],
                 start=True,
                 stop=True,
@@ -181,11 +177,11 @@ def tile_moe_eps_mlp_silu_kernel(tc, xT, w1_words, w1_scales, w2_words, w2_scale
                 turned[:].rearrange("p (g u) s -> p g s u", u=2),
             )
 
-        def permute_words(e, g):
-            half = slice(g * H, (g + 1) * H)
+        def permute_words(e, g0, passes):
+            cols = slice(g0 * H, (g0 + passes) * H)
             nc.vector.tensor_copy(
-                w1[e][:, half].bitcast(U16).rearrange("p (t m) -> p t m", t=4),
-                raw[e][:, half].bitcast(U16).rearrange("p (m t) -> p t m", t=4),
+                w1[e][:, cols].bitcast(U16).rearrange("p (g t m) -> p g t m", g=passes, t=4),
+                raw[e][:, cols].bitcast(U16).rearrange("p (g m t) -> p g t m", g=passes, t=4),
             )
 
         def first_by_column(e, g, bank):
@@ -236,66 +232,35 @@ def tile_moe_eps_mlp_silu_kernel(tc, xT, w1_words, w1_scales, w2_words, w2_scale
         first_by_slot(0, 512, 512, 1)
         first_by_slot(1, 0, 512, 2)
         first_by_slot(1, 512, 512, 3)
-        permute_words(2, 0)
-        permute_words(2, 1)
+        permute_words(2, 0, G)
         for g in range(G):
-            silu_by_column(hidden[2][:, g * 4 * C : (g + 1) * 4 * C], first_by_column(2, g, g)[:])
-        permute_words(3, 0)
-        slots.append(
-            gather(
-                3,
-                shared.tile([P, C], U32, name="s_codes3", align_bytes=64, offset=0),
-                shared.tile([P, C], U8, name="s_bytes3", align_bytes=64, offset=4 * C),
-            )
-        )
-        copy_turned(0, turn(0, 4))
-        turned = turn(1, 5)
-        permute_words(3, 1)
-        last_sums = [first_by_column(3, g, 2 + g) for g in range(G)]
-        for h in range(2):
-            for g in range(G):
-                silu_by_column(last_hidden[h][:, g, :], last_sums[g][:, :, h * HALF : (h + 1) * HALF])
+            silu_by_column(hidden[2][:, g * 4 * C : (g + 1) * 4 * C], first_by_column(2, g, 6 - g)[:])
+        s_codes3 = shared.tile([P, C], U32, name="s_codes3", align_bytes=64, offset=0)
+        s_bytes3 = shared.tile([P, C], U8, name="s_bytes3", align_bytes=64, offset=4 * C)
+        gather(3 * C, 4 * C, T, s_codes3[:], s_bytes3[:])
+        slots.append((s_codes3[:], s_bytes3[:]))
+        turned = [turn(0, 4), turn(1, 7)]
+        permute_words(3, 0, G)
+        e = E - 1
+        for g in range(G):
+            silu_by_column(last_hidden[g][:], first_by_column(e, g, 3 * g)[:])
+        copy_turned(0, turned[0])
+        copy_turned(1, turned[1])
         y02 = banks.tile([P, 2, 2, C], F32, name="y02", tag="bank4")
         second(0, [y02[:, 0, i, :] for i in range(2)])
-        copy_turned(1, turned)
         second(2, [y02[:, 1, i, :] for i in range(2)])
-        y1 = banks.tile([P, 2, C], F32, name="y1", tag="bank5")
-        second(1, [y1[:, i, :] for i in range(2)])
-        e = E - 1
-
-        def quantise_last(h, g0, passes):
-            cols = slice(g0 * C, g0 * C + passes * HALF)
-            nc.vector.quantize_mx(
-                last_codes[h][:, cols].bitcast(FP8X4),
-                last_bytes[h][:, cols],
-                last_hidden[h][:, g0 : g0 + passes, :].rearrange("p g w -> p (g w)"),
-            )
-
-        def last_pass(y, h, g, i):
-            c0 = g * HALF * (1 + h)
-            cols = slice(c0, c0 + C)
-            second_pass(y, e, g, i, last_codes[h][:, cols], last_bytes[h][:, cols])
-
-        ranked = [res[:].rearrange("p i (m e u) -> p e i m u", m=2, e=E) for res in results]
-        by_rank = out.rearrange("(i p) (h c) -> h p i c", i=2, h=2)
-
-        y3 = banks.tile([P, 2, C], F32, name="y3", tag="bank1")
-        quantise_last(0, 0, G)
-        for i in range(2):
-            for g in range(G):
-                last_pass(y3[:, i, :], 0, g, i)
-        last = [banks.tile([P, C], F32, name=f"last{i}", tag=f"bank{6 + i}") for i in range(2)]
+        y1 = [banks.tile([P, C], F32, name=f"y1_{i}", tag=f"bank{(7, 1)[i]}") for i in range(2)]
+        second(1, [y[:] for y in y1])
+        last = [banks.tile([P, C], F32, name=f"last{i}", tag=f"bank{5 + i}") for i in range(2)]
         for g in range(G):
-            quantise_last(1, g, 1)
+            codes, scales = quantise_hidden(f"h{e}_{g}", last_hidden[g], C)
             for i in range(2):
-                last_pass(last[i][:], 1, g, i)
-        nc.scalar.copy(ranked[0][:, 0:3:2], y02[:, :, :, 0:HALF].rearrange("p e i (m u) -> p e i m u", m=2))
-        nc.scalar.copy(ranked[0][:, 1], y1[:, :, 0:HALF].rearrange("p i (m u) -> p i m u", m=2))
-        nc.scalar.copy(ranked[0][:, e], y3[:, :, 0:HALF].rearrange("p i (m u) -> p i m u", m=2))
-        nc.sync.dma_start(by_rank[0], results[0][:])
-        nc.vector.tensor_copy(ranked[1][:, 0:3:2], y02[:, :, :, HALF:C].rearrange("p e i (m u) -> p e i m u", m=2))
-        nc.vector.tensor_copy(ranked[1][:, 1], y1[:, :, HALF:C].rearrange("p i (m u) -> p i m u", m=2))
-        nc.vector.tensor_copy(ranked[1][:, e, 0], last[0][:, 0:HALF].rearrange("p (m u) -> p m u", m=2))
-        nc.scalar.copy(ranked[1][:, e, 1], last[1][:, 0:HALF].rearrange("p (m u) -> p m u", m=2))
-        nc.sync.dma_start(by_rank[1, :, 0], results[1][:, 0, :])
-        nc.scalar.dma_start(by_rank[1, :, 1], results[1][:, 1, :])
+                second_pass(last[i][:], e, g, i, codes[:], scales[:])
+        ranked = results[:].rearrange("p i (m e u) -> p e i m u", m=R, e=E)
+        nc.scalar.copy(ranked[:, 0:3:2], y02[:].rearrange("p e i (m u) -> p e i m u", m=R))
+        nc.vector.tensor_copy(ranked[:, 1, 0], y1[0][:].rearrange("p (m u) -> p m u", m=R))
+        nc.scalar.copy(ranked[:, 1, 1], y1[1][:].rearrange("p (m u) -> p m u", m=R))
+        nc.vector.tensor_copy(ranked[:, e, 0], last[0][:].rearrange("p (m u) -> p m u", m=R))
+        nc.scalar.copy(ranked[:, e, 1], last[1][:].rearrange("p (m u) -> p m u", m=R))
+        nc.sync.dma_start(out[0:P, :], results[:, 0, :])
+        nc.scalar.dma_start(out[P : 2 * P, :], results[:, 1, :])

@@ -229,7 +229,8 @@ def tile_moe_eps_mlp_silu_kernel(tc, xT, w1_words, w1_scales, w2_words, w2_scale
         first_by_slot(0, 0, 128, 6)
         first_by_slot(0, 128, 128, 5)
         first_by_slot(0, 256, 256, 0)
-        first_by_slot(0, 512, 512, 1)
+        first_by_slot(0, 512, 256, 1)
+        first_by_slot(0, 768, 256, 4)
         first_by_slot(1, 0, 512, 2)
         first_by_slot(1, 512, 512, 3)
         permute_words(2, 0, G)

@@ -88,10 +88,12 @@ def tile_moe_eps_mlp_silu_kernel(tc, xT, w1_words, w1_scales, w2_words, w2_scale
         nc.sync.dma_start(raw01[:].bitcast(I32), w1_words[0:2, 0].rearrange("e p b -> p e b").bitcast(I32))
         load_words(2)
         load_words(3)
-        nc.vector.tensor_copy(
-            permuted[:].rearrange("p (g t m) -> p g t m", g=G, t=4),
-            packed[:].rearrange("p (g m t) -> p g t m", g=G, t=4),
-        )
+        for g in range(G):
+            cols = slice(g * 512, (g + 1) * 512)
+            nc.vector.tensor_copy(
+                permuted[:, cols].rearrange("p (t m) -> p t m", t=4),
+                packed[:, cols].rearrange("p (m t) -> p t m", t=4),
+            )
         nc.sync.dma_start(moved[0:112, :].bitcast(I32), permuted[16:P, :].bitcast(I32))
         for r in range(4):
             nc.sync.dma_start(
@@ -115,33 +117,35 @@ def tile_moe_eps_mlp_silu_kernel(tc, xT, w1_words, w1_scales, w2_words, w2_scale
         cast(0, 0, 128, False)
         cast(0, 128, 128, True)
         quantise(0, 256)
-        cast(1, 0, 80, False)
-        cast(1, 80, 176, True)
-        cast(2, 0, 128, False)
+        cast(1, 0, 96, False)
+        cast(1, 96, 160, True)
+        cast(2, 0, 80, False)
+        cast(2, 80, 48, True)
         quantise(256, 256)
         quantise(512, 128)
 
         unused = banks.tile([P, 512], F32, name="unused", tag="bank7")
-        for plane in (permuted, plain, plain):
+        for repeat in range(3):
             nc.tensor.matmul_mx(
                 out=unused[:],
                 lhsT=zero_codes[:].bitcast(FP8X4),
                 lhsT_scale=zero_bytes[:],
                 rhs=packed[:].bitcast(FP4X4),
-                rhs_scale=plane[:, 0:512],
+                rhs_scale=permuted[:, 0:512],
                 start=True,
                 stop=True,
             )
 
-        def gather(j0, j1, tokens, codes, scales):
-            lst = offsets[:, j0 // 16 : j1 // 16]
-            nc.vector.tensor_copy(codes, x_codes[:, 0:tokens].indirect(lst))
-            nc.vector.tensor_copy(scales, x_bytes[:, 0:tokens].indirect(lst))
+        def gather(dst, table, j0, j1):
+            nc.vector.tensor_copy(dst, table.indirect(offsets[:, j0 // 16 : j1 // 16]))
 
         s_codes = keep.tile([P, 3 * C], U32, name="s_codes", align_bytes=64)
         s_bytes = keep.tile([P, 3 * C], U8, name="s_bytes", align_bytes=64)
-        for j0, j1, tokens in ((0, C, T), (C, 3 * C, T)):
-            gather(j0, j1, tokens, s_codes[:, j0:j1], s_bytes[:, j0:j1])
+        gather(s_codes[:, 0:64], x_codes[:, 0:512], 0, 64)
+        gather(s_codes[:, 64:160], x_codes[:], 64, 160)
+        gather(s_bytes[:, 0:C], x_bytes[:], 0, C)
+        gather(s_codes[:, 160 : 3 * C], x_codes[:], 160, 3 * C)
+        gather(s_bytes[:, C : 3 * C], x_bytes[:], C, 3 * C)
         slots = [(s_codes[:, e * C : (e + 1) * C], s_bytes[:, e * C : (e + 1) * C]) for e in range(E - 1)]
         by_slot = [keep.tile([P, H], BF16, name=f"by_slot{e}", align_bytes=64) for e in range(2)]
         hidden = [keep.tile([P, 4 * G * C], BF16, name=f"h{e}", align_bytes=64) for e in range(E - 1)]
@@ -238,7 +242,8 @@ def tile_moe_eps_mlp_silu_kernel(tc, xT, w1_words, w1_scales, w2_words, w2_scale
             silu_by_column(hidden[2][:, g * 4 * C : (g + 1) * 4 * C], first_by_column(2, g, 6 - g)[:])
         s_codes3 = shared.tile([P, C], U32, name="s_codes3", align_bytes=64, offset=0)
         s_bytes3 = shared.tile([P, C], U8, name="s_bytes3", align_bytes=64, offset=4 * C)
-        gather(3 * C, 4 * C, T, s_codes3[:], s_bytes3[:])
+        gather(s_codes3[:], x_codes[:], 3 * C, 4 * C)
+        gather(s_bytes3[:], x_bytes[:], 3 * C, 4 * C)
         slots.append((s_codes3[:], s_bytes3[:]))
         turned = [turn(0, 4), turn(1, 7)]
         permute_words(3, 0, G)

@@ -8,7 +8,8 @@ FLOPS = 805306368
 K, T, E, C, H, N = 512, 640, 4, 128, 1024, 256
 R = 4
 P = 128
-G = H // 512
+PASS = 4 * P
+G = H // PASS
 
 F32 = mybir.dt.float32
 BF16 = mybir.dt.bfloat16
@@ -21,6 +22,8 @@ FP4X4 = mybir.dt.float4_e2m1fn_x4
 ACT = mybir.ActivationFunctionType
 
 CHUNKS = [(0, 256), (256, 256), (512, 128)]
+ON_VECTOR = [176, 96, 80]
+FIRST_WIDTHS = [128, 128, 256, 256, 256]
 
 
 def tile_moe_eps_mlp_silu_kernel(tc, xT, w1_words, w1_scales, w2_words, w2_scales, offs, out):
@@ -71,9 +74,6 @@ def tile_moe_eps_mlp_silu_kernel(tc, xT, w1_words, w1_scales, w2_words, w2_scale
             c0, w = CHUNKS[i]
             nc.sync.dma_start(x_raw[i][:], xT[:, c0 : c0 + w].rearrange("(p j) w -> p j w", j=4))
 
-        def load_words(e):
-            nc.sync.dma_start(raw[e][:].bitcast(I32), w1_words[e, 0].bitcast(I32))
-
         load_x(0)
         for r in range(4):
             nc.sync.dma_start(packed[r:P:16, :].bitcast(I32), w1_scales[2:4, 0, r:16:4, :].rearrange("e q n -> q e n").bitcast(I32))
@@ -86,15 +86,15 @@ def tile_moe_eps_mlp_silu_kernel(tc, xT, w1_words, w1_scales, w2_words, w2_scale
                 w1_scales[0:2, 0, r:16:4, :].rearrange("e q n -> q e n").bitcast(I32),
             )
         nc.sync.dma_start(raw01[:].bitcast(I32), w1_words[0:2, 0].rearrange("e p b -> p e b").bitcast(I32))
-        load_words(2)
-        load_words(3)
+        for e in (2, 3):
+            nc.sync.dma_start(raw[e][:].bitcast(I32), w1_words[e, 0].bitcast(I32))
         for g in range(G):
-            cols = slice(g * 512, (g + 1) * 512)
+            cols = slice(g * PASS, (g + 1) * PASS)
             nc.vector.tensor_copy(
                 permuted[:, cols].rearrange("p (t m) -> p t m", t=4),
                 packed[:, cols].rearrange("p (m t) -> p t m", t=4),
             )
-        nc.sync.dma_start(moved[0:112, :].bitcast(I32), permuted[16:P, :].bitcast(I32))
+        nc.sync.dma_start(moved[0 : P - 16, :].bitcast(I32), permuted[16:P, :].bitcast(I32))
         for r in range(4):
             nc.sync.dma_start(
                 w2_plane[r:P:32].rearrange("p (a n) -> p a n", n=N).bitcast(I32),
@@ -102,36 +102,33 @@ def tile_moe_eps_mlp_silu_kernel(tc, xT, w1_words, w1_scales, w2_words, w2_scale
             )
         nc.sync.dma_start(w2[:].bitcast(I32), w2_words.rearrange("e s p b -> p (e s) b").bitcast(I32))
 
-        def cast(chunk, c, w, on_scalar):
-            t0 = CHUNKS[chunk][0] + c
-            dst = grouped[:, 4 * t0 : 4 * (t0 + w)].rearrange("p (c i j) -> p c j i", i=4, j=4)
-            src = x_raw[chunk][:, :, c : c + w].rearrange("p j (c i) -> p c j i", i=4)
-            if on_scalar:
-                nc.scalar.activation(dst, src, ACT.Copy)
-            else:
-                nc.vector.tensor_copy(dst, src)
+        def round_chunk(i):
+            c0, w = CHUNKS[i]
+            dst = grouped[:, 4 * c0 : 4 * (c0 + w)].rearrange("p (c u j) -> p c j u", u=4, j=4)
+            src = x_raw[i][:].rearrange("p j (c u) -> p c j u", u=4)
+            split = ON_VECTOR[i] // 4
+            nc.vector.tensor_copy(dst[:, 0:split], src[:, 0:split])
+            nc.scalar.activation(dst[:, split : w // 4], src[:, split : w // 4], ACT.Copy)
 
-        def quantise(c0, w):
+        def quantise_chunk(i):
+            c0, w = CHUNKS[i]
             nc.vector.quantize_mx(x_codes[:, c0 : c0 + w].bitcast(FP8X4), x_bytes[:, c0 : c0 + w], grouped[:, 4 * c0 : 4 * (c0 + w)])
 
-        cast(0, 0, 128, False)
-        cast(0, 128, 128, True)
-        quantise(0, 256)
-        cast(1, 0, 96, False)
-        cast(1, 96, 160, True)
-        cast(2, 0, 80, False)
-        cast(2, 80, 48, True)
-        quantise(256, 256)
-        quantise(512, 128)
+        round_chunk(0)
+        quantise_chunk(0)
+        round_chunk(1)
+        round_chunk(2)
+        quantise_chunk(1)
+        quantise_chunk(2)
 
-        unused = banks.tile([P, 512], F32, name="unused", tag="bank7")
+        unused = banks.tile([P, PASS], F32, name="unused", tag="bank7")
         for repeat in range(3):
             nc.tensor.matmul_mx(
                 out=unused[:],
                 lhsT=zero_codes[:].bitcast(FP8X4),
                 lhsT_scale=zero_bytes[:],
                 rhs=packed[:].bitcast(FP4X4),
-                rhs_scale=permuted[:, 0:512],
+                rhs_scale=permuted[:, 0:PASS],
                 start=True,
                 stop=True,
             )
@@ -139,12 +136,13 @@ def tile_moe_eps_mlp_silu_kernel(tc, xT, w1_words, w1_scales, w2_words, w2_scale
         def gather(dst, table, j0, j1):
             nc.vector.tensor_copy(dst, table.indirect(offsets[:, j0 // 16 : j1 // 16]))
 
+        early, rest = C // 2, C + C // R
         s_codes = keep.tile([P, 3 * C], U32, name="s_codes", align_bytes=64)
         s_bytes = keep.tile([P, 3 * C], U8, name="s_bytes", align_bytes=64)
-        gather(s_codes[:, 0:64], x_codes[:, 0:512], 0, 64)
-        gather(s_codes[:, 64:160], x_codes[:], 64, 160)
+        gather(s_codes[:, 0:early], x_codes[:, 0 : CHUNKS[2][0]], 0, early)
+        gather(s_codes[:, early:rest], x_codes[:], early, rest)
         gather(s_bytes[:, 0:C], x_bytes[:], 0, C)
-        gather(s_codes[:, 160 : 3 * C], x_codes[:], 160, 3 * C)
+        gather(s_codes[:, rest : 3 * C], x_codes[:], rest, 3 * C)
         gather(s_bytes[:, C : 3 * C], x_bytes[:], C, 3 * C)
         slots = [(s_codes[:, e * C : (e + 1) * C], s_bytes[:, e * C : (e + 1) * C]) for e in range(E - 1)]
         by_slot = [keep.tile([P, H], BF16, name=f"by_slot{e}", align_bytes=64) for e in range(2)]
@@ -162,9 +160,9 @@ def tile_moe_eps_mlp_silu_kernel(tc, xT, w1_words, w1_scales, w2_words, w2_scale
                 start=True,
                 stop=True,
             )
-            g, p0 = c // 512, c % 512 // 4
+            g, p0 = c // PASS, c % PASS // 4
             nc.scalar.activation(
-                by_slot[e][:, g * 512 : (g + 1) * 512].rearrange("s (u p d) -> s u p d", u=2, d=2)[:, :, p0 : p0 + width // 4, :],
+                by_slot[e][:, g * PASS : (g + 1) * PASS].rearrange("s (u p d) -> s u p d", u=2, d=2)[:, :, p0 : p0 + width // 4, :],
                 sums[:].rearrange("s (p u d) -> s u p d", u=2, d=2),
                 ACT.Silu,
             )
@@ -181,17 +179,16 @@ def tile_moe_eps_mlp_silu_kernel(tc, xT, w1_words, w1_scales, w2_words, w2_scale
                 turned[:].rearrange("p (g u) s -> p g s u", u=2),
             )
 
-        def permute_words(e, g0, passes):
-            cols = slice(g0 * H, (g0 + passes) * H)
+        def permute_words(e):
             nc.vector.tensor_copy(
-                w1[e][:, cols].bitcast(U16).rearrange("p (g t m) -> p g t m", g=passes, t=4),
-                raw[e][:, cols].bitcast(U16).rearrange("p (g m t) -> p g t m", g=passes, t=4),
+                w1[e][:].bitcast(U16).rearrange("p (g t m) -> p g t m", g=G, t=4),
+                raw[e][:].bitcast(U16).rearrange("p (g m t) -> p g t m", g=G, t=4),
             )
 
-        def first_by_column(e, g, bank):
+        def first_by_column(e, g, bank, dst):
             sums = banks.tile([P, 4, C], F32, name=f"a{e}_{g}", tag=f"bank{bank}")
             for t in range(4):
-                c = g * 512 + t * P
+                c = g * PASS + t * P
                 nc.tensor.matmul_mx(
                     out=sums[:, t, :],
                     lhsT=w1[e][:, 2 * c : 2 * c + 2 * P].bitcast(FP4X4),
@@ -201,10 +198,7 @@ def tile_moe_eps_mlp_silu_kernel(tc, xT, w1_words, w1_scales, w2_words, w2_scale
                     start=True,
                     stop=True,
                 )
-            return sums
-
-        def silu_by_column(dst, sums):
-            nc.scalar.activation(dst.rearrange("p (n t) -> p n t", t=4), sums.rearrange("p t n -> p n t"), ACT.Silu)
+            nc.scalar.activation(dst.rearrange("p (s t) -> p s t", t=4), sums[:].rearrange("p t s -> p s t"), ACT.Silu)
 
         def quantise_hidden(name, h, words):
             codes = keep.tile([P, words], U32, name=f"{name}_codes", align_bytes=64)
@@ -230,43 +224,41 @@ def tile_moe_eps_mlp_silu_kernel(tc, xT, w1_words, w1_scales, w2_words, w2_scale
                 for g in range(G):
                     second_pass(y[i], e, g, i, codes[:, g * C : (g + 1) * C], scales[:, g * C : (g + 1) * C])
 
-        first_by_slot(0, 0, 128, 6)
-        first_by_slot(0, 128, 128, 5)
-        first_by_slot(0, 256, 256, 0)
-        first_by_slot(0, 512, 256, 1)
-        first_by_slot(0, 768, 256, 4)
-        first_by_slot(1, 0, 512, 2)
-        first_by_slot(1, 512, 512, 3)
-        permute_words(2, 0, G)
+        for width_index, bank in enumerate((6, 5, 0, 1, 4)):
+            first_by_slot(0, sum(FIRST_WIDTHS[:width_index]), FIRST_WIDTHS[width_index], bank)
         for g in range(G):
-            silu_by_column(hidden[2][:, g * 4 * C : (g + 1) * 4 * C], first_by_column(2, g, 6 - g)[:])
+            first_by_slot(1, g * PASS, PASS, 2 + g)
+        permute_words(2)
+        for g, bank in enumerate((6, 5)):
+            first_by_column(2, g, bank, hidden[2][:, g * 4 * C : (g + 1) * 4 * C])
+        last = E - 1
         s_codes3 = shared.tile([P, C], U32, name="s_codes3", align_bytes=64, offset=0)
         s_bytes3 = shared.tile([P, C], U8, name="s_bytes3", align_bytes=64, offset=4 * C)
-        gather(s_codes3[:], x_codes[:], 3 * C, 4 * C)
-        gather(s_bytes3[:], x_bytes[:], 3 * C, 4 * C)
+        gather(s_codes3[:], x_codes[:], last * C, E * C)
+        gather(s_bytes3[:], x_bytes[:], last * C, E * C)
         slots.append((s_codes3[:], s_bytes3[:]))
         turned = [turn(0, 4), turn(1, 7)]
-        permute_words(3, 0, G)
-        e = E - 1
-        for g in range(G):
-            silu_by_column(last_hidden[g][:], first_by_column(e, g, 3 * g)[:])
-        copy_turned(0, turned[0])
-        copy_turned(1, turned[1])
+        permute_words(last)
+        for g, bank in enumerate((0, 3)):
+            first_by_column(last, g, bank, last_hidden[g][:])
+        for e in range(2):
+            copy_turned(e, turned[e])
+
         y02 = banks.tile([P, 2, 2, C], F32, name="y02", tag="bank4")
         second(0, [y02[:, 0, i, :] for i in range(2)])
         second(2, [y02[:, 1, i, :] for i in range(2)])
-        y1 = [banks.tile([P, C], F32, name=f"y1_{i}", tag=f"bank{(7, 1)[i]}") for i in range(2)]
+        y1 = [banks.tile([P, C], F32, name=f"y1_{i}", tag=f"bank{bank}") for i, bank in enumerate((7, 1))]
         second(1, [y[:] for y in y1])
-        last = [banks.tile([P, C], F32, name=f"last{i}", tag=f"bank{5 + i}") for i in range(2)]
+        y3 = [banks.tile([P, C], F32, name=f"last{i}", tag=f"bank{bank}") for i, bank in enumerate((5, 6))]
         for g in range(G):
-            codes, scales = quantise_hidden(f"h{e}_{g}", last_hidden[g], C)
+            codes, scales = quantise_hidden(f"h{last}_{g}", last_hidden[g], C)
             for i in range(2):
-                second_pass(last[i][:], e, g, i, codes[:], scales[:])
+                second_pass(y3[i][:], last, g, i, codes[:], scales[:])
+
         ranked = results[:].rearrange("p i (m e u) -> p e i m u", m=R, e=E)
         nc.scalar.copy(ranked[:, 0:3:2], y02[:].rearrange("p e i (m u) -> p e i m u", m=R))
-        nc.vector.tensor_copy(ranked[:, 1, 0], y1[0][:].rearrange("p (m u) -> p m u", m=R))
-        nc.scalar.copy(ranked[:, 1, 1], y1[1][:].rearrange("p (m u) -> p m u", m=R))
-        nc.vector.tensor_copy(ranked[:, e, 0], last[0][:].rearrange("p (m u) -> p m u", m=R))
-        nc.scalar.copy(ranked[:, e, 1], last[1][:].rearrange("p (m u) -> p m u", m=R))
+        for e, y in ((1, y1), (last, y3)):
+            nc.vector.tensor_copy(ranked[:, e, 0], y[0][:].rearrange("p (m u) -> p m u", m=R))
+            nc.scalar.copy(ranked[:, e, 1], y[1][:].rearrange("p (m u) -> p m u", m=R))
         nc.sync.dma_start(out[0:P, :], results[:, 0, :])
         nc.scalar.dma_start(out[P : 2 * P, :], results[:, 1, :])

@@ -22,7 +22,7 @@ FP4X4 = mybir.dt.float4_e2m1fn_x4
 ACT = mybir.ActivationFunctionType
 
 CHUNKS = [(0, 256), (256, 256), (512, 128)]
-ON_VECTOR = [176, 96, 80]
+ON_VECTOR = [176, 160, 64]
 FIRST_WIDTHS = [128, 128, 256, 256, 256]
 
 
@@ -31,12 +31,13 @@ def tile_moe_eps_mlp_silu_kernel(tc, xT, w1_words, w1_scales, w2_words, w2_scale
     with ExitStack() as ctx:
         keep = ctx.enter_context(tc.tile_pool(name="keep", bufs=1))
         shared = ctx.enter_context(tc.tile_pool(name="shared", bufs=1))
+        first = ctx.enter_context(tc.tile_pool(name="first", bufs=1))
         banks = ctx.enter_context(tc.psum_pool(name="banks", bufs=1))
 
         offsets = keep.tile([P, E * C // 16], U16, name="offsets")
-        packed = keep.tile([P, H], U8, name="packed", align_bytes=64)
-        permuted = keep.tile([P, H], U8, name="permuted", align_bytes=64)
-        moved = keep.tile([P, H], U8, name="moved", align_bytes=64)
+        packed = first.tile([P, H], U8, name="packed", align_bytes=64, offset=0)
+        permuted = first.tile([P, H], U8, name="permuted", align_bytes=64, offset=H)
+        moved = keep.tile([P, 2 * H], U8, name="moved", align_bytes=64)
         plain = keep.tile([P, 2 * H], U8, name="plain", align_bytes=64)
         x_bytes = keep.tile([P, T], U8, name="x_bytes", align_bytes=64)
         x_codes = keep.tile([P, T], U32, name="x_codes", align_bytes=64)
@@ -47,7 +48,6 @@ def tile_moe_eps_mlp_silu_kernel(tc, xT, w1_words, w1_scales, w2_words, w2_scale
             3: keep.tile([P, 2 * H], U8, name="raw3", align_bytes=64),
         }
         w1 = {e: keep.tile([P, 2 * H], U8, name=f"w1_{e}", align_bytes=64) for e in (2, 3)}
-        w1_plane = {2: permuted, 3: moved}
         identity = keep.tile([P, P], F32, name="identity")
         make_identity(nc, identity[:])
         w2_plane = keep.tile([P, E * G * N], U8, name="w2_plane", align_bytes=64)
@@ -57,34 +57,31 @@ def tile_moe_eps_mlp_silu_kernel(tc, xT, w1_words, w1_scales, w2_words, w2_scale
         warm = keep.tile([P, 1], F32, name="warm")
         warm_out = keep.tile([P, 1], F32, name="warm_out")
         zeros = keep.tile([P, 4 * P], BF16, name="zeros", align_bytes=64)
-        zero_codes = keep.tile([P, P], U32, name="zero_codes", align_bytes=64)
-        zero_bytes = keep.tile([P, P], U8, name="zero_bytes", align_bytes=64)
 
-        nc.vector.memset(packed[:].bitcast(I32), 0)
+        nc.vector.memset(plain[:].bitcast(I32), 0)
         nc.vector.memset(warm[:], 0.0)
         nc.scalar.activation(warm_out[:], warm[:], ACT.Silu)
+        nc.vector.memset(packed[32:64, :].bitcast(I32), 0)
+        nc.vector.memset(packed[64:P, :].bitcast(I32), 0)
         nc.vector.memset(x_bytes[:].bitcast(I32), 0)
-        nc.vector.memset(plain[:].bitcast(I32), 0)
-        nc.vector.memset(moved[:].bitcast(I32), 0)
-        nc.vector.memset(w2_plane[:].bitcast(I32), 0)
+        nc.gpsimd.memset(moved[:].bitcast(I32), 0)
+        nc.gpsimd.memset(w2_plane[:].bitcast(I32), 0)
         nc.vector.memset(zeros[:], 0.0)
-        nc.vector.quantize_mx(zero_codes[:].bitcast(FP8X4), zero_bytes[:], zeros[:])
 
         def load_x(i):
             c0, w = CHUNKS[i]
             nc.sync.dma_start(x_raw[i][:], xT[:, c0 : c0 + w].rearrange("(p j) w -> p j w", j=4))
 
+        nc.sync.dma_start(packed[0:32, :].bitcast(I32), w1_scales[2:4, 0].rearrange("e j n -> j e n").bitcast(I32))
         load_x(0)
-        for r in range(4):
-            nc.sync.dma_start(packed[r:P:16, :].bitcast(I32), w1_scales[2:4, 0, r:16:4, :].rearrange("e q n -> q e n").bitcast(I32))
-        load_x(1)
-        load_x(2)
-        nc.sync.dma_start(offsets[:], offs)
         for r in range(4):
             nc.sync.dma_start(
                 plain[r:P:32].rearrange("p (e n) -> p e n", e=2).bitcast(I32),
                 w1_scales[0:2, 0, r:16:4, :].rearrange("e q n -> q e n").bitcast(I32),
             )
+        load_x(1)
+        load_x(2)
+        nc.sync.dma_start(offsets[:], offs)
         nc.sync.dma_start(raw01[:].bitcast(I32), w1_words[0:2, 0].rearrange("e p b -> p e b").bitcast(I32))
         for e in (2, 3):
             nc.sync.dma_start(raw[e][:].bitcast(I32), w1_words[e, 0].bitcast(I32))
@@ -94,13 +91,11 @@ def tile_moe_eps_mlp_silu_kernel(tc, xT, w1_words, w1_scales, w2_words, w2_scale
                 permuted[:, cols].rearrange("p (t m) -> p t m", t=4),
                 packed[:, cols].rearrange("p (m t) -> p t m", t=4),
             )
-        nc.sync.dma_start(moved[0 : P - 16, :].bitcast(I32), permuted[16:P, :].bitcast(I32))
-        for r in range(4):
+        for q in (0, 2, 1, 3):
             nc.sync.dma_start(
-                w2_plane[r:P:32].rearrange("p (a n) -> p a n", n=N).bitcast(I32),
-                w2_scales[:, :, r:16:4, :].rearrange("e s q n -> q (e s) n").bitcast(I32),
+                moved[32 * q : 32 * q + 4, :].rearrange("p (e n) -> p e n", e=2).bitcast(I32),
+                permuted[8 * q : 8 * q + 8, :].bitcast(I32),
             )
-        nc.sync.dma_start(w2[:].bitcast(I32), w2_words.rearrange("e s p b -> p (e s) b").bitcast(I32))
 
         def round_chunk(i):
             c0, w = CHUNKS[i]
@@ -114,6 +109,9 @@ def tile_moe_eps_mlp_silu_kernel(tc, xT, w1_words, w1_scales, w2_words, w2_scale
             c0, w = CHUNKS[i]
             nc.vector.quantize_mx(x_codes[:, c0 : c0 + w].bitcast(FP8X4), x_bytes[:, c0 : c0 + w], grouped[:, 4 * c0 : 4 * (c0 + w)])
 
+        zero_codes = first.tile([P, P], U32, name="zero_codes", align_bytes=64, offset=0)
+        zero_bytes = first.tile([P, P], U8, name="zero_bytes", align_bytes=64, offset=4 * P)
+        nc.vector.quantize_mx(zero_codes[:].bitcast(FP8X4), zero_bytes[:], zeros[:])
         round_chunk(0)
         quantise_chunk(0)
         round_chunk(1)
@@ -127,10 +125,17 @@ def tile_moe_eps_mlp_silu_kernel(tc, xT, w1_words, w1_scales, w2_words, w2_scale
                 out=unused[:],
                 lhsT=zero_codes[:].bitcast(FP8X4),
                 lhsT_scale=zero_bytes[:],
-                rhs=packed[:].bitcast(FP4X4),
-                rhs_scale=permuted[:, 0:PASS],
+                rhs=w2_plane[:, 0 : 2 * PASS].bitcast(FP4X4),
+                rhs_scale=w2_plane[:, 2 * PASS : 3 * PASS],
                 start=True,
                 stop=True,
+            )
+
+        nc.sync.dma_start(w2[:].bitcast(I32), w2_words.rearrange("e s p b -> p (e s) b").bitcast(I32))
+        for r in range(4):
+            nc.sync.dma_start(
+                w2_plane[r:P:32].rearrange("p (a n) -> p a n", n=N).bitcast(I32),
+                w2_scales[:, :, r:16:4, :].rearrange("e s q n -> q (e s) n").bitcast(I32),
             )
 
         def gather(dst, table, j0, j1):
@@ -145,7 +150,8 @@ def tile_moe_eps_mlp_silu_kernel(tc, xT, w1_words, w1_scales, w2_words, w2_scale
         gather(s_codes[:, rest : 3 * C], x_codes[:], rest, 3 * C)
         gather(s_bytes[:, C : 3 * C], x_bytes[:], C, 3 * C)
         slots = [(s_codes[:, e * C : (e + 1) * C], s_bytes[:, e * C : (e + 1) * C]) for e in range(E - 1)]
-        by_slot = [keep.tile([P, H], BF16, name=f"by_slot{e}", align_bytes=64) for e in range(2)]
+        by_slot = {(e, g): keep.tile([P, PASS], BF16, name=f"by_slot{e}_{g}", align_bytes=64) for e, g in ((0, 0), (0, 1), (1, 0))}
+        by_slot[1, 1] = first.tile([P, PASS], BF16, name="by_slot1_1", align_bytes=64, offset=H)
         hidden = [keep.tile([P, 4 * G * C], BF16, name=f"h{e}", align_bytes=64) for e in range(E - 1)]
         last_hidden = [keep.tile([P, 4 * C], BF16, name=f"h3_{g}", align_bytes=64) for g in range(G)]
 
@@ -162,15 +168,16 @@ def tile_moe_eps_mlp_silu_kernel(tc, xT, w1_words, w1_scales, w2_words, w2_scale
             )
             g, p0 = c // PASS, c % PASS // 4
             nc.scalar.activation(
-                by_slot[e][:, g * PASS : (g + 1) * PASS].rearrange("s (u p d) -> s u p d", u=2, d=2)[:, :, p0 : p0 + width // 4, :],
+                by_slot[e, g][:].rearrange("s (u p d) -> s u p d", u=2, d=2)[:, :, p0 : p0 + width // 4, :],
                 sums[:].rearrange("s (p u d) -> s u p d", u=2, d=2),
                 ACT.Silu,
             )
 
         def turn(e, bank):
             turned = banks.tile([P, 2 * G, C], F32, name=f"turned{e}", tag=f"bank{bank}")
-            for q in range(2 * G):
-                nc.tensor.transpose(turned[:, q, :], by_slot[e][:].bitcast(F32)[:, q * P : (q + 1) * P], identity[:])
+            for g in reversed(range(G)):
+                for u in range(2):
+                    nc.tensor.transpose(turned[:, 2 * g + u, :], by_slot[e, g][:].bitcast(F32)[:, u * P : (u + 1) * P], identity[:])
             return turned
 
         def copy_turned(e, turned):
@@ -192,7 +199,7 @@ def tile_moe_eps_mlp_silu_kernel(tc, xT, w1_words, w1_scales, w2_words, w2_scale
                 nc.tensor.matmul_mx(
                     out=sums[:, t, :],
                     lhsT=w1[e][:, 2 * c : 2 * c + 2 * P].bitcast(FP4X4),
-                    lhsT_scale=w1_plane[e][:, c : c + P],
+                    lhsT_scale=moved[:, (e - 2) * H + c : (e - 2) * H + c + P],
                     rhs=slots[e][0].bitcast(FP8X4),
                     rhs_scale=slots[e][1],
                     start=True,

@@ -74,14 +74,14 @@ def tile_moe_eps_mlp_silu_kernel(tc, xT, w1_words, w1_scales, w2_words, w2_scale
 
         nc.sync.dma_start(packed[0:32, :].bitcast(I32), w1_scales[2:4, 0].rearrange("e j n -> j e n").bitcast(I32))
         load_x(0)
+        load_x(1)
+        load_x(2)
+        nc.sync.dma_start(offsets[:], offs)
         for r in range(4):
             nc.sync.dma_start(
                 plain[r:P:32].rearrange("p (e n) -> p e n", e=2).bitcast(I32),
                 w1_scales[0:2, 0, r:16:4, :].rearrange("e q n -> q e n").bitcast(I32),
             )
-        load_x(1)
-        load_x(2)
-        nc.sync.dma_start(offsets[:], offs)
         nc.sync.dma_start(raw01[:].bitcast(I32), w1_words[0:2, 0].rearrange("e p b -> p e b").bitcast(I32))
         for e in (2, 3):
             nc.sync.dma_start(raw[e][:].bitcast(I32), w1_words[e, 0].bitcast(I32))
@@ -173,9 +173,9 @@ def tile_moe_eps_mlp_silu_kernel(tc, xT, w1_words, w1_scales, w2_words, w2_scale
                 ACT.Silu,
             )
 
-        def turn(e, bank):
+        def turn(e, bank, order):
             turned = banks.tile([P, 2 * G, C], F32, name=f"turned{e}", tag=f"bank{bank}")
-            for g in reversed(range(G)):
+            for g in order:
                 for u in range(2):
                     nc.tensor.transpose(turned[:, 2 * g + u, :], by_slot[e, g][:].bitcast(F32)[:, u * P : (u + 1) * P], identity[:])
             return turned
@@ -244,17 +244,17 @@ def tile_moe_eps_mlp_silu_kernel(tc, xT, w1_words, w1_scales, w2_words, w2_scale
         gather(s_codes3[:], x_codes[:], last * C, E * C)
         gather(s_bytes3[:], x_bytes[:], last * C, E * C)
         slots.append((s_codes3[:], s_bytes3[:]))
-        turned = [turn(0, 4), turn(1, 7)]
+        turned = [turn(0, 7, (0, 1)), turn(1, 4, (1, 0))]
         permute_words(last)
         for g, bank in enumerate((0, 3)):
             first_by_column(last, g, bank, last_hidden[g][:])
         for e in range(2):
             copy_turned(e, turned[e])
 
-        y02 = banks.tile([P, 2, 2, C], F32, name="y02", tag="bank4")
+        y02 = banks.tile([P, 2, 2, C], F32, name="y02", tag="bank7")
         second(0, [y02[:, 0, i, :] for i in range(2)])
         second(2, [y02[:, 1, i, :] for i in range(2)])
-        y1 = [banks.tile([P, C], F32, name=f"y1_{i}", tag=f"bank{bank}") for i, bank in enumerate((7, 1))]
+        y1 = [banks.tile([P, C], F32, name=f"y1_{i}", tag=f"bank{bank}") for i, bank in enumerate((4, 1))]
         second(1, [y[:] for y in y1])
         y3 = [banks.tile([P, C], F32, name=f"last{i}", tag=f"bank{bank}") for i, bank in enumerate((5, 6))]
         for g in range(G):

@@ -22,8 +22,9 @@ FP4X4 = mybir.dt.float4_e2m1fn_x4
 ACT = mybir.ActivationFunctionType
 
 CHUNKS = [(0, 256), (256, 256), (512, 128)]
-ON_VECTOR = [176, 160, 64]
+ON_VECTOR = [176, 144, 64]
 FIRST_WIDTHS = [128, 128, 256, 256, 256]
+ROWS_AT = P - 32
 
 
 def tile_moe_eps_mlp_silu_kernel(tc, xT, w1_words, w1_scales, w2_words, w2_scales, offs, out):
@@ -35,8 +36,8 @@ def tile_moe_eps_mlp_silu_kernel(tc, xT, w1_words, w1_scales, w2_words, w2_scale
         banks = ctx.enter_context(tc.psum_pool(name="banks", bufs=1))
 
         offsets = keep.tile([P, E * C // 16], U16, name="offsets")
-        packed = first.tile([P, H], U8, name="packed", align_bytes=64, offset=0)
-        permuted = first.tile([P, H], U8, name="permuted", align_bytes=64, offset=H)
+        packed = keep.tile([P, H], U8, name="packed", align_bytes=64)
+        permuted = first.tile([P, H], U8, name="permuted", align_bytes=64, offset=4 * H)
         moved = keep.tile([P, 2 * H], U8, name="moved", align_bytes=64)
         plain = keep.tile([P, 2 * H], U8, name="plain", align_bytes=64)
         x_bytes = keep.tile([P, T], U8, name="x_bytes", align_bytes=64)
@@ -52,27 +53,25 @@ def tile_moe_eps_mlp_silu_kernel(tc, xT, w1_words, w1_scales, w2_words, w2_scale
         make_identity(nc, identity[:])
         w2_plane = keep.tile([P, E * G * N], U8, name="w2_plane", align_bytes=64)
         w2 = keep.tile([P, E * G, 2 * N], U8, name="w2", align_bytes=64)
-        x_raw = [keep.tile([P, 4, w], F32, name=f"x_raw{i}", align_bytes=64) for i, (c0, w) in enumerate(CHUNKS)]
+        x_raw = [first.tile([P, 4, CHUNKS[0][1]], F32, name="x_raw0", align_bytes=64, offset=0)]
+        x_raw.extend(keep.tile([P, 4, w], F32, name=f"x_raw{c0}", align_bytes=64) for c0, w in CHUNKS[1:])
         results = keep.tile([P, 2, E * C], F32, name="results")
         warm = keep.tile([P, 1], F32, name="warm")
         warm_out = keep.tile([P, 1], F32, name="warm_out")
-        zeros = keep.tile([P, 4 * P], BF16, name="zeros", align_bytes=64)
 
         nc.vector.memset(plain[:].bitcast(I32), 0)
         nc.vector.memset(warm[:], 0.0)
         nc.scalar.activation(warm_out[:], warm[:], ACT.Silu)
-        nc.vector.memset(packed[32:64, :].bitcast(I32), 0)
-        nc.vector.memset(packed[64:P, :].bitcast(I32), 0)
+        nc.vector.memset(packed[0:ROWS_AT, :].bitcast(I32), 0)
         nc.vector.memset(x_bytes[:].bitcast(I32), 0)
-        nc.gpsimd.memset(moved[:].bitcast(I32), 0)
-        nc.gpsimd.memset(w2_plane[:].bitcast(I32), 0)
-        nc.vector.memset(zeros[:], 0.0)
+        nc.vector.memset(moved[:].bitcast(I32), 0)
+        nc.vector.memset(w2_plane[:].bitcast(I32), 0)
 
         def load_x(i):
             c0, w = CHUNKS[i]
             nc.sync.dma_start(x_raw[i][:], xT[:, c0 : c0 + w].rearrange("(p j) w -> p j w", j=4))
 
-        nc.sync.dma_start(packed[0:32, :].bitcast(I32), w1_scales[2:4, 0].rearrange("e j n -> j e n").bitcast(I32))
+        nc.sync.dma_start(packed[ROWS_AT:P, :].bitcast(I32), w1_scales[2:4, 0].rearrange("e j n -> j e n").bitcast(I32))
         load_x(0)
         load_x(1)
         load_x(2)
@@ -94,7 +93,7 @@ def tile_moe_eps_mlp_silu_kernel(tc, xT, w1_words, w1_scales, w2_words, w2_scale
         for q in (0, 2, 1, 3):
             nc.sync.dma_start(
                 moved[32 * q : 32 * q + 4, :].rearrange("p (e n) -> p e n", e=2).bitcast(I32),
-                permuted[8 * q : 8 * q + 8, :].bitcast(I32),
+                permuted[ROWS_AT + 8 * q : ROWS_AT + 8 * q + 8, :].bitcast(I32),
             )
 
         def round_chunk(i):
@@ -109,10 +108,10 @@ def tile_moe_eps_mlp_silu_kernel(tc, xT, w1_words, w1_scales, w2_words, w2_scale
             c0, w = CHUNKS[i]
             nc.vector.quantize_mx(x_codes[:, c0 : c0 + w].bitcast(FP8X4), x_bytes[:, c0 : c0 + w], grouped[:, 4 * c0 : 4 * (c0 + w)])
 
+        round_chunk(0)
         zero_codes = first.tile([P, P], U32, name="zero_codes", align_bytes=64, offset=0)
         zero_bytes = first.tile([P, P], U8, name="zero_bytes", align_bytes=64, offset=4 * P)
-        nc.vector.quantize_mx(zero_codes[:].bitcast(FP8X4), zero_bytes[:], zeros[:])
-        round_chunk(0)
+        nc.vector.quantize_mx(zero_codes[:].bitcast(FP8X4), zero_bytes[:], w2_plane[:, 0 : 2 * PASS].bitcast(BF16))
         quantise_chunk(0)
         round_chunk(1)
         round_chunk(2)
@@ -125,8 +124,8 @@ def tile_moe_eps_mlp_silu_kernel(tc, xT, w1_words, w1_scales, w2_words, w2_scale
                 out=unused[:],
                 lhsT=zero_codes[:].bitcast(FP8X4),
                 lhsT_scale=zero_bytes[:],
-                rhs=w2_plane[:, 0 : 2 * PASS].bitcast(FP4X4),
-                rhs_scale=w2_plane[:, 2 * PASS : 3 * PASS],
+                rhs=permuted[:].bitcast(FP4X4),
+                rhs_scale=permuted[:, 0:PASS],
                 start=True,
                 stop=True,
             )
@@ -151,7 +150,7 @@ def tile_moe_eps_mlp_silu_kernel(tc, xT, w1_words, w1_scales, w2_words, w2_scale
         gather(s_bytes[:, C : 3 * C], x_bytes[:], C, 3 * C)
         slots = [(s_codes[:, e * C : (e + 1) * C], s_bytes[:, e * C : (e + 1) * C]) for e in range(E - 1)]
         by_slot = {(e, g): keep.tile([P, PASS], BF16, name=f"by_slot{e}_{g}", align_bytes=64) for e, g in ((0, 0), (0, 1), (1, 0))}
-        by_slot[1, 1] = first.tile([P, PASS], BF16, name="by_slot1_1", align_bytes=64, offset=H)
+        by_slot[1, 1] = first.tile([P, PASS], BF16, name="by_slot1_1", align_bytes=64, offset=4 * H)
         hidden = [keep.tile([P, 4 * G * C], BF16, name=f"h{e}", align_bytes=64) for e in range(E - 1)]
         last_hidden = [keep.tile([P, 4 * C], BF16, name=f"h3_{g}", align_bytes=64) for g in range(G)]
 

@@ -31,7 +31,6 @@ def tile_moe_eps_mlp_silu_kernel(tc, xT, w1_words, w1_scales, w2_words, w2_scale
     nc = tc.nc
     with ExitStack() as ctx:
         keep = ctx.enter_context(tc.tile_pool(name="keep", bufs=1))
-        shared = ctx.enter_context(tc.tile_pool(name="shared", bufs=1))
         first = ctx.enter_context(tc.tile_pool(name="first", bufs=1))
         banks = ctx.enter_context(tc.psum_pool(name="banks", bufs=1))
 
@@ -44,10 +43,7 @@ def tile_moe_eps_mlp_silu_kernel(tc, xT, w1_words, w1_scales, w2_words, w2_scale
         x_codes = keep.tile([P, T], U32, name="x_codes", align_bytes=64)
         grouped = keep.tile([P, 4 * T], BF16, name="grouped", align_bytes=64)
         raw01 = keep.tile([P, 2, 2 * H], U8, name="raw01", align_bytes=64)
-        raw = {
-            2: shared.tile([P, 2 * H], U8, name="raw2", align_bytes=64, offset=0),
-            3: keep.tile([P, 2 * H], U8, name="raw3", align_bytes=64),
-        }
+        raw = {e: keep.tile([P, 2 * H], U8, name=f"raw{e}", align_bytes=64) for e in (2, 3)}
         w1 = {e: keep.tile([P, 2 * H], U8, name=f"w1_{e}", align_bytes=64) for e in (2, 3)}
         identity = keep.tile([P, P], F32, name="identity")
         make_identity(nc, identity[:])
@@ -141,14 +137,16 @@ def tile_moe_eps_mlp_silu_kernel(tc, xT, w1_words, w1_scales, w2_words, w2_scale
             nc.vector.tensor_copy(dst, table.indirect(offsets[:, j0 // 16 : j1 // 16]))
 
         early, rest = C // 2, C + C // R
-        s_codes = keep.tile([P, 3 * C], U32, name="s_codes", align_bytes=64)
-        s_bytes = keep.tile([P, 3 * C], U8, name="s_bytes", align_bytes=64)
+        s_codes = keep.tile([P, E * C], U32, name="s_codes", align_bytes=64)
+        s_bytes = keep.tile([P, E * C], U8, name="s_bytes", align_bytes=64)
         gather(s_codes[:, 0:early], x_codes[:, 0 : CHUNKS[2][0]], 0, early)
         gather(s_codes[:, early:rest], x_codes[:], early, rest)
         gather(s_bytes[:, 0:C], x_bytes[:], 0, C)
-        gather(s_codes[:, rest : 3 * C], x_codes[:], rest, 3 * C)
-        gather(s_bytes[:, C : 3 * C], x_bytes[:], C, 3 * C)
-        slots = [(s_codes[:, e * C : (e + 1) * C], s_bytes[:, e * C : (e + 1) * C]) for e in range(E - 1)]
+        gather(s_codes[:, rest : 2 * C], x_codes[:], rest, 2 * C)
+        gather(s_bytes[:, C : 2 * C], x_bytes[:], C, 2 * C)
+        gather(s_codes[:, 2 * C : E * C], x_codes[:], 2 * C, E * C)
+        gather(s_bytes[:, 2 * C : E * C], x_bytes[:], 2 * C, E * C)
+        slots = [(s_codes[:, e * C : (e + 1) * C], s_bytes[:, e * C : (e + 1) * C]) for e in range(E)]
         by_slot = {(e, g): keep.tile([P, PASS], BF16, name=f"by_slot{e}_{g}", align_bytes=64) for e, g in ((0, 0), (0, 1), (1, 0))}
         by_slot[1, 1] = first.tile([P, PASS], BF16, name="by_slot1_1", align_bytes=64, offset=4 * H)
         hidden = [keep.tile([P, 4 * G * C], BF16, name=f"h{e}", align_bytes=64) for e in range(E - 1)]
@@ -186,7 +184,7 @@ def tile_moe_eps_mlp_silu_kernel(tc, xT, w1_words, w1_scales, w2_words, w2_scale
             )
 
         def permute_words(e):
-            nc.vector.tensor_copy(
+            nc.gpsimd.tensor_copy(
                 w1[e][:].bitcast(U16).rearrange("p (g t m) -> p g t m", g=G, t=4),
                 raw[e][:].bitcast(U16).rearrange("p (g m t) -> p g t m", g=G, t=4),
             )
@@ -238,11 +236,6 @@ def tile_moe_eps_mlp_silu_kernel(tc, xT, w1_words, w1_scales, w2_words, w2_scale
         for g, bank in enumerate((6, 5)):
             first_by_column(2, g, bank, hidden[2][:, g * 4 * C : (g + 1) * 4 * C])
         last = E - 1
-        s_codes3 = shared.tile([P, C], U32, name="s_codes3", align_bytes=64, offset=0)
-        s_bytes3 = shared.tile([P, C], U8, name="s_bytes3", align_bytes=64, offset=4 * C)
-        gather(s_codes3[:], x_codes[:], last * C, E * C)
-        gather(s_bytes3[:], x_bytes[:], last * C, E * C)
-        slots.append((s_codes3[:], s_bytes3[:]))
         turned = [turn(0, 7, (0, 1)), turn(1, 4, (1, 0))]
         permute_words(last)
         for g, bank in enumerate((0, 3)):

@@ -10,6 +10,7 @@ R = 4
 P = 128
 PASS = 4 * P
 G = H // PASS
+LINE = 256
 
 F32 = mybir.dt.float32
 BF16 = mybir.dt.bfloat16
@@ -34,24 +35,28 @@ def tile_moe_eps_mlp_silu_kernel(tc, xT, w1_words, w1_scales, w2_words, w2_scale
         first = ctx.enter_context(tc.tile_pool(name="first", bufs=1))
         banks = ctx.enter_context(tc.psum_pool(name="banks", bufs=1))
 
+        def shifted(name, columns, dtype, size):
+            lead = LINE // 2 // size
+            return keep.tile([P, lead + columns], dtype, name=name, align_bytes=LINE)[:, lead : lead + columns]
+
         offsets = keep.tile([P, E * C // 16], U16, name="offsets")
-        packed = keep.tile([P, H], U8, name="packed", align_bytes=64)
-        permuted = first.tile([P, H], U8, name="permuted", align_bytes=64, offset=4 * H)
-        moved = keep.tile([P, 2 * H], U8, name="moved", align_bytes=64)
-        plain = keep.tile([P, 2 * H], U8, name="plain", align_bytes=64)
-        x_bytes = keep.tile([P, T], U8, name="x_bytes", align_bytes=64)
-        x_codes = keep.tile([P, T], U32, name="x_codes", align_bytes=64)
-        grouped = keep.tile([P, 4 * T], BF16, name="grouped", align_bytes=64)
-        raw01 = keep.tile([P, 2, 2 * H], U8, name="raw01", align_bytes=64)
-        raw = {e: keep.tile([P, 2 * H], U8, name=f"raw{e}", align_bytes=64) for e in (2, 3)}
-        w1 = {e: keep.tile([P, 2 * H], U8, name=f"w1_{e}", align_bytes=64) for e in (2, 3)}
-        identity = keep.tile([P, P], F32, name="identity")
+        packed = keep.tile([P, H], U8, name="packed", align_bytes=LINE)
+        permuted = first.tile([P, H], U8, name="permuted", align_bytes=LINE, offset=4 * H)
+        moved = keep.tile([P, 2 * H], U8, name="moved", align_bytes=LINE)
+        plain = keep.tile([P, 2 * H], U8, name="plain", align_bytes=LINE)
+        x_bytes = keep.tile([P, T], U8, name="x_bytes", align_bytes=LINE)
+        x_codes = keep.tile([P, T], U32, name="x_codes", align_bytes=LINE)
+        grouped = keep.tile([P, 4 * T], BF16, name="grouped", align_bytes=LINE)
+        raw01 = keep.tile([P, 2, 2 * H], U8, name="raw01", align_bytes=LINE)
+        raw = {e: keep.tile([P, 2 * H], U8, name=f"raw{e}", align_bytes=LINE) for e in (2, 3)}
+        w1 = {e: keep.tile([P, 2 * H], U8, name=f"w1_{e}", align_bytes=LINE) for e in (2, 3)}
+        identity = keep.tile([P, P], F32, name="identity", align_bytes=LINE)
         make_identity(nc, identity[:])
-        w2_plane = keep.tile([P, E * G * N], U8, name="w2_plane", align_bytes=64)
-        w2 = keep.tile([P, E * G, 2 * N], U8, name="w2", align_bytes=64)
-        x_raw = [first.tile([P, 4, CHUNKS[0][1]], F32, name="x_raw0", align_bytes=64, offset=0)]
-        x_raw.extend(keep.tile([P, 4, w], F32, name=f"x_raw{c0}", align_bytes=64) for c0, w in CHUNKS[1:])
-        results = keep.tile([P, 2, E * C], F32, name="results")
+        w2_plane = keep.tile([P, E * G * N], U8, name="w2_plane", align_bytes=LINE)
+        w2 = keep.tile([P, E * G, 2 * N], U8, name="w2", align_bytes=LINE)
+        x_raw = [first.tile([P, 4, CHUNKS[0][1]], F32, name="x_raw0", align_bytes=LINE, offset=0)]
+        x_raw.extend(keep.tile([P, 4, w], F32, name=f"x_raw{c0}", align_bytes=LINE) for c0, w in CHUNKS[1:])
+        results = keep.tile([P, 2, E * C], F32, name="results", align_bytes=LINE)
         warm = keep.tile([P, 1], F32, name="warm")
         warm_out = keep.tile([P, 1], F32, name="warm_out")
 
@@ -105,8 +110,8 @@ def tile_moe_eps_mlp_silu_kernel(tc, xT, w1_words, w1_scales, w2_words, w2_scale
             nc.vector.quantize_mx(x_codes[:, c0 : c0 + w].bitcast(FP8X4), x_bytes[:, c0 : c0 + w], grouped[:, 4 * c0 : 4 * (c0 + w)])
 
         round_chunk(0)
-        zero_codes = first.tile([P, P], U32, name="zero_codes", align_bytes=64, offset=0)
-        zero_bytes = first.tile([P, P], U8, name="zero_bytes", align_bytes=64, offset=4 * P)
+        zero_codes = first.tile([P, P], U32, name="zero_codes", align_bytes=LINE, offset=0)
+        zero_bytes = first.tile([P, P], U8, name="zero_bytes", align_bytes=LINE, offset=4 * P)
         nc.vector.quantize_mx(zero_codes[:].bitcast(FP8X4), zero_bytes[:], w2_plane[:, 0 : 2 * PASS].bitcast(BF16))
         quantise_chunk(0)
         round_chunk(1)
@@ -137,8 +142,8 @@ def tile_moe_eps_mlp_silu_kernel(tc, xT, w1_words, w1_scales, w2_words, w2_scale
             nc.vector.tensor_copy(dst, table.indirect(offsets[:, j0 // 16 : j1 // 16]))
 
         early, rest = C // 2, C + C // R
-        s_codes = keep.tile([P, E * C], U32, name="s_codes", align_bytes=64)
-        s_bytes = keep.tile([P, E * C], U8, name="s_bytes", align_bytes=64)
+        s_codes = shifted("s_codes", E * C, U32, 4)
+        s_bytes = shifted("s_bytes", E * C, U8, 1)
         gather(s_codes[:, 0:early], x_codes[:, 0 : CHUNKS[2][0]], 0, early)
         gather(s_codes[:, early:rest], x_codes[:], early, rest)
         gather(s_bytes[:, 0:C], x_bytes[:], 0, C)
@@ -147,10 +152,10 @@ def tile_moe_eps_mlp_silu_kernel(tc, xT, w1_words, w1_scales, w2_words, w2_scale
         gather(s_codes[:, 2 * C : E * C], x_codes[:], 2 * C, E * C)
         gather(s_bytes[:, 2 * C : E * C], x_bytes[:], 2 * C, E * C)
         slots = [(s_codes[:, e * C : (e + 1) * C], s_bytes[:, e * C : (e + 1) * C]) for e in range(E)]
-        by_slot = {(e, g): keep.tile([P, PASS], BF16, name=f"by_slot{e}_{g}", align_bytes=64) for e, g in ((0, 0), (0, 1), (1, 0))}
-        by_slot[1, 1] = first.tile([P, PASS], BF16, name="by_slot1_1", align_bytes=64, offset=4 * H)
-        hidden = [keep.tile([P, 4 * G * C], BF16, name=f"h{e}", align_bytes=64) for e in range(E - 1)]
-        last_hidden = [keep.tile([P, 4 * C], BF16, name=f"h3_{g}", align_bytes=64) for g in range(G)]
+        by_slot = {(e, g): keep.tile([P, PASS], BF16, name=f"by_slot{e}_{g}", align_bytes=LINE) for e, g in ((0, 0), (0, 1), (1, 0))}
+        by_slot[1, 1] = first.tile([P, PASS], BF16, name="by_slot1_1", align_bytes=LINE, offset=4 * H)
+        hidden = [keep.tile([P, 4 * G * C], BF16, name=f"h{e}", align_bytes=LINE) for e in range(E - 1)]
+        last_hidden = [keep.tile([P, 4 * C], BF16, name=f"h3_{g}", align_bytes=LINE) for g in range(G)]
 
         def first_by_slot(e, c, width, bank):
             sums = banks.tile([P, width], F32, name=f"a{e}_{c}", tag=f"bank{bank}")
@@ -205,8 +210,8 @@ def tile_moe_eps_mlp_silu_kernel(tc, xT, w1_words, w1_scales, w2_words, w2_scale
             nc.scalar.activation(dst.rearrange("p (s t) -> p s t", t=4), sums[:].rearrange("p t s -> p s t"), ACT.Silu)
 
         def quantise_hidden(name, h, words):
-            codes = keep.tile([P, words], U32, name=f"{name}_codes", align_bytes=64)
-            scales = keep.tile([P, words], U8, name=f"{name}_bytes", align_bytes=64)
+            codes = shifted(f"{name}_codes", words, U32, 4)
+            scales = shifted(f"{name}_bytes", words, U8, 1)
             nc.vector.quantize_mx(codes[:].bitcast(FP8X4), scales[:], h[:])
             return codes, scales
 

@@ -22,8 +22,6 @@ FP8X4 = mybir.dt.float8_e4m3fn_x4
 FP4X4 = mybir.dt.float4_e2m1fn_x4
 ACT = mybir.ActivationFunctionType
 
-CHUNKS = [(0, 256), (256, 256), (512, 128)]
-ON_VECTOR = [176, 144, 64]
 FIRST_WIDTHS = [128, 128, 256, 256, 256]
 ROWS_AT = P - 32
 
@@ -32,7 +30,7 @@ def tile_moe_eps_mlp_silu_kernel(tc, xT, w1_words, w1_scales, w2_words, w2_scale
     nc = tc.nc
     with ExitStack() as ctx:
         keep = ctx.enter_context(tc.tile_pool(name="keep", bufs=1))
-        first = ctx.enter_context(tc.tile_pool(name="first", bufs=1))
+        shared = ctx.enter_context(tc.tile_pool(name="shared", bufs=1))
         banks = ctx.enter_context(tc.psum_pool(name="banks", bufs=1))
 
         def shifted(name, columns, dtype, size):
@@ -40,120 +38,92 @@ def tile_moe_eps_mlp_silu_kernel(tc, xT, w1_words, w1_scales, w2_words, w2_scale
             return keep.tile([P, lead + columns], dtype, name=name, align_bytes=LINE)[:, lead : lead + columns]
 
         offsets = keep.tile([P, E * C // 16], U16, name="offsets")
-        packed = keep.tile([P, H], U8, name="packed", align_bytes=LINE)
-        permuted = first.tile([P, H], U8, name="permuted", align_bytes=LINE, offset=4 * H)
         moved = keep.tile([P, 2 * H], U8, name="moved", align_bytes=LINE)
         plain = keep.tile([P, 2 * H], U8, name="plain", align_bytes=LINE)
-        x_bytes = keep.tile([P, T], U8, name="x_bytes", align_bytes=LINE)
-        x_codes = keep.tile([P, T], U32, name="x_codes", align_bytes=LINE)
-        grouped = keep.tile([P, 4 * T], BF16, name="grouped", align_bytes=LINE)
-        raw01 = keep.tile([P, 2, 2 * H], U8, name="raw01", align_bytes=LINE)
-        raw = {e: keep.tile([P, 2 * H], U8, name=f"raw{e}", align_bytes=LINE) for e in (2, 3)}
+        rows = [keep.tile([P, T], F32, name=f"rows{j}", align_bytes=LINE) for j in range(4)]
+        raw = [keep.tile([P, 2 * H], U8, name=f"raw{e}", align_bytes=LINE) for e in range(E)]
         w1 = {e: keep.tile([P, 2 * H], U8, name=f"w1_{e}", align_bytes=LINE) for e in (2, 3)}
         identity = keep.tile([P, P], F32, name="identity", align_bytes=LINE)
-        make_identity(nc, identity[:])
-        w2_plane = keep.tile([P, E * G * N], U8, name="w2_plane", align_bytes=LINE)
-        w2 = keep.tile([P, E * G, 2 * N], U8, name="w2", align_bytes=LINE)
-        x_raw = [first.tile([P, 4, CHUNKS[0][1]], F32, name="x_raw0", align_bytes=LINE, offset=0)]
-        x_raw.extend(keep.tile([P, 4, w], F32, name=f"x_raw{c0}", align_bytes=LINE) for c0, w in CHUNKS[1:])
+        second_weights = keep.tile([P, 3 * E * G * N], U8, name="second_weights", align_bytes=LINE)
+        w2, w2_plane = second_weights[:, 0 : 2 * E * G * N], second_weights[:, 2 * E * G * N : 3 * E * G * N]
+        packed = second_weights[:, 2 * E * G * N - H // 2 : 2 * E * G * N + H // 2]
+        permuted = shared.tile([P, H], U8, name="permuted", align_bytes=LINE, offset=H)
         results = keep.tile([P, 2, E * C], F32, name="results", align_bytes=LINE)
         warm = keep.tile([P, 1], F32, name="warm")
         warm_out = keep.tile([P, 1], F32, name="warm_out")
 
+        nc.scalar.dma_start(packed[ROWS_AT:P, :].bitcast(I32), w1_scales[2:4, 0].rearrange("e j n -> j e n").bitcast(I32))
         nc.vector.memset(plain[:].bitcast(I32), 0)
         nc.vector.memset(warm[:], 0.0)
         nc.scalar.activation(warm_out[:], warm[:], ACT.Silu)
         nc.vector.memset(packed[0:ROWS_AT, :].bitcast(I32), 0)
-        nc.vector.memset(x_bytes[:].bitcast(I32), 0)
         nc.vector.memset(moved[:].bitcast(I32), 0)
-        nc.vector.memset(w2_plane[:].bitcast(I32), 0)
+        nc.vector.memset(w2_plane[:, H // 2 : 2 * H].bitcast(I32), 0)
+        make_identity(nc, identity[:])
 
-        def load_x(i):
-            c0, w = CHUNKS[i]
-            nc.sync.dma_start(x_raw[i][:], xT[:, c0 : c0 + w].rearrange("(p j) w -> p j w", j=4))
-
-        nc.sync.dma_start(packed[ROWS_AT:P, :].bitcast(I32), w1_scales[2:4, 0].rearrange("e j n -> j e n").bitcast(I32))
-        load_x(0)
-        load_x(1)
-        load_x(2)
+        by_row = xT.rearrange("(p j) w -> p j w", j=4)
+        nc.sync.dma_start(rows[0][:], by_row[:, 0, :])
         nc.sync.dma_start(offsets[:], offs)
+        for j in range(1, 4):
+            nc.sync.dma_start(rows[j][:], by_row[:, j, :])
         for r in range(4):
             nc.sync.dma_start(
                 plain[r:P:32].rearrange("p (e n) -> p e n", e=2).bitcast(I32),
                 w1_scales[0:2, 0, r:16:4, :].rearrange("e q n -> q e n").bitcast(I32),
             )
-        nc.sync.dma_start(raw01[:].bitcast(I32), w1_words[0:2, 0].rearrange("e p b -> p e b").bitcast(I32))
-        for e in (2, 3):
+        for e in (0, 2, 1, 3):
             nc.sync.dma_start(raw[e][:].bitcast(I32), w1_words[e, 0].bitcast(I32))
-        for g in range(G):
-            cols = slice(g * PASS, (g + 1) * PASS)
-            nc.vector.tensor_copy(
-                permuted[:, cols].rearrange("p (t m) -> p t m", t=4),
-                packed[:, cols].rearrange("p (m t) -> p t m", t=4),
-            )
+        nc.gpsimd.tensor_copy(
+            permuted[:].rearrange("p (g t m) -> p g t m", g=G, t=4),
+            packed.rearrange("p (g m t) -> p g t m", g=G, t=4),
+        )
         for q in (0, 2, 1, 3):
             nc.sync.dma_start(
                 moved[32 * q : 32 * q + 4, :].rearrange("p (e n) -> p e n", e=2).bitcast(I32),
                 permuted[ROWS_AT + 8 * q : ROWS_AT + 8 * q + 8, :].bitcast(I32),
             )
-
-        def round_chunk(i):
-            c0, w = CHUNKS[i]
-            dst = grouped[:, 4 * c0 : 4 * (c0 + w)].rearrange("p (c u j) -> p c j u", u=4, j=4)
-            src = x_raw[i][:].rearrange("p j (c u) -> p c j u", u=4)
-            split = ON_VECTOR[i] // 4
-            nc.vector.tensor_copy(dst[:, 0:split], src[:, 0:split])
-            nc.scalar.activation(dst[:, split : w // 4], src[:, split : w // 4], ACT.Copy)
-
-        def quantise_chunk(i):
-            c0, w = CHUNKS[i]
-            nc.vector.quantize_mx(x_codes[:, c0 : c0 + w].bitcast(FP8X4), x_bytes[:, c0 : c0 + w], grouped[:, 4 * c0 : 4 * (c0 + w)])
-
-        round_chunk(0)
-        zero_codes = first.tile([P, P], U32, name="zero_codes", align_bytes=LINE, offset=0)
-        zero_bytes = first.tile([P, P], U8, name="zero_bytes", align_bytes=LINE, offset=4 * P)
-        nc.vector.quantize_mx(zero_codes[:].bitcast(FP8X4), zero_bytes[:], w2_plane[:, 0 : 2 * PASS].bitcast(BF16))
-        quantise_chunk(0)
-        round_chunk(1)
-        round_chunk(2)
-        quantise_chunk(1)
-        quantise_chunk(2)
-
-        unused = banks.tile([P, PASS], F32, name="unused", tag="bank7")
-        for repeat in range(3):
-            nc.tensor.matmul_mx(
-                out=unused[:],
-                lhsT=zero_codes[:].bitcast(FP8X4),
-                lhsT_scale=zero_bytes[:],
-                rhs=permuted[:].bitcast(FP4X4),
-                rhs_scale=permuted[:, 0:PASS],
-                start=True,
-                stop=True,
-            )
-
-        nc.sync.dma_start(w2[:].bitcast(I32), w2_words.rearrange("e s p b -> p (e s) b").bitcast(I32))
+        nc.sync.dma_start(w2.rearrange("p (a b) -> p a b", b=2 * N).bitcast(I32), w2_words.rearrange("e s p b -> p (e s) b").bitcast(I32))
         for r in range(4):
             nc.sync.dma_start(
                 w2_plane[r:P:32].rearrange("p (a n) -> p a n", n=N).bitcast(I32),
                 w2_scales[:, :, r:16:4, :].rearrange("e s q n -> q (e s) n").bitcast(I32),
             )
 
-        def gather(dst, table, j0, j1):
-            nc.vector.tensor_copy(dst, table.indirect(offsets[:, j0 // 16 : j1 // 16]))
+        def picked(j, e0, e1):
+            return rows[j][:].indirect(offsets[:, e0 * C // 16 : e1 * C // 16])
 
-        early, rest = C // 2, C + C // R
-        s_codes = shifted("s_codes", E * C, U32, 4)
-        s_bytes = shifted("s_bytes", E * C, U8, 1)
-        gather(s_codes[:, 0:early], x_codes[:, 0 : CHUNKS[2][0]], 0, early)
-        gather(s_codes[:, early:rest], x_codes[:], early, rest)
-        gather(s_bytes[:, 0:C], x_bytes[:], 0, C)
-        gather(s_codes[:, rest : 2 * C], x_codes[:], rest, 2 * C)
-        gather(s_bytes[:, C : 2 * C], x_bytes[:], C, 2 * C)
-        gather(s_codes[:, 2 * C : E * C], x_codes[:], 2 * C, E * C)
-        gather(s_bytes[:, 2 * C : E * C], x_bytes[:], 2 * C, E * C)
-        slots = [(s_codes[:, e * C : (e + 1) * C], s_bytes[:, e * C : (e + 1) * C]) for e in range(E)]
+        woven = [shared.tile([P, 4 * C], BF16, name="woven0", align_bytes=LINE, offset=0)]
+        flat1 = keep.tile([P, 4, C], BF16, name="flat1", align_bytes=LINE)
+        flat23 = keep.tile([P, 4, 2 * C], BF16, name="flat23", align_bytes=LINE)
+        for j in range(4):
+            nc.vector.tensor_copy(woven[0][:].rearrange("p (s j) -> p s j", j=4)[:, :, j], picked(j, 0, 1))
+            if j < 3:
+                nc.vector.tensor_copy(flat1[:, j, :], picked(j, 1, 2))
+            else:
+                nc.scalar.activation(flat1[:, j, :], picked(j, 1, 2), ACT.Copy)
+            nc.scalar.activation(flat23[:, j, :], picked(j, 2, 4), ACT.Copy)
+
+        def quantise(name, h, words):
+            codes = shifted(f"{name}_codes", words, U32, 4)
+            scales = shifted(f"{name}_bytes", words, U8, 1)
+            nc.vector.quantize_mx(codes[:].bitcast(FP8X4), scales[:], h[:])
+            return codes, scales
+
+        def weave(dst, src):
+            nc.vector.tensor_copy(dst[:].rearrange("p (c u j) -> p c j u", u=4, j=4), src.rearrange("p j (c u) -> p c j u", u=4))
+
+        slots = [quantise("x0", woven[0], C)]
+        woven.append(shared.tile([P, 4 * C], BF16, name="woven1", align_bytes=LINE, offset=0))
+        woven.extend(keep.tile([P, 4 * C], BF16, name=f"woven{e}", align_bytes=LINE) for e in (2, 3))
+        weave(woven[1], flat1[:])
+        weave(woven[2], flat23[:, :, 0:C])
+        slots.append(quantise("x1", woven[1], C))
+        weave(woven[3], flat23[:, :, C : 2 * C])
+        slots.append(quantise("x2", woven[2], C))
+        slots.append(quantise("x3", woven[3], C))
+
         by_slot = {(e, g): keep.tile([P, PASS], BF16, name=f"by_slot{e}_{g}", align_bytes=LINE) for e, g in ((0, 0), (0, 1), (1, 0))}
-        by_slot[1, 1] = first.tile([P, PASS], BF16, name="by_slot1_1", align_bytes=LINE, offset=4 * H)
+        by_slot[1, 1] = shared.tile([P, PASS], BF16, name="by_slot1_1", align_bytes=LINE, offset=H)
         hidden = [keep.tile([P, 4 * G * C], BF16, name=f"h{e}", align_bytes=LINE) for e in range(E - 1)]
         last_hidden = [keep.tile([P, 4 * C], BF16, name=f"h3_{g}", align_bytes=LINE) for g in range(G)]
 
@@ -163,7 +133,7 @@ def tile_moe_eps_mlp_silu_kernel(tc, xT, w1_words, w1_scales, w2_words, w2_scale
                 out=sums[:],
                 lhsT=slots[e][0].bitcast(FP8X4),
                 lhsT_scale=slots[e][1],
-                rhs=raw01[:, e, 2 * c : 2 * (c + width)].bitcast(FP4X4),
+                rhs=raw[e][:, 2 * c : 2 * (c + width)].bitcast(FP4X4),
                 rhs_scale=plain[:, e * H + c : e * H + c + width],
                 start=True,
                 stop=True,
@@ -189,10 +159,11 @@ def tile_moe_eps_mlp_silu_kernel(tc, xT, w1_words, w1_scales, w2_words, w2_scale
             )
 
         def permute_words(e):
-            nc.gpsimd.tensor_copy(
-                w1[e][:].bitcast(U16).rearrange("p (g t m) -> p g t m", g=G, t=4),
-                raw[e][:].bitcast(U16).rearrange("p (g m t) -> p g t m", g=G, t=4),
-            )
+            for g in range(G):
+                nc.gpsimd.tensor_copy(
+                    w1[e][:, 2 * g * PASS : 2 * (g + 1) * PASS].bitcast(U16).rearrange("p (t m) -> p t m", t=4),
+                    raw[e][:, 2 * g * PASS : 2 * (g + 1) * PASS].bitcast(U16).rearrange("p (m t) -> p t m", t=4),
+                )
 
         def first_by_column(e, g, bank, dst):
             sums = banks.tile([P, 4, C], F32, name=f"a{e}_{g}", tag=f"bank{bank}")
@@ -209,17 +180,11 @@ def tile_moe_eps_mlp_silu_kernel(tc, xT, w1_words, w1_scales, w2_words, w2_scale
                 )
             nc.scalar.activation(dst.rearrange("p (s t) -> p s t", t=4), sums[:].rearrange("p t s -> p s t"), ACT.Silu)
 
-        def quantise_hidden(name, h, words):
-            codes = shifted(f"{name}_codes", words, U32, 4)
-            scales = shifted(f"{name}_bytes", words, U8, 1)
-            nc.vector.quantize_mx(codes[:].bitcast(FP8X4), scales[:], h[:])
-            return codes, scales
-
         def second_pass(y, e, g, i, codes, scales):
             a = e * G + g
             nc.tensor.matmul_mx(
                 out=y,
-                lhsT=w2[:, a, 2 * P * i : 2 * P * i + 2 * P].bitcast(FP4X4),
+                lhsT=w2[:, 2 * (a * N + P * i) : 2 * (a * N + P * i + P)].bitcast(FP4X4),
                 lhsT_scale=w2_plane[:, a * N + P * i : a * N + P * i + P],
                 rhs=codes.bitcast(FP8X4),
                 rhs_scale=scales,
@@ -228,34 +193,33 @@ def tile_moe_eps_mlp_silu_kernel(tc, xT, w1_words, w1_scales, w2_words, w2_scale
             )
 
         def second(e, y):
-            codes, scales = quantise_hidden(f"h{e}", hidden[e], G * C)
+            codes, scales = quantise(f"h{e}", hidden[e], G * C)
             for i in range(2):
                 for g in range(G):
                     second_pass(y[i], e, g, i, codes[:, g * C : (g + 1) * C], scales[:, g * C : (g + 1) * C])
 
         for width_index, bank in enumerate((6, 5, 0, 1, 4)):
             first_by_slot(0, sum(FIRST_WIDTHS[:width_index]), FIRST_WIDTHS[width_index], bank)
-        for g in range(G):
-            first_by_slot(1, g * PASS, PASS, 2 + g)
+        for quarter, bank in enumerate((7, 3, 6, 5)):
+            first_by_slot(1, quarter * PASS // 2, PASS // 2, bank)
         permute_words(2)
-        for g, bank in enumerate((6, 5)):
+        for g, bank in enumerate((0, 1)):
             first_by_column(2, g, bank, hidden[2][:, g * 4 * C : (g + 1) * 4 * C])
         last = E - 1
-        turned = [turn(0, 7, (0, 1)), turn(1, 4, (1, 0))]
+        copy_turned(0, turn(0, 7, (0, 1)))
         permute_words(last)
-        for g, bank in enumerate((0, 3)):
-            first_by_column(last, g, bank, last_hidden[g][:])
-        for e in range(2):
-            copy_turned(e, turned[e])
+        first_by_column(last, 0, 4, last_hidden[0][:])
+        copy_turned(1, turn(1, 3, (1, 0)))
+        first_by_column(last, 1, 0, last_hidden[1][:])
 
         y02 = banks.tile([P, 2, 2, C], F32, name="y02", tag="bank7")
         second(0, [y02[:, 0, i, :] for i in range(2)])
         second(2, [y02[:, 1, i, :] for i in range(2)])
-        y1 = [banks.tile([P, C], F32, name=f"y1_{i}", tag=f"bank{bank}") for i, bank in enumerate((4, 1))]
+        y1 = [banks.tile([P, C], F32, name=f"y1_{i}", tag=f"bank{bank}") for i, bank in enumerate((2, 4))]
         second(1, [y[:] for y in y1])
         y3 = [banks.tile([P, C], F32, name=f"last{i}", tag=f"bank{bank}") for i, bank in enumerate((5, 6))]
         for g in range(G):
-            codes, scales = quantise_hidden(f"h{last}_{g}", last_hidden[g], C)
+            codes, scales = quantise(f"h{last}_{g}", last_hidden[g], C)
             for i in range(2):
                 second_pass(y3[i][:], last, g, i, codes[:], scales[:])
 

@@ -52,7 +52,6 @@ def tile_moe_eps_mlp_silu_kernel(tc, xT, w1_words, w1_scales, w2_words, w2_scale
         warm = keep.tile([P, 1], F32, name="warm")
         warm_out = keep.tile([P, 1], F32, name="warm_out")
 
-        nc.scalar.dma_start(packed[ROWS_AT:P, :].bitcast(I32), w1_scales[2:4, 0].rearrange("e j n -> j e n").bitcast(I32))
         nc.vector.memset(plain[:].bitcast(I32), 0)
         nc.vector.memset(warm[:], 0.0)
         nc.scalar.activation(warm_out[:], warm[:], ACT.Silu)
@@ -62,6 +61,7 @@ def tile_moe_eps_mlp_silu_kernel(tc, xT, w1_words, w1_scales, w2_words, w2_scale
         make_identity(nc, identity[:])
 
         by_row = xT.rearrange("(p j) w -> p j w", j=4)
+        nc.sync.dma_start(packed[ROWS_AT:P, :].bitcast(I32), w1_scales[2:4, 0].rearrange("e j n -> j e n").bitcast(I32))
         nc.sync.dma_start(rows[0][:], by_row[:, 0, :])
         nc.sync.dma_start(offsets[:], offs)
         for j in range(1, 4):
@@ -71,9 +71,9 @@ def tile_moe_eps_mlp_silu_kernel(tc, xT, w1_words, w1_scales, w2_words, w2_scale
                 plain[r:P:32].rearrange("p (e n) -> p e n", e=2).bitcast(I32),
                 w1_scales[0:2, 0, r:16:4, :].rearrange("e q n -> q e n").bitcast(I32),
             )
-        for e in (0, 2, 1, 3):
+        for e in range(E):
             nc.sync.dma_start(raw[e][:].bitcast(I32), w1_words[e, 0].bitcast(I32))
-        nc.gpsimd.tensor_copy(
+        nc.vector.tensor_copy(
             permuted[:].rearrange("p (g t m) -> p g t m", g=G, t=4),
             packed.rearrange("p (g m t) -> p g t m", g=G, t=4),
         )
@@ -159,11 +159,10 @@ def tile_moe_eps_mlp_silu_kernel(tc, xT, w1_words, w1_scales, w2_words, w2_scale
             )
 
         def permute_words(e):
-            for g in range(G):
-                nc.gpsimd.tensor_copy(
-                    w1[e][:, 2 * g * PASS : 2 * (g + 1) * PASS].bitcast(U16).rearrange("p (t m) -> p t m", t=4),
-                    raw[e][:, 2 * g * PASS : 2 * (g + 1) * PASS].bitcast(U16).rearrange("p (m t) -> p t m", t=4),
-                )
+            nc.vector.tensor_copy(
+                w1[e][:].bitcast(U16).rearrange("p (g t m) -> p g t m", g=G, t=4),
+                raw[e][:].bitcast(U16).rearrange("p (g m t) -> p g t m", g=G, t=4),
+            )
 
         def first_by_column(e, g, bank, dst):
             sums = banks.tile([P, 4, C], F32, name=f"a{e}_{g}", tag=f"bank{bank}")

@@ -227,5 +227,4 @@ def tile_moe_eps_mlp_silu_kernel(tc, xT, w1_words, w1_scales, w2_words, w2_scale
         for e, y in ((1, y1), (last, y3)):
             nc.vector.tensor_copy(ranked[:, e, 0], y[0][:].rearrange("p (m u) -> p m u", m=R))
             nc.scalar.copy(ranked[:, e, 1], y[1][:].rearrange("p (m u) -> p m u", m=R))
-        nc.sync.dma_start(out[0:P, :], results[:, 0, :])
-        nc.scalar.dma_start(out[P : 2 * P, :], results[:, 1, :])
+        nc.sync.dma_start(out.rearrange("(i p) s -> p i s", p=P), results[:])

@@ -61,9 +61,9 @@ def tile_moe_eps_mlp_silu_kernel(tc, xT, w1_words, w1_scales, w2_words, w2_scale
         make_identity(nc, identity[:])
 
         by_row = xT.rearrange("(p j) w -> p j w", j=4)
-        nc.sync.dma_start(packed[ROWS_AT:P, :].bitcast(I32), w1_scales[2:4, 0].rearrange("e j n -> j e n").bitcast(I32))
         nc.sync.dma_start(rows[0][:], by_row[:, 0, :])
         nc.sync.dma_start(offsets[:], offs)
+        nc.sync.dma_start(packed[ROWS_AT:P, :].bitcast(I32), w1_scales[2:4, 0].rearrange("e j n -> j e n").bitcast(I32))
         for j in range(1, 4):
             nc.sync.dma_start(rows[j][:], by_row[:, j, :])
         for r in range(4):
@@ -73,7 +73,7 @@ def tile_moe_eps_mlp_silu_kernel(tc, xT, w1_words, w1_scales, w2_words, w2_scale
             )
         for e in range(E):
             nc.sync.dma_start(raw[e][:].bitcast(I32), w1_words[e, 0].bitcast(I32))
-        nc.vector.tensor_copy(
+        nc.gpsimd.tensor_copy(
             permuted[:].rearrange("p (g t m) -> p g t m", g=G, t=4),
             packed.rearrange("p (g m t) -> p g t m", g=G, t=4),
         )
@@ -214,8 +214,8 @@ def tile_moe_eps_mlp_silu_kernel(tc, xT, w1_words, w1_scales, w2_words, w2_scale
         y02 = banks.tile([P, 2, 2, C], F32, name="y02", tag="bank7")
         second(0, [y02[:, 0, i, :] for i in range(2)])
         second(2, [y02[:, 1, i, :] for i in range(2)])
-        y1 = [banks.tile([P, C], F32, name=f"y1_{i}", tag=f"bank{bank}") for i, bank in enumerate((2, 4))]
-        second(1, [y[:] for y in y1])
+        y1 = banks.tile([P, 2, C], F32, name="y1", tag="bank2")
+        second(1, [y1[:, i, :] for i in range(2)])
         y3 = [banks.tile([P, C], F32, name=f"last{i}", tag=f"bank{bank}") for i, bank in enumerate((5, 6))]
         for g in range(G):
             codes, scales = quantise(f"h{last}_{g}", last_hidden[g], C)
@@ -224,7 +224,7 @@ def tile_moe_eps_mlp_silu_kernel(tc, xT, w1_words, w1_scales, w2_words, w2_scale
 
         ranked = results[:].rearrange("p i (m e u) -> p e i m u", m=R, e=E)
         nc.scalar.copy(ranked[:, 0:3:2], y02[:].rearrange("p e i (m u) -> p e i m u", m=R))
-        for e, y in ((1, y1), (last, y3)):
-            nc.vector.tensor_copy(ranked[:, e, 0], y[0][:].rearrange("p (m u) -> p m u", m=R))
-            nc.scalar.copy(ranked[:, e, 1], y[1][:].rearrange("p (m u) -> p m u", m=R))
+        nc.vector.tensor_copy(ranked[:, 1], y1[:].rearrange("p i (m u) -> p i m u", m=R))
+        nc.scalar.copy(ranked[:, last, 0], y3[0][:].rearrange("p (m u) -> p m u", m=R))
+        nc.vector.tensor_copy(ranked[:, last, 1], y3[1][:].rearrange("p (m u) -> p m u", m=R))
         nc.sync.dma_start(out.rearrange("(i p) s -> p i s", p=P), results[:])

from contextlib import ExitStack

import concourse.mybir as mybir
from concourse.masks import make_identity

FLOPS = 805306368

K, T, E, C, H, N = 512, 640, 4, 128, 1024, 256
R = 4
P = 128
PASS = 4 * P
G = H // PASS
LINE = 256

F32 = mybir.dt.float32
BF16 = mybir.dt.bfloat16
I32 = mybir.dt.int32
U32 = mybir.dt.uint32
U16 = mybir.dt.uint16
U8 = mybir.dt.uint8
FP8X4 = mybir.dt.float8_e4m3fn_x4
FP4X4 = mybir.dt.float4_e2m1fn_x4
ACT = mybir.ActivationFunctionType

FIRST_WIDTHS = [128, 128, 256, 256, 256]
ROWS_AT = P - 32


def tile_moe_eps_mlp_silu_kernel(tc, xT, w1_words, w1_scales, w2_words, w2_scales, offs, out):
    nc = tc.nc
    with ExitStack() as ctx:
        keep = ctx.enter_context(tc.tile_pool(name="keep", bufs=1))
        shared = ctx.enter_context(tc.tile_pool(name="shared", bufs=1))
        banks = ctx.enter_context(tc.psum_pool(name="banks", bufs=1))

        def shifted(name, columns, dtype, size):
            lead = LINE // 2 // size
            return keep.tile([P, lead + columns], dtype, name=name, align_bytes=LINE)[:, lead : lead + columns]

        offsets = keep.tile([P, E * C // 16], U16, name="offsets")
        moved = keep.tile([P, 2 * H], U8, name="moved", align_bytes=LINE)
        plain = keep.tile([P, 2 * H], U8, name="plain", align_bytes=LINE)
        rows = [keep.tile([P, T], F32, name=f"rows{j}", align_bytes=LINE) for j in range(4)]
        raw = [keep.tile([P, 2 * H], U8, name=f"raw{e}", align_bytes=LINE) for e in range(E)]
        w1 = {e: keep.tile([P, 2 * H], U8, name=f"w1_{e}", align_bytes=LINE) for e in (2, 3)}
        identity = keep.tile([P, P], F32, name="identity", align_bytes=LINE)
        second_weights = keep.tile([P, 3 * E * G * N], U8, name="second_weights", align_bytes=LINE)
        w2, w2_plane = second_weights[:, 0 : 2 * E * G * N], second_weights[:, 2 * E * G * N : 3 * E * G * N]
        packed = second_weights[:, 2 * E * G * N - H // 2 : 2 * E * G * N + H // 2]
        permuted = shared.tile([P, H], U8, name="permuted", align_bytes=LINE, offset=H)
        results = keep.tile([P, 2, E * C], F32, name="results", align_bytes=LINE)
        warm = keep.tile([P, 1], F32, name="warm")
        warm_out = keep.tile([P, 1], F32, name="warm_out")

        nc.vector.memset(plain[:].bitcast(I32), 0)
        nc.vector.memset(warm[:], 0.0)
        nc.scalar.activation(warm_out[:], warm[:], ACT.Silu)
        nc.vector.memset(packed[0:ROWS_AT, :].bitcast(I32), 0)
        nc.vector.memset(moved[:].bitcast(I32), 0)
        nc.vector.memset(w2_plane[:, H // 2 : 2 * H].bitcast(I32), 0)
        make_identity(nc, identity[:])

        by_row = xT.rearrange("(p j) w -> p j w", j=4)
        nc.sync.dma_start(rows[0][:], by_row[:, 0, :])
        nc.sync.dma_start(offsets[:], offs)
        nc.sync.dma_start(packed[ROWS_AT:P, :].bitcast(I32), w1_scales[2:4, 0].rearrange("e j n -> j e n").bitcast(I32))
        for j in range(1, 4):
            nc.sync.dma_start(rows[j][:], by_row[:, j, :])
        for r in range(4):
            nc.sync.dma_start(
                plain[r:P:32].rearrange("p (e n) -> p e n", e=2).bitcast(I32),
                w1_scales[0:2, 0, r:16:4, :].rearrange("e q n -> q e n").bitcast(I32),
            )
        for e in range(E):
            nc.sync.dma_start(raw[e][:].bitcast(I32), w1_words[e, 0].bitcast(I32))
        nc.gpsimd.tensor_copy(
            permuted[:].rearrange("p (g t m) -> p g t m", g=G, t=4),
            packed.rearrange("p (g m t) -> p g t m", g=G, t=4),
        )
        for q in (0, 2, 1, 3):
            nc.sync.dma_start(
                moved[32 * q : 32 * q + 4, :].rearrange("p (e n) -> p e n", e=2).bitcast(I32),
                permuted[ROWS_AT + 8 * q : ROWS_AT + 8 * q + 8, :].bitcast(I32),
            )
        nc.sync.dma_start(w2.rearrange("p (a b) -> p a b", b=2 * N).bitcast(I32), w2_words.rearrange("e s p b -> p (e s) b").bitcast(I32))
        for r in range(4):
            nc.sync.dma_start(
                w2_plane[r:P:32].rearrange("p (a n) -> p a n", n=N).bitcast(I32),
                w2_scales[:, :, r:16:4, :].rearrange("e s q n -> q (e s) n").bitcast(I32),
            )

        def picked(j, e0, e1):
            return rows[j][:].indirect(offsets[:, e0 * C // 16 : e1 * C // 16])

        woven = [shared.tile([P, 4 * C], BF16, name="woven0", align_bytes=LINE, offset=0)]
        flat1 = keep.tile([P, 4, C], BF16, name="flat1", align_bytes=LINE)
        flat23 = keep.tile([P, 4, 2 * C], BF16, name="flat23", align_bytes=LINE)
        for j in range(4):
            nc.vector.tensor_copy(woven[0][:].rearrange("p (s j) -> p s j", j=4)[:, :, j], picked(j, 0, 1))
            if j < 3:
                nc.vector.tensor_copy(flat1[:, j, :], picked(j, 1, 2))
            else:
                nc.scalar.activation(flat1[:, j, :], picked(j, 1, 2), ACT.Copy)
            nc.scalar.activation(flat23[:, j, :], picked(j, 2, 4), ACT.Copy)

        def quantise(name, h, words):
            codes = shifted(f"{name}_codes", words, U32, 4)
            scales = shifted(f"{name}_bytes", words, U8, 1)
            nc.vector.quantize_mx(codes[:].bitcast(FP8X4), scales[:], h[:])
            return codes, scales

        def weave(dst, src):
            nc.vector.tensor_copy(dst[:].rearrange("p (c u j) -> p c j u", u=4, j=4), src.rearrange("p j (c u) -> p c j u", u=4))

        slots = [quantise("x0", woven[0], C)]
        woven.append(shared.tile([P, 4 * C], BF16, name="woven1", align_bytes=LINE, offset=0))
        woven.extend(keep.tile([P, 4 * C], BF16, name=f"woven{e}", align_bytes=LINE) for e in (2, 3))
        weave(woven[1], flat1[:])
        weave(woven[2], flat23[:, :, 0:C])
        slots.append(quantise("x1", woven[1], C))
        weave(woven[3], flat23[:, :, C : 2 * C])
        slots.append(quantise("x2", woven[2], C))
        slots.append(quantise("x3", woven[3], C))

        by_slot = {(e, g): keep.tile([P, PASS], BF16, name=f"by_slot{e}_{g}", align_bytes=LINE) for e, g in ((0, 0), (0, 1), (1, 0))}
        by_slot[1, 1] = shared.tile([P, PASS], BF16, name="by_slot1_1", align_bytes=LINE, offset=H)
        hidden = [keep.tile([P, 4 * G * C], BF16, name=f"h{e}", align_bytes=LINE) for e in range(E - 1)]
        last_hidden = [keep.tile([P, 4 * C], BF16, name=f"h3_{g}", align_bytes=LINE) for g in range(G)]

        def first_by_slot(e, c, width, bank):
            sums = banks.tile([P, width], F32, name=f"a{e}_{c}", tag=f"bank{bank}")
            nc.tensor.matmul_mx(
                out=sums[:],
                lhsT=slots[e][0].bitcast(FP8X4),
                lhsT_scale=slots[e][1],
                rhs=raw[e][:, 2 * c : 2 * (c + width)].bitcast(FP4X4),
                rhs_scale=plain[:, e * H + c : e * H + c + width],
                start=True,
                stop=True,
            )
            g, p0 = c // PASS, c % PASS // 4
            nc.scalar.activation(
                by_slot[e, g][:].rearrange("s (u p d) -> s u p d", u=2, d=2)[:, :, p0 : p0 + width // 4, :],
                sums[:].rearrange("s (p u d) -> s u p d", u=2, d=2),
                ACT.Silu,
            )

        def turn(e, bank, order):
            turned = banks.tile([P, 2 * G, C], F32, name=f"turned{e}", tag=f"bank{bank}")
            for g in order:
                for u in range(2):
                    nc.tensor.transpose(turned[:, 2 * g + u, :], by_slot[e, g][:].bitcast(F32)[:, u * P : (u + 1) * P], identity[:])
            return turned

        def copy_turned(e, turned):
            nc.vector.tensor_copy(
                hidden[e][:].bitcast(F32).rearrange("p (g s u) -> p g s u", g=G, u=2),
                turned[:].rearrange("p (g u) s -> p g s u", u=2),
            )

        def permute_words(e):
            nc.vector.tensor_copy(
                w1[e][:].bitcast(U16).rearrange("p (g t m) -> p g t m", g=G, t=4),
                raw[e][:].bitcast(U16).rearrange("p (g m t) -> p g t m", g=G, t=4),
            )

        def first_by_column(e, g, bank, dst):
            sums = banks.tile([P, 4, C], F32, name=f"a{e}_{g}", tag=f"bank{bank}")
            for t in range(4):
                c = g * PASS + t * P
                nc.tensor.matmul_mx(
                    out=sums[:, t, :],
                    lhsT=w1[e][:, 2 * c : 2 * c + 2 * P].bitcast(FP4X4),
                    lhsT_scale=moved[:, (e - 2) * H + c : (e - 2) * H + c + P],
                    rhs=slots[e][0].bitcast(FP8X4),
                    rhs_scale=slots[e][1],
                    start=True,
                    stop=True,
                )
            nc.scalar.activation(dst.rearrange("p (s t) -> p s t", t=4), sums[:].rearrange("p t s -> p s t"), ACT.Silu)

        def second_pass(y, e, g, i, codes, scales):
            a = e * G + g
            nc.tensor.matmul_mx(
                out=y,
                lhsT=w2[:, 2 * (a * N + P * i) : 2 * (a * N + P * i + P)].bitcast(FP4X4),
                lhsT_scale=w2_plane[:, a * N + P * i : a * N + P * i + P],
                rhs=codes.bitcast(FP8X4),
                rhs_scale=scales,
                start=(g == 0),
                stop=(g == G - 1),
            )

        def second(e, y):
            codes, scales = quantise(f"h{e}", hidden[e], G * C)
            for i in range(2):
                for g in range(G):
                    second_pass(y[i], e, g, i, codes[:, g * C : (g + 1) * C], scales[:, g * C : (g + 1) * C])

        for width_index, bank in enumerate((6, 5, 0, 1, 4)):
            first_by_slot(0, sum(FIRST_WIDTHS[:width_index]), FIRST_WIDTHS[width_index], bank)
        for quarter, bank in enumerate((7, 3, 6, 5)):
            first_by_slot(1, quarter * PASS // 2, PASS // 2, bank)
        permute_words(2)
        for g, bank in enumerate((0, 1)):
            first_by_column(2, g, bank, hidden[2][:, g * 4 * C : (g + 1) * 4 * C])
        last = E - 1
        copy_turned(0, turn(0, 7, (0, 1)))
        permute_words(last)
        first_by_column(last, 0, 4, last_hidden[0][:])
        copy_turned(1, turn(1, 3, (1, 0)))
        first_by_column(last, 1, 0, last_hidden[1][:])

        y02 = banks.tile([P, 2, 2, C], F32, name="y02", tag="bank7")
        second(0, [y02[:, 0, i, :] for i in range(2)])
        second(2, [y02[:, 1, i, :] for i in range(2)])
        y1 = banks.tile([P, 2, C], F32, name="y1", tag="bank2")
        second(1, [y1[:, i, :] for i in range(2)])
        y3 = [banks.tile([P, C], F32, name=f"last{i}", tag=f"bank{bank}") for i, bank in enumerate((5, 6))]
        for g in range(G):
            codes, scales = quantise(f"h{last}_{g}", last_hidden[g], C)
            for i in range(2):
                second_pass(y3[i][:], last, g, i, codes[:], scales[:])

        ranked = results[:].rearrange("p i (m e u) -> p e i m u", m=R, e=E)
        nc.scalar.copy(ranked[:, 0:3:2], y02[:].rearrange("p e i (m u) -> p e i m u", m=R))
        nc.vector.tensor_copy(ranked[:, 1], y1[:].rearrange("p i (m u) -> p i m u", m=R))
        nc.scalar.copy(ranked[:, last, 0], y3[0][:].rearrange("p (m u) -> p m u", m=R))
        nc.vector.tensor_copy(ranked[:, last, 1], y3[1][:].rearrange("p (m u) -> p m u", m=R))
        nc.sync.dma_start(out.rearrange("(i p) s -> p i s", p=P), results[:])
